import numpy as np, ml_dtypes
CORES = [2,6,10,14,18,22,26,30]
N = 8
import mx_ref
BF = ml_dtypes.bfloat16
def gentries(a):
    return np.ascontiguousarray(a.reshape(8, 16, -1).transpose(0, 2, 1)).reshape(8, -1)
def gtable(e):
    e = np.asarray(e); return np.ascontiguousarray(e.reshape(8, -1, 16).transpose(0, 2, 1)).reshape(128, -1).astype(np.int32)
def gcols(t, e):
    v = np.concatenate([t.reshape(8, 16, -1, 4), np.zeros((8, 16, 1, 4), BF)], axis=2)
    return np.ascontiguousarray(np.stack([v[g][:, e[g]] for g in range(8)])).reshape(128, -1)
def tile(rs):
    return np.stack(rs, axis=2).reshape(128, -1).astype(BF)
def pick(q, e):
    c = np.concatenate([q[0].reshape(128, -1, 4), np.zeros((128, 1, 4), np.uint8)], axis=1); s = np.concatenate([q[1], np.ones((16, 1), np.uint8)], axis=1)
    return (np.ascontiguousarray(c[:, e].reshape(128, -1)), np.ascontiguousarray(s[:, e]))
def join(*qs):
    return (np.concatenate([q[0] for q in qs], axis=1), np.concatenate([q[1] for q in qs], axis=1))
def put(q, e, v):
    c, s = q[0].reshape(128, -1, 4).copy(), q[1].copy(); c[:, e] = v[0].reshape(128, -1, 4); s[:, e] = v[1]
    return (c.reshape(128, -1), s)
def pk(c, s):
    return (np.ascontiguousarray(c), mx_ref.live(s))
def emit(q):
    return q[0], q[1]
def packed(v, rng):
    q = [mx_ref.quantize(np.ascontiguousarray(v[r])) for r in range(N)]
    return np.stack([a for a, b in q]), np.stack([mx_ref.plane(b, rng) for a, b in q])
def values_of_codes():
    e, c = np.zeros((128, 128, 4), np.float32), np.zeros((128, 2, 4), np.uint8)
    e[np.arange(128), np.arange(128), 0] = 1
    c[:127, :, 0] = np.arange(256).reshape(2, 128).T[:127]
    return mx_ref.matmul(mx_ref.quantize(e.reshape(128, 512).astype(BF)), (c.reshape(128, 8), np.full((16, 2), 127, np.uint8))).T.reshape(-1).astype(np.float64)
CODE_VALUE, SCALE_VALUE = values_of_codes(), 2.0 ** (np.arange(256) - 127.0)
def decode(q):
    return (CODE_VALUE[q[0]].reshape(16, 8, -1, 4) * SCALE_VALUE[q[1]][:, None, :, None] + 0.0).reshape(128, -1).astype(np.float32)
def f(rng, *shape):
    return mx_ref.flush((rng.standard_normal(shape, dtype=np.float32) * np.exp2(rng.integers(-2, 3, shape[:-1] + (1,)))).astype(BF))
def wide(rng, *shape, cols=0):
    v = rng.standard_normal(shape, dtype=np.float32) * np.exp2(rng.integers(-12, 13, shape)).astype(np.float32)
    if cols: v *= np.repeat(np.exp2(rng.integers(-cols, cols + 1, shape[:-2] + (1, shape[-1] // 4))) * (rng.random(shape[:-2] + (1, shape[-1] // 4)) > 0.0625), 4, axis=-1).astype(np.float32)
    return mx_ref.flush(v.astype(BF))
C = 352
MASK = [1, 2, 4]
def numbers_of(rng):
    return {"x": np.array(f(rng, N, 128, 4 * C)), "u": np.array(f(rng, N, 128, 512)), "v": np.array(f(rng, N, 128, 512))}
def following(o):
    e = np.zeros_like(o)
    np.put_along_axis(e, o, np.roll(o, -1, axis=-1), axis=-1)
    return e
def rings(rng):
    return following(rng.permuted(np.tile(np.arange(C), (N, 8, 1)), axis=2))
def runs(rng, when, same=False):
    o, go = np.zeros((N, 8, C), np.int64), np.zeros((N, 8, C), bool)
    for r in range(N):
        k = rng.permutation(C)
        for g in range(8):
            p = r ^ MASK[when[g]]
            if p < r: continue
            if not same: k = rng.permutation(C)
            for i, m in ((r, [1, 0, 3, 2]), (p, [2, 0, 3, 1])):
                q = rng.permuted(k.reshape(4, -1), axis=1)[m]
                o[i, g] = np.concatenate([q[:2].T.reshape(-1), q[2:].T.reshape(-1)])
                go[i, g, q[:2].reshape(-1)] = True
    return following(o), go
def stored(e):
    return {"nx": np.stack([gtable(e[r]) for r in range(N)])}
def layers(rng, still=[]):
    w = np.array(f(rng, N, 128, 2048)).reshape(N, 8, 16, 4, 8, 16, 4)
    for i in still:
        w[:, :, i] = 0
        w[:, :, :, :, :, i] = 0
    return w
def weights(rng, w):
    c, s = packed(np.ascontiguousarray(w).reshape(N, 128, 2048), rng)
    return {"wc": c, "ws": s}
def setup_inputs(rng):
    return {**numbers_of(rng), **stored(rings(rng)), **weights(rng, layers(rng))}
def setup_inputs_ties(rng):
    d = numbers_of(rng)
    o = rng.permutation(N)
    k = rng.integers(-1, 2, (N, 8, C)).astype(np.float32)
    k[o[1]] = 1
    x = d["x"].reshape(N, 8, 16, C, 4)
    x[:, :, 0] = 0
    x[:, :, 0, :, 0] = k.astype(BF)
    c = np.ones(N, np.float32)
    c[o[0]] = 0
    c[o[2]] = -1
    u = d["u"].reshape(N, 128, 128, 4)
    u[:, :, ::16] = 0
    for h in range(0, 128, 16): u[:, h, h, 0] = c.astype(BF)
    e, i = rings(rng), np.arange(C)
    for r in range(N):
        p, h = r ^ MASK[0], rng.permutation(8)
        if p < r: continue
        e[p, h[0]] = e[r, h[0]]
        e[p, h[1]] = np.argsort(e[r, h[1]])
        e[r, h[2]], e[p, h[2]] = (i + 1) % C, (i - 1) % C
        e[r, h[3]] = e[p, h[3]] = (i + 1) % C
    w = layers(rng)
    w[:, :, :, :, :, :8] = 0
    return {"x": x.reshape(N, 128, 4 * C), "u": u.reshape(N, 128, 512), "v": d["v"], **stored(e), **weights(rng, w)}
def setup_inputs_near(rng):
    d = numbers_of(rng)
    o = rng.permutation(N) % 4
    k = np.where(o % 2 == 0, 1.0, 2.0 ** -30)
    x = np.zeros((N, 8, 16, C, 4))
    s = rng.integers(-1, 2, (N, 8, C)) * k[:, None, None]
    x[:, :, 0, :, 0] = 1.125 * s
    x[:, :, 1, :, 0] = -1.25 * s
    x[:, :, 8, :, 0] = rng.integers(-1, 2, (N, 8, C)) * 2.0 ** -27
    x[:, :, 8, :, 1] = 2.0 ** -27
    x[:, :, 9:] = (1.0 + rng.integers(0, 128, (N, 8, 7, C, 4)) * 2.0 ** -7) * 2.0 ** -27 * rng.choice([-1.0, 1.0], (N, 8, 7, C, 4))
    w = layers(rng, list(range(9)))
    for r in range(N):
        if o[r] % 2 == 1: x[r, :, 7, :, 0] = 2.0 ** -26
        if o[r] == 3:
            x[r, :, :2] = 0
            x[r, :, 7, :, 0] = 2.0 ** -27
            for g in range(8):
                w[r, g, 8, 0, g, 0, 0] = 2.0 ** -10
                w[r, g, 8, 0, g, 0, 1] = 2.0 ** -8
                w[r, g, 8, 0, g, 1, 0] = -2.0 ** -10
                w[r, g, 8, 0, g, 1, 1] = -1.125 * 2.0 ** -8
        else:
            at = [0, C - 1, int(rng.integers(C)), int(rng.integers(C))]
            for g, j in zip(rng.permutation(8)[:4], at): x[r, g, 0, j, 0] = 2.0 ** 30 * rng.choice([-1.0, 1.0])
    u = d["u"].reshape(N, 128, 128, 4)
    u[:, :, ::16] = 0
    for h in range(0, 128, 16):
        u[:, h, h, 0] = (1.125 * k).astype(np.float32).astype(BF)
        u[:, h + 1, h, 0] = k.astype(np.float32).astype(BF)
    return {"x": x.astype(np.float32).reshape(N, 128, 4 * C).astype(BF), "u": u.reshape(N, 128, 512), "v": d["v"], **stored(rings(rng)), **weights(rng, w)}
def setup_inputs_runs(rng):
    d = numbers_of(rng)
    o = rng.permutation(8)
    when = np.zeros(8, np.int64)
    when[o[4:6]] = 1
    when[o[6:]] = 2
    e, go = runs(rng, when)
    low = -rng.integers(0, 2, (N, 8, C))
    t = np.where(go, 1, low)
    for r in range(N):
        h = rng.permutation(o[:4])
        t[r, h[0]] = 1
        t[r, h[1]] = low[r, h[1]]
    for g in o[4:]:
        for i in range(when[g]): t[:, g] = np.take_along_axis(t[:, g], e[:, g], axis=1)
    x = (1.0 + (2 * rng.integers(0, 64, (N, 16, 8, C, 4)) + 1) * 2.0 ** -7) * np.exp2(-rng.integers(0, 7, (N, 16, 8, C, 4)).astype(np.float64)) * rng.choice([-1.0, 1.0], (N, 16, 8, C, 4))
    c = rng.choice([-1.0, 1.0], (N, 16, 1))
    k = np.exp2(when - 8.0)[:, None]
    x[:, :, 0, :, 0] = np.where(rng.random((N, 16, C)) < 0.5, 1.96875, 1.875) * 2.0 ** 8 * c
    x[:, :, 3, :, 0] = 1.875 * 2.0 ** 7
    x[:, ::2, 1, :, 0] = (8 + t) * k
    x[:, ::2, 2, :, 0] = 8 * k
    u = d["u"].reshape(N, 128, 128, 4)
    u[:, :, ::16] = 0
    for h in range(0, 128, 16):
        u[:, h + 1, h, 0] = 1
        u[:, h + 2, h, 0] = -1
    w = layers(rng, [0, 3, 8, 11])
    for g in range(8):
        for i in (0, 1):
            w[:, g, 8 * i + 3, 0, g, 8 * i, 0] = (64 * c[:, 2 * g + i, 0]).astype(np.float32).astype(BF)
            w[:, g, 8 * i + 3, 0, g, 8 * i + 3, 0] = 32
    for g in o[4:]:
        x[:, 2 * g, 4, :, 0] = -1.0
        x[:, 2 * g, 5, :, 0] = 1.0 - when[g]
        u[:, 16 * g + 4, 16 * g, 0] = 1
        for i in (1, 2, 4, 5): w[:, :, :, :, g, i] = 0
        w[:, g, 4, 0, g, 4, 0] = -32
        w[:, g, 5, 0, g, 4, 0] = 64
        w[:, g, 5, 0, g, 5, 0] = -32
    return {"x": x.astype(np.float32).reshape(N, 128, 4 * C).astype(BF), "u": u.reshape(N, 128, 512), "v": d["v"], **stored(e), **weights(rng, w)}
def setup_inputs_ends(rng):
    d = numbers_of(rng)
    e, go = runs(rng, np.zeros(8, np.int64), True)
    o = rng.permutation(N) % 4
    s = go[:, 0] * 2.0 - 1.0
    small = (1.0 + 0.125 * rng.integers(0, 8, (N, 8, 16, C, 4))) * 2.0 ** -20
    x = (0.9 + 0.1 * rng.random((N, 8, 16, C, 4))) * 2.0 ** 30
    u = d["u"].astype(np.float32).reshape(N, 128, 128, 4)
    v = np.zeros((N, 128, 512), np.float32)
    w = np.zeros((N, 128, 4, 128, 4), np.float32)
    i = np.arange(128)
    for r in range(N):
        if o[r] == 0: x[r] *= s[r][:, None]
        if o[r] == 1: x[r] *= -1
        if o[r] == 2: x[r] *= rng.choice([-1.0, 1.0], (8, 1, C, 1))
        if o[r] == 3: x[r] = small[r] * s[r][:, None]
        x[r, 7, 8:] = small[r, 7, 8:] * rng.choice([-1.0, 1.0], (8, C, 4))
        c = np.array([0.0, 1, 1, 1, -1, -1, -1, -1])[rng.permutation(8)][None, :, None]
        if o[r] < 3: u[r, :, ::16] = c * (0.9 + 0.1 * rng.random((128, 8, 4))) * 2.0 ** 30
        else: u[r, :, ::16] = c * (1.0 + 0.125 * rng.integers(0, 8, (128, 8, 4))) * 2.0 ** -30
        if o[r] < 2: v[r] = (0.9 + 0.1 * rng.random((128, 512))) * 2.0 ** 30
        else: v[r] = (1.0 + 0.125 * rng.integers(0, 8, (128, 512))) * 2.0 ** -30
        v[r] *= rng.choice([-1.0, 1.0], (128, 512))
        k = np.full(128, 32.0)
        if o[r] == 3: k = np.where(i < 120, 2.0 ** -8, 2.0 ** 8)
        for b in range(4): w[r, i, b, i, b] = k
    return {"x": x.astype(np.float32).reshape(N, 128, 4 * C).astype(BF), "u": u.reshape(N, 128, 512).astype(BF), "v": v.astype(BF), **stored(e), **weights(rng, w.astype(BF))}
def setup_inputs_spread(rng):
    d = setup_inputs(rng)
    d["x"] = wide(rng, N, 128, 4 * C, cols=6)
    return d
def check_inputs(d):
    b = []
    for k in ("x", "u", "v"):
        a = np.abs(d[k].astype(np.float32))
        if not (np.isfinite(a).all() and ((a == 0) | (a >= 2.0 ** -30) & (a <= 2.0 ** 30)).all()): b.append("a value of " + k)
    if not ((d["nx"] >= 0) & (d["nx"] < C)).all(): b.append("an entry of nx")
    else:
        e = np.concatenate([gentries(d["nx"][r]) for r in range(N)])
        at, back = np.zeros(8 * N, np.int64), np.zeros(8 * N, np.int64)
        for i in range(1, C + 1):
            at = e[np.arange(8 * N), at]
            back = np.where((at == 0) & (back == 0), i, back)
        if not (back == C).all(): b.append("a ring of nx")
    none, least, most = [emit(mx_ref.quantize(np.full((128, 16), k, np.float32).astype(BF)))[1][0, 0] for k in (0.0, 2.0 ** -8, 2.0 ** 8)]
    for r in range(N):
        if ((d["wc"][r] == 0x7F) | (d["wc"][r] == 0xFF)).any(): b.append("wc: a code that is no number")
        s = mx_ref.live(d["ws"][r])
        if ((s != none) & ((s < least) | (s > most))).any(): b.append("ws: a scale out of range")
    return b
def at(a, e):
    return np.take_along_axis(a, e, axis=1)
def mean(a, b):
    return ((a.astype(np.float32) + b.astype(np.float32)) * np.float32(0.5)).astype(BF)
def reference(x, u, v, nx, wc, ws):
    qu = [mx_ref.quantize(u[r]) for r in range(N)]
    lay = [pk(wc[r], ws[r]) for r in range(N)]
    ring = [gentries(nx[r]).astype(np.int64) for r in range(N)]
    now = [x[r] for r in range(N)]
    for m in MASK:
        t, new, back, z = [], [], [], []
        for r in range(N):
            q = mx_ref.quantize(now[r])
            t.append(decode(q).astype(BF))
            up = mx_ref.matmul(qu[r], q)[::16] > 0
            guest = ring[r ^ m]
            host = np.argsort(guest, axis=1)
            leave = up & ~at(up, host)
            a = ring[r]
            for i in range(8):
                a = np.where(at(leave, a), at(a, a), a)
            new.append(np.where(leave, at(a, host), np.where(at(leave, guest), guest, a)))
            back.append(np.argsort(new[r], axis=1))
            z.append(mx_ref.quantize(mean(gcols(t[r], new[r]), gcols(t[r], back[r]))))
        for r in range(N):
            h = tile([mx_ref.matmul(pick(lay[r], np.arange(128 * b, 128 * b + 128)), z[r ^ m]) * np.float32(0.03125) for b in range(4)])
            now[r] = mean(gcols(t[r], back[r]), gcols(h, new[r]))
        ring = new
    y, nr = np.zeros((N, 128, C), np.float32), np.zeros((N, 8, C), np.float32)
    oc, osc = np.zeros((N, 128, 4 * C), np.uint8), np.zeros((N, 16, C), np.uint8)
    for r in range(N):
        q = mx_ref.quantize(now[r])
        y[r] = mx_ref.matmul(mx_ref.quantize(v[r]), q)
        nr[r] = ring[r]
        oc[r], osc[r] = emit(q)
    return {"y": y, "nr": nr, "oc": oc, "osc": osc}

@@ -1,0 +1,525 @@
+from concourse.mybir import dt, AluOpType, ActivationFunctionType
+
+C = 352
+CH = [(0, 224), (224, 352)]
+CH0 = [(0, 192), (192, 352)]
+MASKS = [1, 2, 4]
+ROUNDS = 3
+W16 = C // 16
+K = float(2 ** 20)
+GS = 160
+TOP = 6
+F8 = "float8_e4m3fn_x4"
+
+SCRATCH = {
+    "nxi": ("sbuf", [128, W16], "int32"), "lnxi": ("sbuf", [128, W16], "int32"),
+    "ut": ("sbuf", [128, 512], "bfloat16"), "vt": ("sbuf", [128, 512], "bfloat16"),
+    "wq": ("sbuf", [128, 512], F8), "wsq": ("sbuf", [128, 512], "uint8"),
+    "uq": ("sbuf", [128, 128], F8), "uqs": ("sbuf", [128, 128], "uint8"),
+    "up16": ("sbuf", [128, 128], F8), "up16s": ("sbuf", [128, 128], "uint8"),
+    "vq": ("sbuf", [128, 128], F8), "vqs": ("sbuf", [128, 128], "uint8"),
+    "eq": ("sbuf", [128, 512], F8), "eqs": ("sbuf", [128, 512], "uint8"),
+    "zq": ("sbuf", [128, C], F8), "zqs": ("sbuf", [128, C], "uint8"),
+    "EB": ("sbuf", [128, 516], "bfloat16"), "ONES": ("sbuf", [128, 2 * C], "bfloat16"),
+    "pi": ("sbuf", [128, 1], "int32"), "pj": ("sbuf", [128, 1], "int32"),
+    "FS": ("sbuf", [128, 2 * C + 8], "float32"), "RS": ("sbuf", [128, 2 * C + 8], "float32"),
+    "inv": ("sbuf", [128, 2 * C], "bfloat16"),
+    "cab": ("sbuf", [128, 2 * W16], "float32"), "tab": ("sbuf", [128, 2 * W16], "float32"),
+    "iab": ("sbuf", [128, 2 * W16], "int32"), "jab": ("sbuf", [128, 2 * W16], "int32"),
+    "PA": ("psum", [128, 2048], "float32"), "PB": ("psum", [128, 1024], "float32"), "PS": ("psum", [128, 1024], "float32"),
+}
+for _n in ("X0", "X1", "TH", "THP", "TB", "TBP", "Z", "HH"):
+    SCRATCH[_n] = ("sbuf", [128, 4 * C], "bfloat16")
+for _n in ("RC", "NC", "CNT"):
+    SCRATCH[_n] = ("sbuf", [128, 2 * C], "float32")
+for _n in ("IOTA", "J16", "t1", "CODD", "CEV", "PTa", "PTb", "PTc", "OB", "SELO", "SELA", "SELP", "SEL0", "SEL1", "SEL2",
+           "POS", "BPS", "APS", "VBP", "GA", "GB", "ysb", "nrs"):
+    SCRATCH[_n] = ("sbuf", [128, C], "float32")
+for _n in ("SELD", "SELB", "sc", "upf", "lv", "LS"):
+    SCRATCH[_n] = ("sbuf", [128, C], "bfloat16")
+for _n in ("p16", "p16h", "off", "noff", "thrB", "thr2", "thr3"):
+    SCRATCH[_n] = ("sbuf", [128, 1], "float32")
+for _n in ("C16", "jw", "offi", "offg", "m1", "m2", "m3", "posw", "af", "dpos"):
+    SCRATCH[_n] = ("sbuf", [128, W16], "float32")
+for _n in ("l16", "La", "Lb", "slw", "p2u", "ow", "aw"):
+    SCRATCH[_n] = ("sbuf", [128, W16], "uint16")
+for _k in range(1, ROUNDS + 2):
+    SCRATCH["xq%d" % _k] = ("sbuf", [128, C], F8)
+    SCRATCH["xs%d" % _k] = ("sbuf", [128, C], "uint8")
+for _k in range(1, ROUNDS + 1):
+    SCRATCH["lq%d" % _k] = ("sbuf", [128, C], F8)
+    SCRATCH["ls%d" % _k] = ("sbuf", [128, C], "uint8")
+    for _n in ("abw", "lab", "lnx"):
+        SCRATCH[_n + str(_k)] = ("sbuf", [128, 2 * W16], "uint16")
+
+LOCAL = ["nx", "x", "u", "ws", "wc", "v", "y0", "y1", "nr", "oc0", "oc1", "osc0", "osc1", "osc2", "osc3"]
+REMOTE = ["nx", "nx2", "nx3", "ab1", "ab2", "ab3"] + [n + str(k) + str(c) for k in (1, 2, 3) for n in "qs" for c in (0, 1)]
+SEMAPHORES = ["cv", "cs", "ct", "cg"] + ["d_" + n for n in LOCAL] + ["r_" + n for n in REMOTE] + ["l_" + n for n in REMOTE]
+
+
+def rank_program(g, core, T, topo):
+    rank = T.rank_of(core)
+    if rank is None:
+        return
+    A = AluOpType
+    AF = ActivationFunctionType
+    eng = {"v": g.vector, "s": g.scalar, "t": g.tensor, "g": g, "y": g.sync}
+    total, know = {}, {q: {} for q in eng}
+    writes, reads = {}, {}
+
+    def norm(k):
+        return k if isinstance(k, tuple) else (k, 0, 1 << 20)
+
+    def conflicts(table, k):
+        return [e for e in table.get(k[0], []) if e[0] < k[2] and k[1] < e[1]]
+
+    def order(q, rd, wr):
+        need = []
+        for k in rd:
+            need += [e[2] for e in conflicts(writes, k)]
+            if k[0] in ("PA", "PB", "PS"):
+                need += [e[2] for e in conflicts(reads, k) if e[2][3] != q]
+        for k in wr:
+            need += [e[2] for e in conflicts(writes, k)]
+            need += [e[2] for e in conflicts(reads, k)]
+        kn = know[q]
+        want = {}
+        for sem, val, clock, _ in need:
+            if kn.get(sem, 0) < val and want.get(sem, (0,))[0] < val:
+                want[sem] = (val, clock)
+        for sem in list(want):
+            if any(o != sem and want[o][1].get(sem, 0) >= want[sem][0] for o in want):
+                del want[sem]
+        for sem, (val, clock) in want.items():
+            eng[q].wait_ge(T.sem[sem], val)
+            for s2, v2 in clock.items():
+                kn[s2] = max(kn.get(s2, 0), v2)
+            kn[sem] = max(kn.get(sem, 0), val)
+
+    def note(q, sem, inc, rd, wr):
+        total[sem] = total.get(sem, 0) + inc
+        clock = dict(know[q])
+        clock[sem] = total[sem]
+        ev = (sem, total[sem], clock, q)
+        for k in wr:
+            for t in (writes, reads):
+                t[k[0]] = [e for e in t.get(k[0], []) if not (k[1] <= e[0] and e[1] <= k[2])]
+            writes[k[0]].append((k[1], k[2], ev))
+        for k in rd:
+            reads[k[0]] = reads.get(k[0], []) + [(k[1], k[2], ev)]
+
+    COUNT = {"v": "cv", "s": "cs", "t": "ct", "g": "cg"}
+
+    def op(q, call, rd, wr):
+        rd, wr = [norm(k) for k in rd], [norm(k) for k in wr]
+        order(q, rd, wr)
+        call().then_inc(T.sem[COUNT[q]], 1)
+        note(q, COUNT[q], 1, rd, wr)
+
+    def dma(q, name, out, in_, rd, wr):
+        rd, wr = [norm(k) for k in rd], [norm(k) for k in wr]
+        order(q, rd, wr)
+        eng[q].dma_start(out, in_).then_inc(T.sem["d_" + name], 16)
+        note(q, "d_" + name, 16, rd, wr)
+
+    def send(name, dst, out, in_, rd):
+        order("g", [norm(rd)], [])
+        rid, pid = topo.addr(dst)[:2]
+        g.remote_dma(out, in_, T.sem["r_" + name], T.sem["l_" + name], pid, rid, topo.mask(core, dst))
+        note("g", "l_" + name, len(topo.engines(core, dst)), [norm(rd)], [])
+
+    def arrives(name, src, buf, lo=0, hi=1 << 20):
+        n = len(topo.engines(src, core))
+        total["r_" + name] = n
+        writes[buf] = writes.get(buf, []) + [(lo, hi, ("r_" + name, n, {"r_" + name: n}, "x"))]
+
+    partner = [T.cores[rank ^ m] for m in MASKS]
+    for k in (1, 2, 3):
+        for c, (lo, hi) in enumerate(CH):
+            arrives("q%d%d" % (k, c), partner[k - 1], "lq%d" % k, lo, hi)
+            arrives("s%d%d" % (k, c), partner[k - 1], "ls%d" % k, lo, hi)
+        arrives("ab%d" % k, partner[k - 1], "lab%d" % k)
+    arrives("nx", partner[0], "lnxi")
+    for k in (2, 3):
+        arrives("nx%d" % k, partner[k - 1], "lnx%d" % k)
+
+    V, S = g.vector, g.scalar
+
+    def ts(out, in0, s1, s2, o0, o1, rd, wr):
+        if o1 is None:
+            op("v", lambda: V.tensor_scalar(out, in0, s1, None, o0), rd, wr)
+        else:
+            op("v", lambda: V.tensor_scalar(out, in0, s1, s2, o0, o1), rd, wr)
+
+    def tt(out, in0, in1, o, rd, wr):
+        op("v", lambda: V.tensor_tensor(out, in0, in1, o), rd, wr)
+
+    def vcopy(out, in_, rd, wr):
+        op("v", lambda: V.tensor_copy(out, in_), rd, wr)
+
+    def fill(ap, val, wr):
+        op("v", lambda: V.memset(ap, val), [], wr)
+
+    def scan(out, d0, d1, init, o0, o1, rd, wr):
+        op("v", lambda: V.tensor_tensor_scan(out, d0, d1, init, o0, o1), rd, wr)
+
+    def keep16(out, src, rd, wr):
+        n = out.shape[1]
+        scan(out, T.SELD[:, 0:n], src, 0.0, A.add, A.max, ["SELD"] + rd, wr)
+
+    def act(out, in_, rd, wr, scale=None):
+        if scale is None:
+            op("s", lambda: S.activation(out, in_, AF.Copy), rd, wr)
+        else:
+            op("s", lambda: S.activation(out, in_, AF.Copy, scale=scale), rd, wr)
+
+    def sid(out, in_, rd, wr, scale, bias):
+        op("s", lambda: S.activation(out, in_, AF.Identity, bias=bias, scale=scale), rd, wr)
+
+    def quant(codes, plane, lo, hi, src, rd):
+        op("v", lambda: V.quantize_mx(T[codes][:, lo:hi], T[plane][:, lo:hi], src), rd, [(codes, lo, hi), (plane, lo, hi)])
+
+    def mm(P, s, n, l, ls, a, r, rs, lo, hi):
+        op("t", lambda: g.tensor.matmul_mx(T[P][:, 512 * s:512 * s + n], T[l][:, a:a + 128], T[ls][:, a:a + 128],
+                                           T[r][:, lo:hi], T[rs][:, lo:hi], True, True),
+           [(l, a, a + 128), (ls, a, a + 128), (r, lo, hi), (rs, lo, hi)], [(P, 512 * s, 512 * s + 512)])
+
+    def bank(P, s, n):
+        return T[P][:, 512 * s:512 * s + n], (P, 512 * s, 512 * s + 512)
+
+    dma("y", "nx", T.nxi[:], T.nx[:], [], ["nxi"])
+    dma("s", "x", T.X0[:], T.x[:], [], ["X0"])
+    dma("y", "u", T.ut[:], T.u[:], [], ["ut"])
+    dma("y", "ws", T.wsq[:], T.ws[:], [], ["wsq"])
+    dma("y", "wc", T.wq[:].bitcast(dt.uint8), T.wc[:], [], ["wq"])
+    dma("y", "v", T.vt[:], T.v[:], [], ["vt"])
+
+    def iota(name, pattern):
+        op("g", lambda: g.iota(T[name][:], pattern, 0, 0, allow_small_or_imprecise_dtypes=True), [], [name])
+
+    op("g", lambda: g.iota(T.pi[:], [[0, 1]], 0, 1), [], ["pi"])
+    iota("J16", [[0, W16], [1, 16]])
+    iota("IOTA", [[1, C]])
+    iota("C16", [[16, W16]])
+    send("nx", partner[0], T.lnxi[:], T.nxi[:], "nxi")
+
+    ts(T.pj[:], T.pi[:], 15, None, A.bitwise_and, None, ["pi"], ["pj"])
+    fill(T.ONES[:], 1.0, ["ONES"])
+    ts(T.p16h[:], T.pj[:], 0.5, None, A.add, None, ["pj"], ["p16h"])
+    ts(T.p16[:], T.pj[:], 0.0, None, A.add, None, ["pj"], ["p16"])
+    ts(T.t1[:], T.J16[:], T.p16h[:, 0:1], 2.0 ** 26, A.subtract, A.mult, ["J16", "p16h"], ["t1"])
+    ts(T.off[:], T.p16[:], -K, 15.0 * K, A.mult, A.add, ["p16"], ["off"])
+    ts(T.SELD[:], T.t1[:], K, None, A.min, None, ["t1"], ["SELD"])
+    vcopy(T.La[:], T.nxi[:], ["nxi"], ["La"])
+    fill(T.ow[:], 0, ["ow"])
+    fill(T.OB[:, 0:1], 0.0, [("OB", 0, 1)])
+    op("g", lambda: g.affine_select(T.EB[:], T.ONES[:, 0:516], [[1, 516]], A.is_equal, 0.0, -4, -4), ["ONES"], ["EB"])
+
+    def table(i):
+        if i == 1:
+            sid(T.jw[:], T.C16[:], ["C16", "p16"], ["jw"], 1.0, T.p16[:, 0:1])
+            sid(T.offi[:], T.jw[:], ["jw", "off"], ["offi"], 1024.0, T.off[:, 0:1])
+        if i == 2:
+            sid(T.CODD[:], T.IOTA[:], ["IOTA"], ["CODD"], 1024.0, 512.0)
+        if i == 3:
+            act(T.CEV[:], T.IOTA[:], ["IOTA"], ["CEV"], scale=1024.0)
+        if i == 4:
+            sid(T.offg[:], T.offi[:], ["offi"], ["offg"], 1.0, 512.0)
+            sid(T.noff[:], T.off[:], ["off"], ["noff"], -1.0, 0.0)
+        if i == 7:
+            sid(T.thrB[:], T.off[:], ["off"], ["thrB"], 2.0 ** -19, 0.5)
+            sid(T.thr2[:], T.off[:], ["off"], ["thr2"], 1.0, 400000.0)
+            sid(T.thr3[:], T.off[:], ["off"], ["thr3"], 1.0, -600000.0)
+            sid(T.FS[:, 0:1], T.p16[:], ["p16"], [("FS", 0, 1)], 0.0, -float(2 ** 20))
+            sid(T.RS[:, 2 * C + 7:2 * C + 8], T.p16[:], ["p16"], [("RS", 2 * C + 7, 2 * C + 8)], 0.0, float(2 ** 19))
+
+    def ucols():
+        vcopy(T.l16[:], T.C16[:], ["C16"], ["l16"])
+        quant("uq", "uqs", 0, 128, T.ut[:], ["ut"])
+        vcopy(T.up16[:, 0:128].bitcast(dt.uint32), T.uq[:, 0:128].bitcast(dt.uint32).indirect(T.l16[:, 0:8]), ["uq", "l16"], ["up16"])
+        act(T.up16s[:, 0:128], T.uqs[:, 0:128].indirect(T.l16[:, 0:8]), ["uqs", "l16"], ["up16s"])
+
+    def etiles():
+        for b in range(4):
+            quant("eq", "eqs", 128 * b, 128 * b + 128, T.EB[:, 4 - b:516 - b], ["EB"])
+
+    def scores(k, c):
+        lo, hi = CH[c]
+        mm("PS", c, hi - lo, "up16", "up16s", 0, "xq%d" % k, "xs%d" % k, lo, hi)
+
+    def ship(k, c):
+        p, (lo, hi) = partner[k - 1], CH[c]
+        send("q%d%d" % (k, c), p, T["lq%d" % k][:, lo:hi].bitcast(dt.uint8), T["xq%d" % k][:, lo:hi].bitcast(dt.uint8), ("xq%d" % k, lo, hi))
+        send("s%d%d" % (k, c), p, T["ls%d" % k][:, lo:hi], T["xs%d" % k][:, lo:hi], ("xs%d" % k, lo, hi))
+
+    def signs():
+        for c, (lo, hi) in enumerate(CH):
+            src, key = bank("PS", c, hi - lo)
+            op("s", lambda: S.activation(T.sc[:, lo:hi], src, AF.Sign), [key], [("sc", lo, hi)])
+            ts(T.upf[:, lo:hi], T.sc[:, lo:hi], 0.0, None, A.max, None, [("sc", lo, hi)], [("upf", lo, hi)])
+
+    def unpack(k):
+        for b in range(4):
+            mm("PA", b, C, "eq", "eqs", 128 * b, "xq%d" % k, "xs%d" % k, 0, C)
+
+    def keep(b):
+        src, key = bank("PA", b, C)
+        act(T.TH[:, C * b:C * b + C], src, [key], [("TH", C * b, C * b + C)], scale=0.5)
+
+    def unpack_far(k, b):
+        src, key = bank("PB", b % 2, C)
+        mm("PB", b % 2, C, "eq", "eqs", 128 * b, "lq%d" % k, "ls%d" % k, 0, C)
+        act(T.THP[:, C * b:C * b + C], src, [key], [("THP", C * b, C * b + C)], scale=0.5)
+
+    def places():
+        keep16(T.SELP[:], T.POS[:], ["POS"], ["SELP"])
+        sid(T.posw[:], T.SELP[:, 15:C:16], ["SELP", "noff"], ["posw"], 1.0, T.noff[:, 0:1])
+
+    def lay_order():
+        ts(T.p2u[:], T.SELP[:, 15:C:16], T.off[:, 0:1], 2.0 ** -10, A.subtract, A.mult, ["SELP", "off"], ["p2u"])
+        op("v", lambda: V.tensor_copy(T.OB[:].indirect(T.p2u[:]), T.IOTA[:]), ["IOTA", "p2u"], ["OB"])
+
+    def far_ring(lst, key):
+        act(T.APS[:], T.IOTA[:].indirect(T[lst][:, 0:W16]), ["IOTA", key], ["APS"])
+
+    def far_places(lst):
+        sid(T.VBP[:], T.POS[:].indirect(T[lst][:, W16:2 * W16]), ["POS", lst], ["VBP"], 1.0, 512.0)
+
+    def guests(lo, hi):
+        tt(T.RC[:, 1 + 2 * lo:2 * hi:2], T.APS[:].indirect(T.ow[:, lo // 16:hi // 16]), T.CODD[:, lo:hi], A.add,
+           ["APS", ("ow", lo, hi), "CODD"], [("RCO", lo, hi)])
+
+    def evens(lo, hi):
+        tt(T.RC[:, 2 * lo:2 * hi:2], T.OB[:, lo:hi], T.CEV[:, lo:hi], A.add, [("OB", lo, hi), "CEV"], [("RCE", lo, hi)])
+
+    def guest_scan(lo, hi):
+        keep16(T.SELA[:, lo:hi], T.RC[:, 1 + 2 * lo:2 * hi:2], [("RCO", lo, hi)], [("SELA", lo, hi)])
+
+    def guest_cols():
+        tt(T.af[:], T.SELA[:, 15:C:16], T.offg[:], A.subtract, ["SELA", "offg"], ["af"])
+
+    def guest_list():
+        vcopy(T.aw[:], T.af[:], ["af"], ["aw"])
+
+    def hosts():
+        keep16(T.SEL0[:], T.VBP[:], ["VBP"], ["SEL0"])
+        tt(T.dpos[:], T.SEL0[:, 15:C:16], T.SELP[:, 15:C:16], A.subtract, ["SEL0", "SELP"], ["dpos"])
+
+    def negatives():
+        sid(T.NC[:], T.RC[:], ["RCE", "RCO"], ["NC"], 1.0, -float(2 ** 19))
+
+    def leavers(lst):
+        tt(T.lv[:], T.upf[:].indirect(T[lst][:, W16:2 * W16]), T.sc[:], A.is_lt, ["upf", "sc", lst], ["lv"])
+
+    def void_evens():
+        act(T.inv[:, 0:2 * C:2], T.lv[:].indirect(T.ow[:]), ["lv", "ow"], ["inve"])
+
+    def leaver_bits():
+        scan(T.LS[:], T.SELB[:], T.lv[:], 0.0, A.add, A.max, ["SELB", "lv"], ["LS"])
+
+    def splice(k):
+        lst, abw = "lnx%d" % k, "abw%d" % k
+        h = W16
+        if k > 1:
+            leavers(lst)
+            keep(0)
+            keep(1)
+            void_evens()
+        sid(T.inv[:, 1 + 2 * GS:2 * C:2], T.lv[:].indirect(T.aw[:, GS // 16:h]), ["lv", "aw"], ["invp"], -1.0, 1.0)
+        if k > 1:
+            leaver_bits()
+        ts(T.inv[:, 1:2 * GS:2], T.lv[:].indirect(T.aw[:, 0:GS // 16]), -1.0, 1.0, A.mult, A.add, ["lv", "aw"], ["invo"])
+        ts(T.m1[:], T.LS[:, 15:C:16], T.thrB[:, 0:1], None, A.is_ge, None, ["LS", "thrB"], ["m1"])
+        tt(T.m2[:], T.m1[:], T.dpos[:], A.mult, ["m1", "dpos"], ["m2"])
+        tt(T.m3[:], T.m2[:], T.posw[:], A.add, ["m2", "posw"], ["m3"])
+        ts(T.slw[:], T.m3[:], 2.0 ** -9, None, A.mult, None, ["m3"], ["slw"])
+        keep(2)
+        keep(3)
+        void = ["inve", "invo", "invp"]
+        scan(T.FS[:, 1:2 * C + 1], T.inv[:], T.NC[:], -float(2 ** 20), A.mult, A.min, void + ["NC"], [("FS", 1, 2 * C + 8)])
+        act(T.GB[:], T.FS[:, 0:2 * C].indirect(T.slw[:]), ["FS", "slw"], ["GB"])
+        scan(T.RS[:, 2 * C + 6:6:-1], T.inv[:, ::-1], T.RC[:, ::-1], float(2 ** 19), A.mult, A.max,
+             void + ["RCE", "RCO"], [("RS", 0, 2 * C + 7)])
+        act(T.GA[:], T.RS[:, 8:2 * C + 8].indirect(T.slw[:]), ["RS", "slw"], ["GA"])
+        keep16(T.SEL1[:], T.GB[:], ["GB"], ["SEL1"])
+        sid(T.cab[:, h:2 * h], T.SEL1[:, 15:C:16], ["SEL1", "noff"], [("cab", h, 2 * h)], 1.0, T.noff[:, 0:1])
+        if k < ROUNDS:
+            scan(T.CNT[:, 0:C], T.ONES[:, 0:C], T.inv[:, 0:C], -1.0, A.add, A.subtract, ["ONES"] + void, [("CNT", 0, C)])
+        else:
+            quant("vq", "vqs", 0, 128, T.vt[:], ["vt"])
+        keep16(T.SEL2[:], T.GA[:], ["GA"], ["SEL2"])
+        sid(T.cab[:, 0:h], T.SEL2[:, 15:C:16], ["SEL2", "noff"], [("cab", 0, h)], 1.0, T.noff[:, 0:1])
+        ts(T.tab[:, h:2 * h], T.SEL1[:, 15:C:16], T.thr3[:, 0:1], T.FS[:, 2 * C:2 * C + 1], A.is_le, A.mult, ["SEL1", "thr3", "FS"], [("tab", h, 2 * h)])
+        ts(T.tab[:, 0:h], T.SEL2[:, 15:C:16], T.thr2[:, 0:1], T.RS[:, 7:8], A.is_ge, A.mult, ["SEL2", "thr2", "RS"], [("tab", 0, h)])
+        tt(T.iab[:], T.cab[:], T.tab[:], A.add, ["cab", "tab"], ["iab"])
+        ts(T.jab[:], T.iab[:], 511, None, A.bitwise_and, None, ["iab"], ["jab"])
+        vcopy(T[abw][:], T.jab[:], ["jab"], [abw])
+        send("ab%d" % k, partner[k - 1], T["lab%d" % k][:], T[abw][:], abw)
+        if k < ROUNDS:
+            send("nx%d" % (k + 1), partner[k], T["lnx%d" % (k + 1)][:], T[abw][:], abw)
+
+    def jump(out, win, lst, share):
+        for lo, hi in CH0[::-1] if share else CH0:
+            (vcopy if share and lo == 0 else act)(T[out][:, lo:hi], T[win][:].indirect(T[lst][:, lo // 16:hi // 16]), [win, lst], [(out, lo, hi)])
+
+    def ahead(P, m, n, a):
+        b = 0 if m < 16 else m
+        act(T.OB[:, m:m + n], T[P][:].indirect(T.ow[:, a // 16:(a + n) // 16]), [P, ("ow", a, a + n)], [("OB", m, m + n)])
+        keep16(T.SELO[:, b:b + n], T.OB[:, b:b + n], [("OB", b, b + n)], [("SELO", b, b + n)])
+
+    def enlist(m, n):
+        b = 0 if m < 16 else m
+        ts(T.ow[:, b // 16:(b + n) // 16], T.SELO[:, b + 15:b + n:16], T.off[:, 0:1], None, A.subtract, None,
+           [("SELO", b, b + n), "off"], [("ow", b, b + n)])
+
+    jump("PTa", "IOTA", "La", True)
+    for i in range(TOP + 1):
+        L, L2 = ("La", "Lb") if i % 2 == 0 else ("Lb", "La")
+        P, P2 = (("PTa", "PTb"), ("PTb", "PTc"), ("PTc", "PTa"))[i % 3]
+        n = "SEL%d" % (i % 3)
+        if i < TOP:
+            jump(P2, P, L, i < 3)
+        if i < TOP - 1:
+            for lo, hi in CH0:
+                keep16(T[n][:, lo:hi], T[P2][:, lo:hi], [(P2, lo, hi)], [(n, lo, hi)])
+        ahead(P, 2 ** i, max(16, 2 ** i), 0)
+        if i < TOP - 1:
+            ts(T[L2][:], T[n][:, 15:C:16], T.off[:, 0:1], None, A.subtract, None, [n, "off"], [L2])
+        enlist(2 ** i, max(16, 2 ** i))
+        table(i)
+        if i == 1:
+            ucols()
+        if i == 2:
+            etiles()
+        if i == 3:
+            for c, (lo, hi) in enumerate(CH):
+                quant("xq1", "xs1", lo, hi, T.X0[:, 4 * lo:4 * hi], ["X0"])
+                scores(1, c)
+                ship(1, c)
+            unpack(1)
+        if i == 4:
+            vcopy(T.lnx1[:, 0:W16], T.lnxi[:], ["lnxi"], [("lnx1", 0, W16)])
+            op("v", lambda: V.tensor_copy(T.BPS[:].indirect(T.lnx1[:, 0:W16]), T.IOTA[:]), ["IOTA", ("lnx1", 0, W16)], ["BPS"])
+        if i == 5:
+            far_ring("lnx1", ("lnx1", 0, W16))
+            signs()
+            keep16(T.SELA[:], T.BPS[:], ["BPS"], ["SELA"])
+            ts(T.lnx1[:, W16:2 * W16], T.SELA[:, 15:C:16], T.off[:, 0:1], None, A.subtract, None, ["SELA", "off"], [("lnx1", W16, 2 * W16)])
+    far = ("PTa", "PTb", "PTc")[TOP % 3]
+    leavers("lnx1")
+    ahead(far, 128, 64, 64)
+    enlist(128, 64)
+    guests(0, 128)
+    act(T.SELB[:], T.SELD[:], ["SELD"], ["SELB"], scale=2.0 ** -19)
+    ahead(far, 192, 64, 128)
+    enlist(192, 64)
+    guest_scan(0, 128)
+    keep(0)
+    leaver_bits()
+    ahead(far, 256, 64, 192)
+    enlist(256, 64)
+    evens(0, 192)
+    ahead(far, 320, 32, 256)
+    enlist(320, 32)
+    guests(128, C)
+    op("v", lambda: V.tensor_copy(T.POS[:].indirect(T.ow[:]), T.CEV[:]), ["ow", "CEV"], ["POS"])
+    void_evens()
+    table(7)
+    keep(1)
+    far_places("lnx1")
+    guest_scan(128, C)
+    places()
+    guest_cols()
+    evens(192, C)
+    guest_list()
+    negatives()
+    hosts()
+
+    for k in range(1, ROUNDS + 1):
+        last = k == ROUNDS
+        if k > 1:
+            signs()
+        splice(k)
+        abw, lab, lnx = "abw%d" % k, "lab%d" % k, "lnx%d" % (k + 1)
+        xq, xs = "xq%d" % (k + 1), "xs%d" % (k + 1)
+
+        def own(t, q, lo=0, hi=C):
+            (act if q == "s" else vcopy)(T.TB[:, C * t + lo:C * t + hi],
+                                         T.TH[:, C * t:C * t + C].indirect(T[abw][:, W16 + lo // 16:W16 + hi // 16]),
+                                         [("TH", C * t, C * t + C), abw], [("TB", C * t + lo, C * t + hi)])
+        if not last:
+            scan(T.CNT[:, C:2 * C], T.ONES[:, C:2 * C], T.inv[:, C:2 * C], T.CNT[:, C - 1:C], A.add, A.subtract,
+                 ["ONES", "inve", "invo", "invp", ("CNT", 0, C)], [("CNT", C, 2 * C)])
+            unpack_far(k, 0)
+            act(T.POS[:], T.CNT[:].indirect(T.slw[:]), ["CNT", "slw"], ["POS"], scale=1024.0)
+            own(0, "v")
+            for b in (1, 2, 3):
+                unpack_far(k, b)
+            places()
+            own(1, "s")
+            lay_order()
+            keep16(T.SELO[:], T.OB[:], ["OB"], ["SELO"])
+            evens(0, C)
+            ts(T.ow[:], T.SELO[:, 15:C:16], T.off[:, 0:1], None, A.subtract, None, ["SELO", "off"], ["ow"])
+        else:
+            for b in range(4):
+                unpack_far(k, b)
+            for t in range(4):
+                own(t, "v")
+        for c, (lo, hi) in enumerate(CH):
+            for t in range(4):
+                W = C * t
+                act(T.TBP[:, W + lo:W + hi], T.THP[:, W:W + C].indirect(T[lab][:, W16 + lo // 16:W16 + hi // 16]),
+                    [("THP", W, W + C), lab], [("TBP", W + lo, W + hi)])
+                tt(T.Z[:, 4 * lo + t:4 * hi:4], T.THP[:, W:W + C].indirect(T[lab][:, lo // 16:hi // 16]), T.TBP[:, W + lo:W + hi], A.add,
+                   [("THP", W, W + C), lab, ("TBP", W + lo, W + hi)], [("Z%d" % t, lo, hi)])
+            quant("zq", "zqs", lo, hi, T.Z[:, 4 * lo:4 * hi], [("Z%d" % t, lo, hi) for t in range(4)])
+        if not last:
+            far_ring(lnx, lnx)
+        else:
+            act(T.nrs[:], T.IOTA[:].indirect(T[abw][:, 0:W16]), ["IOTA", abw], ["nrs"])
+            dma("y", "nr", T.nr[:], T.nrs[0:128:16, :], ["nrs"], [])
+        for c, (lo, hi) in enumerate(CH):
+            for b in range(4):
+                P, s = ("PA", b) if c == 0 else ("PB", b) if b < 2 else ("PA", b - 2)
+                mm(P, s, hi - lo, "wq", "wsq", 128 * b, "zq", "zqs", lo, hi)
+                src, key = bank(P, s, hi - lo)
+                if last and c == 1 and b % 2:
+                    ts(T.HH[:, C * b + lo:C * b + hi], src, 2.0 ** -6, None, A.mult, None, [key], [("HH", C * b + lo, C * b + hi)])
+                else:
+                    act(T.HH[:, C * b + lo:C * b + hi], src, [key], [("HH", C * b + lo, C * b + hi)], scale=2.0 ** -6)
+        if not last:
+            guests(0, C)
+            guest_scan(0, C)
+            guest_cols()
+            for lo, hi in CH:
+                for t in (2, 3):
+                    own(t, "s", lo, hi)
+            far_places(lnx)
+            negatives()
+        for c, (lo, hi) in enumerate(CH):
+            for t in range(4):
+                W = C * t
+                tt(T.X1[:, 4 * lo + t:4 * hi:4], T.HH[:, W:W + C].indirect(T[abw][:, lo // 16:hi // 16]), T.TB[:, W + lo:W + hi], A.add,
+                   [("HH", W, W + C), abw, ("TB", W + lo, W + hi)], [("X1_%d" % t, lo, hi)])
+                if not last and c == 0 and t == 0:
+                    guest_list()
+            quant(xq, xs, lo, hi, T.X1[:, 4 * lo:4 * hi], [("X1_%d" % t, lo, hi) for t in range(4)])
+            if not last:
+                scores(k + 1, c)
+                ship(k + 1, c)
+            else:
+                mm("PS", c, hi - lo, "vq", "vqs", 0, xq, xs, lo, hi)
+                dma("y", "oc%d" % c, T.oc[:, 4 * lo:4 * hi], T[xq][:, lo:hi].bitcast(dt.uint8), [(xq, lo, hi)], [])
+                if c == 1:
+                    for i in range(4):
+                        dma("y", "osc%d" % i, T.osc[4 * i:4 * i + 4, :], T[xs][32 * i:32 * i + 4, :], [xs], [])
+                src, key = bank("PS", c, hi - lo)
+                act(T.ysb[:, lo:hi], src, [key], [("ysb", lo, hi)])
+                dma("y", "y%d" % c, T.y[:, lo:hi], T.ysb[:, lo:hi], [("ysb", lo, hi)], [])
+        if not last:
+            unpack(k + 1)
+            hosts()
+    for sem, val in total.items():
+        if know["g"].get(sem, 0) < val:
+            g.wait_ge(T.sem[sem], val)

@@ -2,58 +2,63 @@ from concourse.mybir import dt, AluOpType, ActivationFunctionType
 
 C = 352
 CH = [(0, 224), (224, 352)]
-CH0 = [(0, 192), (192, 352)]
 MASKS = [1, 2, 4]
 ROUNDS = 3
+OWN = {1: True, 2: False, 3: False}
 W16 = C // 16
-K = float(2 ** 20)
-GS = 160
-TOP = 6
+HALF = C // 2
+MOST = C // 2 + 1
+E = 2.0 ** -30
+FB = 368
+RB = 16
+TOP = 7
+SHARE = [192, 192, 192, 160, 0, 0, 0, 0]
+GV = 224
+XT = 2
+HORDER = {True: [(0, 0), (0, 1), (1, 0), (0, 2), (1, 1), (0, 3), (1, 2), (1, 3)],
+          False: [(0, 0), (0, 1), (0, 2), (1, 0), (1, 1), (0, 3), (1, 2), (1, 3)]}
 F8 = "float8_e4m3fn_x4"
 
 SCRATCH = {
-    "nxi": ("sbuf", [128, W16], "int32"), "lnxi": ("sbuf", [128, W16], "int32"),
+    "nxi": ("sbuf", [128, W16], "int32"),
     "ut": ("sbuf", [128, 512], "bfloat16"), "vt": ("sbuf", [128, 512], "bfloat16"),
     "wq": ("sbuf", [128, 512], F8), "wsq": ("sbuf", [128, 512], "uint8"),
     "uq": ("sbuf", [128, 128], F8), "uqs": ("sbuf", [128, 128], "uint8"),
     "up16": ("sbuf", [128, 128], F8), "up16s": ("sbuf", [128, 128], "uint8"),
     "vq": ("sbuf", [128, 128], F8), "vqs": ("sbuf", [128, 128], "uint8"),
     "eq": ("sbuf", [128, 512], F8), "eqs": ("sbuf", [128, 512], "uint8"),
-    "zq": ("sbuf", [128, C], F8), "zqs": ("sbuf", [128, C], "uint8"),
-    "EB": ("sbuf", [128, 516], "bfloat16"), "ONES": ("sbuf", [128, 2 * C], "bfloat16"),
-    "pi": ("sbuf", [128, 1], "int32"), "pj": ("sbuf", [128, 1], "int32"),
-    "FS": ("sbuf", [128, 2 * C + 8], "float32"), "RS": ("sbuf", [128, 2 * C + 8], "float32"),
-    "inv": ("sbuf", [128, 2 * C], "bfloat16"),
-    "cab": ("sbuf", [128, 2 * W16], "float32"), "tab": ("sbuf", [128, 2 * W16], "float32"),
-    "iab": ("sbuf", [128, 2 * W16], "int32"), "jab": ("sbuf", [128, 2 * W16], "int32"),
+    "EB": ("sbuf", [128, 516], "bfloat16"),
+    "pi": ("sbuf", [128, 1], "int32"), "pj": ("sbuf", [128, 1], "int32"), "p16": ("sbuf", [128, 1], "float32"),
+    "FS": ("sbuf", [128, FB + 2 * C + 16], "bfloat16"), "RS": ("sbuf", [128, RB + 2 * C + MOST + 15], "bfloat16"),
+    "J16": ("sbuf", [128, 16], "float32"), "DA": ("sbuf", [128, 16], "float32"), "DB": ("sbuf", [128, 16], "float32"),
+    "D16": ("sbuf", [128, 16], "bfloat16"),
     "PA": ("psum", [128, 2048], "float32"), "PB": ("psum", [128, 1024], "float32"), "PS": ("psum", [128, 1024], "float32"),
 }
 for _n in ("X0", "X1", "TH", "THP", "TB", "TBP", "Z", "HH"):
     SCRATCH[_n] = ("sbuf", [128, 4 * C], "bfloat16")
-for _n in ("RC", "NC", "CNT"):
-    SCRATCH[_n] = ("sbuf", [128, 2 * C], "float32")
-for _n in ("IOTA", "J16", "t1", "CODD", "CEV", "PTa", "PTb", "PTc", "OB", "SELO", "SELA", "SELP", "SEL0", "SEL1", "SEL2",
-           "POS", "BPS", "APS", "VBP", "GA", "GB", "ysb", "nrs"):
-    SCRATCH[_n] = ("sbuf", [128, C], "float32")
-for _n in ("SELD", "SELB", "sc", "upf", "lv", "LS"):
+for _n in ("ONES", "D0", "D1", "CNT"):
+    SCRATCH[_n] = ("sbuf", [128, 2 * C], "bfloat16")
+for _n in ("IOTA", "DG", "PTa", "PTb", "PTc", "OB", "GU", "SELO", "SELA", "SELP", "SELH", "SELL", "SEL0", "SEL1", "SEL2",
+           "POS", "BPS", "APS", "VBP", "GA", "GB", "sc", "up", "lv", "st"):
     SCRATCH[_n] = ("sbuf", [128, C], "bfloat16")
-for _n in ("p16", "p16h", "off", "noff", "thrB", "thr2", "thr3"):
-    SCRATCH[_n] = ("sbuf", [128, 1], "float32")
-for _n in ("C16", "jw", "offi", "offg", "m1", "m2", "m3", "posw", "af", "dpos"):
+for _n in ("ysb", "nrs"):
+    SCRATCH[_n] = ("sbuf", [128, C], "float32")
+for _n in ("C16", "jw", "jm", "j2", "m1", "m2", "m3", "pw", "dq", "dk"):
     SCRATCH[_n] = ("sbuf", [128, W16], "float32")
-for _n in ("l16", "La", "Lb", "slw", "p2u", "ow", "aw"):
+for _n in ("lp", "l16", "L1", "La", "Lb", "slw", "p2u", "ow", "aw", "hq"):
     SCRATCH[_n] = ("sbuf", [128, W16], "uint16")
 for _k in range(1, ROUNDS + 2):
     SCRATCH["xq%d" % _k] = ("sbuf", [128, C], F8)
     SCRATCH["xs%d" % _k] = ("sbuf", [128, C], "uint8")
 for _k in range(1, ROUNDS + 1):
-    SCRATCH["lq%d" % _k] = ("sbuf", [128, C], F8)
-    SCRATCH["ls%d" % _k] = ("sbuf", [128, C], "uint8")
+    for _n in "lz":
+        SCRATCH[_n + "q%d" % _k] = ("sbuf", [128, C], F8)
+        SCRATCH[_n + "s%d" % _k] = ("sbuf", [128, C], "uint8")
     for _n in ("abw", "lab", "lnx"):
         SCRATCH[_n + str(_k)] = ("sbuf", [128, 2 * W16], "uint16")
 
 LOCAL = ["nx", "x", "u", "ws", "wc", "v", "y0", "y1", "nr", "oc0", "oc1", "osc0", "osc1", "osc2", "osc3"]
-REMOTE = ["nx", "nx2", "nx3", "ab1", "ab2", "ab3"] + [n + str(k) + str(c) for k in (1, 2, 3) for n in "qs" for c in (0, 1)]
+REMOTE = ["nx1", "nx2", "nx3", "ab1", "ab2", "ab3"] + [n + str(k) + str(c) for k in (1, 2, 3) for n in "qs" for c in (0, 1)]
 SEMAPHORES = ["cv", "cs", "ct", "cg"] + ["d_" + n for n in LOCAL] + ["r_" + n for n in REMOTE] + ["l_" + n for n in REMOTE]
 
 
@@ -137,11 +142,12 @@ def rank_program(g, core, T, topo):
     for k in (1, 2, 3):
         for c, (lo, hi) in enumerate(CH):
             arrives("q%d%d" % (k, c), partner[k - 1], "lq%d" % k, lo, hi)
-            arrives("s%d%d" % (k, c), partner[k - 1], "ls%d" % k, lo, hi)
-        arrives("ab%d" % k, partner[k - 1], "lab%d" % k)
-    arrives("nx", partner[0], "lnxi")
-    for k in (2, 3):
-        arrives("nx%d" % k, partner[k - 1], "lnx%d" % k)
+            if OWN[k]:
+                arrives("s%d%d" % (k, c), partner[k - 1], "ls%d" % k, lo, hi)
+        if not OWN[k]:
+            arrives("s%d1" % k, partner[k - 1], "ls%d" % k)
+            arrives("ab%d" % k, partner[k - 1], "lab%d" % k)
+        arrives("nx%d" % k, partner[k - 1], "lnx%d" % k, 0, W16 if k == 1 else 2 * W16)
 
     V, S = g.vector, g.scalar
 
@@ -163,15 +169,11 @@ def rank_program(g, core, T, topo):
     def scan(out, d0, d1, init, o0, o1, rd, wr):
         op("v", lambda: V.tensor_tensor_scan(out, d0, d1, init, o0, o1), rd, wr)
 
-    def keep16(out, src, rd, wr):
-        n = out.shape[1]
-        scan(out, T.SELD[:, 0:n], src, 0.0, A.add, A.max, ["SELD"] + rd, wr)
-
-    def act(out, in_, rd, wr, scale=None):
+    def act(out, in_, rd, wr, scale=None, func=AF.Copy):
         if scale is None:
-            op("s", lambda: S.activation(out, in_, AF.Copy), rd, wr)
+            op("s", lambda: S.activation(out, in_, func), rd, wr)
         else:
-            op("s", lambda: S.activation(out, in_, AF.Copy, scale=scale), rd, wr)
+            op("s", lambda: S.activation(out, in_, func, scale=scale), rd, wr)
 
     def sid(out, in_, rd, wr, scale, bias):
         op("s", lambda: S.activation(out, in_, AF.Identity, bias=bias, scale=scale), rd, wr)
@@ -187,327 +189,378 @@ def rank_program(g, core, T, topo):
     def bank(P, s, n):
         return T[P][:, 512 * s:512 * s + n], (P, 512 * s, 512 * s + 512)
 
+    def gather(q, out, win, lst, lo, hi, at=0):
+        (vcopy if q == "v" else act)(T[out][:, lo:hi], T[win][:].indirect(T[lst][:, (at + lo) // 16:(at + hi) // 16]),
+                                     [win, (lst, (at + lo) // 16, (at + hi) // 16)], [(out, lo, hi)])
+
+    def keep16(out, src, lo=0, hi=C):
+        scan(T[out][:, lo:hi], T[src][:, lo:hi], T.DG[:, 0:hi - lo], 0.0, A.add, A.mult, ["DG", (src, lo, hi)], [(out, lo, hi)])
+
+    def kept(sel, lo=0, hi=C):
+        return T[sel][:, lo + 15:hi:16]
+
+    def enlist(lst, sel, lo=0, hi=C, at=0):
+        ts(T[lst][:, (at + lo) // 16:(at + hi) // 16], kept(sel, lo, hi), 1 / E, HALF + 0.25, A.mult, A.add,
+           [(sel, lo, hi)], [(lst, (at + lo) // 16, (at + hi) // 16)])
+
     dma("y", "nx", T.nxi[:], T.nx[:], [], ["nxi"])
-    dma("s", "x", T.X0[:], T.x[:], [], ["X0"])
     dma("y", "u", T.ut[:], T.u[:], [], ["ut"])
-    dma("y", "ws", T.wsq[:], T.ws[:], [], ["wsq"])
-    dma("y", "wc", T.wq[:].bitcast(dt.uint8), T.wc[:], [], ["wq"])
-    dma("y", "v", T.vt[:], T.v[:], [], ["vt"])
+    dma("y", "x", T.X0[:], T.x[:], [], ["X0"])
 
     def iota(name, pattern):
         op("g", lambda: g.iota(T[name][:], pattern, 0, 0, allow_small_or_imprecise_dtypes=True), [], [name])
 
     op("g", lambda: g.iota(T.pi[:], [[0, 1]], 0, 1), [], ["pi"])
-    iota("J16", [[0, W16], [1, 16]])
-    iota("IOTA", [[1, C]])
-    iota("C16", [[16, W16]])
-    send("nx", partner[0], T.lnxi[:], T.nxi[:], "nxi")
-
-    ts(T.pj[:], T.pi[:], 15, None, A.bitwise_and, None, ["pi"], ["pj"])
+    iota("J16", [[1, 16]])
     fill(T.ONES[:], 1.0, ["ONES"])
-    ts(T.p16h[:], T.pj[:], 0.5, None, A.add, None, ["pj"], ["p16h"])
-    ts(T.p16[:], T.pj[:], 0.0, None, A.add, None, ["pj"], ["p16"])
-    ts(T.t1[:], T.J16[:], T.p16h[:, 0:1], 2.0 ** 26, A.subtract, A.mult, ["J16", "p16h"], ["t1"])
-    ts(T.off[:], T.p16[:], -K, 15.0 * K, A.mult, A.add, ["p16"], ["off"])
-    ts(T.SELD[:], T.t1[:], K, None, A.min, None, ["t1"], ["SELD"])
-    vcopy(T.La[:], T.nxi[:], ["nxi"], ["La"])
-    fill(T.ow[:], 0, ["ow"])
-    fill(T.OB[:, 0:1], 0.0, [("OB", 0, 1)])
     op("g", lambda: g.affine_select(T.EB[:], T.ONES[:, 0:516], [[1, 516]], A.is_equal, 0.0, -4, -4), ["ONES"], ["EB"])
+    iota("C16", [[16, W16]])
+    ts(T.pj[:], T.pi[:], 15, None, A.bitwise_and, None, ["pi"], ["pj"])
+    scan(T.IOTA[:], T.ONES[:, 0:C], T.ONES[:, 0:C], -HALF - 1.0, A.mult, A.add, ["ONES"], ["IOTA"])
+    vcopy(T.p16[:], T.pj[:], ["pj"], ["p16"])
+    fill(T.ow[:], 0, ["ow"])
+    ts(T.DA[:], T.J16[:], T.p16[:, 0:1], None, A.is_gt, None, ["J16", "p16"], ["DA"])
+    ts(T.DB[:], T.J16[:], T.p16[:, 0:1], 1 / E, A.is_equal, A.mult, ["J16", "p16"], ["DB"])
+    ts(T.lp[:], T.ONES[:, 0:W16], T.p16[:, 0:1], None, A.mult, None, ["ONES", "p16"], ["lp"])
+    tt(T.D16[:], T.DA[:], T.DB[:], A.add, ["DA", "DB"], ["D16"])
+    fill(T.OB[:, 0:1], -float(HALF), [("OB", 0, 1)])
+    ts(T.D16[:, 15:16], T.D16[:, 15:16], E * E, None, A.mult, None, ["D16"], ["D16"])
+    gather("s", "DG", "D16", "lp", 0, C)
+    for b in range(4):
+        quant("eq", "eqs", 128 * b, 128 * b + 128, T.EB[:, 4 - b:516 - b], ["EB"])
+    vcopy(T.L1[:], T.nxi[:], ["nxi"], ["L1"])
+    send("nx1", partner[0], T.lnx1[:, 0:W16], T.L1[:], "L1")
+    dma("y", "ws", T.wsq[:], T.ws[:], [("lnx1", 0, W16)], ["wsq"])
+    dma("y", "wc", T.wq[:].bitcast(dt.uint8), T.wc[:], [], ["wq"])
+    dma("y", "v", T.vt[:], T.v[:], [], ["vt"])
 
-    def table(i):
-        if i == 1:
-            sid(T.jw[:], T.C16[:], ["C16", "p16"], ["jw"], 1.0, T.p16[:, 0:1])
-            sid(T.offi[:], T.jw[:], ["jw", "off"], ["offi"], 1024.0, T.off[:, 0:1])
-        if i == 2:
-            sid(T.CODD[:], T.IOTA[:], ["IOTA"], ["CODD"], 1024.0, 512.0)
-        if i == 3:
-            act(T.CEV[:], T.IOTA[:], ["IOTA"], ["CEV"], scale=1024.0)
-        if i == 4:
-            sid(T.offg[:], T.offi[:], ["offi"], ["offg"], 1.0, 512.0)
-            sid(T.noff[:], T.off[:], ["off"], ["noff"], -1.0, 0.0)
-        if i == 7:
-            sid(T.thrB[:], T.off[:], ["off"], ["thrB"], 2.0 ** -19, 0.5)
-            sid(T.thr2[:], T.off[:], ["off"], ["thr2"], 1.0, 400000.0)
-            sid(T.thr3[:], T.off[:], ["off"], ["thr3"], 1.0, -600000.0)
-            sid(T.FS[:, 0:1], T.p16[:], ["p16"], [("FS", 0, 1)], 0.0, -float(2 ** 20))
-            sid(T.RS[:, 2 * C + 7:2 * C + 8], T.p16[:], ["p16"], [("RS", 2 * C + 7, 2 * C + 8)], 0.0, float(2 ** 19))
+    def columns():
+        vcopy(T.l16[:], T.C16[:], ["C16"], ["l16"])
+        sid(T.jw[:], T.C16[:], ["C16", "p16"], ["jw"], 1.0, T.p16[:, 0:1])
+        sid(T.jm[:], T.jw[:], ["jw"], ["jm"], E, -HALF * E)
+        sid(T.j2[:], T.jw[:], ["jw"], ["j2"], E * E, 0.25 * E * E)
 
     def ucols():
-        vcopy(T.l16[:], T.C16[:], ["C16"], ["l16"])
         quant("uq", "uqs", 0, 128, T.ut[:], ["ut"])
-        vcopy(T.up16[:, 0:128].bitcast(dt.uint32), T.uq[:, 0:128].bitcast(dt.uint32).indirect(T.l16[:, 0:8]), ["uq", "l16"], ["up16"])
         act(T.up16s[:, 0:128], T.uqs[:, 0:128].indirect(T.l16[:, 0:8]), ["uqs", "l16"], ["up16s"])
+        vcopy(T.up16[:, 0:128].bitcast(dt.uint32), T.uq[:, 0:128].bitcast(dt.uint32).indirect(T.l16[:, 0:8]), ["uq", "l16"], ["up16"])
 
-    def etiles():
-        for b in range(4):
-            quant("eq", "eqs", 128 * b, 128 * b + 128, T.EB[:, 4 - b:516 - b], ["EB"])
-
-    def scores(k, c):
-        lo, hi = CH[c]
+    def scores(k, c, lo, hi):
         mm("PS", c, hi - lo, "up16", "up16s", 0, "xq%d" % k, "xs%d" % k, lo, hi)
 
-    def ship(k, c):
+    def ship(k, c, n):
         p, (lo, hi) = partner[k - 1], CH[c]
-        send("q%d%d" % (k, c), p, T["lq%d" % k][:, lo:hi].bitcast(dt.uint8), T["xq%d" % k][:, lo:hi].bitcast(dt.uint8), ("xq%d" % k, lo, hi))
-        send("s%d%d" % (k, c), p, T["ls%d" % k][:, lo:hi], T["xs%d" % k][:, lo:hi], ("xs%d" % k, lo, hi))
+        send("q%d%d" % (k, c), p, T["lq%d" % k][:, lo:hi].bitcast(dt.uint8), T[n % "q"][:, lo:hi].bitcast(dt.uint8), (n % "q", lo, hi))
+        if not OWN[k]:
+            if c == 0:
+                return
+            lo = 0
+        send("s%d%d" % (k, c), p, T["ls%d" % k][:, lo:hi], T[n % "s"][:, lo:hi], (n % "s", lo, hi))
 
-    def signs():
-        for c, (lo, hi) in enumerate(CH):
-            src, key = bank("PS", c, hi - lo)
-            op("s", lambda: S.activation(T.sc[:, lo:hi], src, AF.Sign), [key], [("sc", lo, hi)])
-            ts(T.upf[:, lo:hi], T.sc[:, lo:hi], 0.0, None, A.max, None, [("sc", lo, hi)], [("upf", lo, hi)])
+    def signs(q, c, lo, hi):
+        src, key = bank("PS", c, hi - lo)
+        if q == "v":
+            ts(T.up[:, lo:hi], src, 0.0, None, A.is_gt, None, [key], [("up", lo, hi)])
+            if hi - lo < C:
+                ts(T.sc[:, lo:hi], src, 0.0, None, A.is_gt, None, [key], [("sc", lo, hi)])
+            else:
+                vcopy(T.sc[:], T.up[:], ["up"], ["sc"])
+        else:
+            act(T.sc[:, lo:hi], src, [key], [("sc", lo, hi)], func=AF.Sign)
+            act(T.up[:, lo:hi], T.sc[:, lo:hi], [("sc", lo, hi)], [("up", lo, hi)], func=AF.Relu)
 
-    def unpack(k):
-        for b in range(4):
-            mm("PA", b, C, "eq", "eqs", 128 * b, "xq%d" % k, "xs%d" % k, 0, C)
+    def place(c, b):
+        return ("PA", b) if c == 0 else ("PB", b) if b < 2 else ("PA", b - 2)
 
-    def keep(b):
-        src, key = bank("PA", b, C)
-        act(T.TH[:, C * b:C * b + C], src, [key], [("TH", C * b, C * b + C)], scale=0.5)
+    def unpack(k, c, lo, hi, bs=range(4)):
+        for b in bs:
+            mm(*place(c, b), hi - lo, "eq", "eqs", 128 * b, "xq%d" % k, "xs%d" % k, lo, hi)
 
-    def unpack_far(k, b):
-        src, key = bank("PB", b % 2, C)
-        mm("PB", b % 2, C, "eq", "eqs", 128 * b, "lq%d" % k, "ls%d" % k, 0, C)
-        act(T.THP[:, C * b:C * b + C], src, [key], [("THP", C * b, C * b + C)], scale=0.5)
+    def halve(q, out, src, key, okey, scale):
+        if q == "s":
+            act(out, src, [key], [okey], scale=scale)
+        else:
+            ts(out, src, scale, None, A.mult, None, [key], [okey])
 
-    def places():
-        keep16(T.SELP[:], T.POS[:], ["POS"], ["SELP"])
-        sid(T.posw[:], T.SELP[:, 15:C:16], ["SELP", "noff"], ["posw"], 1.0, T.noff[:, 0:1])
+    def keep(b, q="s", c=0, lo=0, hi=C):
+        src, key = bank(*place(c, b), hi - lo)
+        halve(q, T.TH[:, C * b + lo:C * b + hi], src, key, ("TH", C * b + lo, C * b + hi), 0.5)
 
-    def lay_order():
-        ts(T.p2u[:], T.SELP[:, 15:C:16], T.off[:, 0:1], 2.0 ** -10, A.subtract, A.mult, ["SELP", "off"], ["p2u"])
-        op("v", lambda: V.tensor_copy(T.OB[:].indirect(T.p2u[:]), T.IOTA[:]), ["IOTA", "p2u"], ["OB"])
-
-    def far_ring(lst, key):
-        act(T.APS[:], T.IOTA[:].indirect(T[lst][:, 0:W16]), ["IOTA", key], ["APS"])
-
-    def far_places(lst):
-        sid(T.VBP[:], T.POS[:].indirect(T[lst][:, W16:2 * W16]), ["POS", lst], ["VBP"], 1.0, 512.0)
-
-    def guests(lo, hi):
-        tt(T.RC[:, 1 + 2 * lo:2 * hi:2], T.APS[:].indirect(T.ow[:, lo // 16:hi // 16]), T.CODD[:, lo:hi], A.add,
-           ["APS", ("ow", lo, hi), "CODD"], [("RCO", lo, hi)])
-
-    def evens(lo, hi):
-        tt(T.RC[:, 2 * lo:2 * hi:2], T.OB[:, lo:hi], T.CEV[:, lo:hi], A.add, [("OB", lo, hi), "CEV"], [("RCE", lo, hi)])
-
-    def guest_scan(lo, hi):
-        keep16(T.SELA[:, lo:hi], T.RC[:, 1 + 2 * lo:2 * hi:2], [("RCO", lo, hi)], [("SELA", lo, hi)])
-
-    def guest_cols():
-        tt(T.af[:], T.SELA[:, 15:C:16], T.offg[:], A.subtract, ["SELA", "offg"], ["af"])
-
-    def guest_list():
-        vcopy(T.aw[:], T.af[:], ["af"], ["aw"])
-
-    def hosts():
-        keep16(T.SEL0[:], T.VBP[:], ["VBP"], ["SEL0"])
-        tt(T.dpos[:], T.SEL0[:, 15:C:16], T.SELP[:, 15:C:16], A.subtract, ["SEL0", "SELP"], ["dpos"])
-
-    def negatives():
-        sid(T.NC[:], T.RC[:], ["RCE", "RCO"], ["NC"], 1.0, -float(2 ** 19))
+    def unpack_far(k, b, q="s"):
+        src, key = bank("PA", 2 + b % 2, C)
+        mm("PA", 2 + b % 2, C, "eq", "eqs", 128 * b, "lq%d" % k, "ls%d" % k, 0, C)
+        halve(q, T.THP[:, C * b:C * b + C], src, key, ("THP", C * b, C * b + C), 0.5)
 
     def leavers(lst):
-        tt(T.lv[:], T.upf[:].indirect(T[lst][:, W16:2 * W16]), T.sc[:], A.is_lt, ["upf", "sc", lst], ["lv"])
+        tt(T.lv[:], T.up[:].indirect(T[lst][:, W16:2 * W16]), T.sc[:], A.is_lt, ["up", "sc", lst], ["lv"])
 
-    def void_evens():
-        act(T.inv[:, 0:2 * C:2], T.lv[:].indirect(T.ow[:]), ["lv", "ow"], ["inve"])
-
-    def leaver_bits():
-        scan(T.LS[:], T.SELB[:], T.lv[:], 0.0, A.add, A.max, ["SELB", "lv"], ["LS"])
-
-    def splice(k):
-        lst, abw = "lnx%d" % k, "abw%d" % k
-        h = W16
-        if k > 1:
-            leavers(lst)
-            keep(0)
-            keep(1)
-            void_evens()
-        sid(T.inv[:, 1 + 2 * GS:2 * C:2], T.lv[:].indirect(T.aw[:, GS // 16:h]), ["lv", "aw"], ["invp"], -1.0, 1.0)
-        if k > 1:
-            leaver_bits()
-        ts(T.inv[:, 1:2 * GS:2], T.lv[:].indirect(T.aw[:, 0:GS // 16]), -1.0, 1.0, A.mult, A.add, ["lv", "aw"], ["invo"])
-        ts(T.m1[:], T.LS[:, 15:C:16], T.thrB[:, 0:1], None, A.is_ge, None, ["LS", "thrB"], ["m1"])
-        tt(T.m2[:], T.m1[:], T.dpos[:], A.mult, ["m1", "dpos"], ["m2"])
-        tt(T.m3[:], T.m2[:], T.posw[:], A.add, ["m2", "posw"], ["m3"])
-        ts(T.slw[:], T.m3[:], 2.0 ** -9, None, A.mult, None, ["m3"], ["slw"])
-        keep(2)
-        keep(3)
-        void = ["inve", "invo", "invp"]
-        scan(T.FS[:, 1:2 * C + 1], T.inv[:], T.NC[:], -float(2 ** 20), A.mult, A.min, void + ["NC"], [("FS", 1, 2 * C + 8)])
-        act(T.GB[:], T.FS[:, 0:2 * C].indirect(T.slw[:]), ["FS", "slw"], ["GB"])
-        scan(T.RS[:, 2 * C + 6:6:-1], T.inv[:, ::-1], T.RC[:, ::-1], float(2 ** 19), A.mult, A.max,
-             void + ["RCE", "RCO"], [("RS", 0, 2 * C + 7)])
-        act(T.GA[:], T.RS[:, 8:2 * C + 8].indirect(T.slw[:]), ["RS", "slw"], ["GA"])
-        keep16(T.SEL1[:], T.GB[:], ["GB"], ["SEL1"])
-        sid(T.cab[:, h:2 * h], T.SEL1[:, 15:C:16], ["SEL1", "noff"], [("cab", h, 2 * h)], 1.0, T.noff[:, 0:1])
-        if k < ROUNDS:
-            scan(T.CNT[:, 0:C], T.ONES[:, 0:C], T.inv[:, 0:C], -1.0, A.add, A.subtract, ["ONES"] + void, [("CNT", 0, C)])
+    def stayers(q):
+        if q == "s":
+            sid(T.st[:], T.lv[:], ["lv"], ["st"], -1.0, 1.0)
         else:
-            quant("vq", "vqs", 0, 128, T.vt[:], ["vt"])
-        keep16(T.SEL2[:], T.GA[:], ["GA"], ["SEL2"])
-        sid(T.cab[:, 0:h], T.SEL2[:, 15:C:16], ["SEL2", "noff"], [("cab", 0, h)], 1.0, T.noff[:, 0:1])
-        ts(T.tab[:, h:2 * h], T.SEL1[:, 15:C:16], T.thr3[:, 0:1], T.FS[:, 2 * C:2 * C + 1], A.is_le, A.mult, ["SEL1", "thr3", "FS"], [("tab", h, 2 * h)])
-        ts(T.tab[:, 0:h], T.SEL2[:, 15:C:16], T.thr2[:, 0:1], T.RS[:, 7:8], A.is_ge, A.mult, ["SEL2", "thr2", "RS"], [("tab", 0, h)])
-        tt(T.iab[:], T.cab[:], T.tab[:], A.add, ["cab", "tab"], ["iab"])
-        ts(T.jab[:], T.iab[:], 511, None, A.bitwise_and, None, ["iab"], ["jab"])
-        vcopy(T[abw][:], T.jab[:], ["jab"], [abw])
-        send("ab%d" % k, partner[k - 1], T["lab%d" % k][:], T[abw][:], abw)
+            ts(T.st[:], T.lv[:], -1.0, 1.0, A.mult, A.add, ["lv"], ["st"])
+
+    def void(odd, lo=0, hi=C):
+        w, l = ("st", "aw") if odd else ("lv", "ow")
+        act(T.D0[:, 2 * lo + odd:2 * hi:2], T[w][:].indirect(T[l][:, lo // 16:hi // 16]), [w, (l, lo // 16, hi // 16)], [("D0%d" % odd, lo, hi)])
+
+    def real(odd, lo=0, hi=C):
+        w, l, t = ("lv", "aw", "GU") if odd else ("st", "ow", "OB")
+        tt(T.D1[:, 2 * lo + odd:2 * hi:2], T[w][:].indirect(T[l][:, lo // 16:hi // 16]), T[t][:, lo:hi], A.mult,
+           [w, (l, lo // 16, hi // 16), (t, lo, hi)], [("D1%d" % odd, lo, hi)])
+
+    def slots(odds, lo=0, hi=C):
+        return [("D%d%d" % (d, o), lo, hi) for d in (0, 1) for o in odds]
+
+    def first_real():
+        r = RB + 2 * C - 1
+        scan(T.RS[:, r + MOST - 1:r - 1:-1], T.D0[:, 2 * MOST - 2::-2], T.D1[:, 2 * MOST - 2::-2], 0.0, A.mult, A.add,
+             slots([0], 0, MOST), [("RS", r, r + MOST)])
+
+    def last_real():
+        a = 2 * (C - MOST)
+        scan(T.FS[:, FB + 1 - 2 * MOST:FB + 1], T.D0[:, a:2 * C], T.D1[:, a:2 * C], 0.0, A.mult, A.add,
+             slots([0, 1], C - MOST, C), [("FS", 0, FB + 1)])
+
+    def before():
+        scan(T.FS[:, FB + 1:FB + 1 + 2 * C], T.D0[:], T.D1[:], T.FS[:, FB:FB + 1], A.mult, A.add,
+             slots([0, 1]) + [("FS", FB, FB + 1)], [("FS", FB + 1, FB + 1 + 2 * C)])
+
+    def behind():
+        r = RB + 2 * C - 1
+        scan(T.RS[:, r - 1:RB - 2:-1], T.D0[:, ::-1], T.D1[:, ::-1], T.RS[:, r:r + 1], A.mult, A.add,
+             slots([0, 1]) + [("RS", r, r + 1)], [("RS", 0, r)])
+
+    def neighbours(q, out, lo, hi):
+        win, a = ("RS", RB) if out == "GA" else ("FS", FB)
+        (vcopy if q == "v" else act)(T[out][:, lo:hi], T[win][:, a:a + 2 * C].indirect(T.slw[:, lo // 16:hi // 16]),
+                                     [(win, a, a + 2 * C), "slw"], [(out, lo, hi)])
+
+    def lists(k):
+        abw = "abw%d" % k
+        before()
+        neighbours("s", "GB", 0, C)
+        behind()
+        neighbours("v", "GA", 0, GV)
+        neighbours("s", "GA", GV, C)
+        keep16("SEL1", "GB")
+        enlist(abw, "SEL1", 0, C, C)
+        keep16("SEL2", "GA")
+        enlist(abw, "SEL2")
+        if not OWN[k]:
+            send("ab%d" % k, partner[k - 1], T["lab%d" % k][:], T[abw][:], abw)
         if k < ROUNDS:
             send("nx%d" % (k + 1), partner[k], T["lnx%d" % (k + 1)][:], T[abw][:], abw)
 
+    def splice(k):
+        leavers("lnx%d" % k)
+        keep(0)
+        stayers("s")
+        real(1)
+        void(0)
+        keep16("SELL", "lv")
+        real(0)
+        void(1)
+        tt(T.m2[:], kept("SELL"), T.dk[:], A.mult, ["SELL", "dk"], ["m2"])
+        first_real()
+        tt(T.m3[:], T.m2[:], T.pw[:], A.add, ["m2", "pw"], ["m3"])
+        keep(1)
+        last_real()
+        ts(T.slw[:], T.m3[:], 1 / E / E, None, A.mult, None, ["m3"], ["slw"])
+        keep(2)
+        lists(k)
+        keep(3)
+
+    def count():
+        scan(T.CNT[:], T.ONES[:], T.D0[:], -HALF - 1.0, A.add, A.subtract, ["ONES", "D00", "D01"], ["CNT"])
+
+    def places():
+        gather("s", "POS", "CNT", "slw", 0, C)
+
+    def lay(lst, lo=0, hi=C):
+        out, key = {"p2u": ("OB", "OB"), "ow": ("POS", "POS"), "lnx1": ("BPS", "BPS")}[lst]
+        op("v", lambda: V.tensor_copy(T[out][:].indirect(T[lst][:, lo // 16:hi // 16]), T.IOTA[:, lo:hi]),
+           ["IOTA", (lst, lo // 16, hi // 16)], [key])
+
+    def own_slots():
+        sid(T.pw[:], kept("SELP"), ["SELP"], ["pw"], 2 * E, (C + 0.25) * E * E)
+
+    def host_slots():
+        keep16("SELH", "VBP")
+        tt(T.dq[:], kept("SELH"), kept("SELP"), A.subtract, ["SELH", "SELP"], ["dq"])
+        sid(T.dk[:], T.dq[:], ["dq"], ["dk"], 2.0, E)
+
     def jump(out, win, lst, share):
-        for lo, hi in CH0[::-1] if share else CH0:
-            (vcopy if share and lo == 0 else act)(T[out][:, lo:hi], T[win][:].indirect(T[lst][:, lo // 16:hi // 16]), [win, lst], [(out, lo, hi)])
+        cut = share or 192
+        gather("v" if share else "s", out, win, lst, 0, cut)
+        gather("s", out, win, lst, cut, C)
+        return cut
 
     def ahead(P, m, n, a):
-        b = 0 if m < 16 else m
-        act(T.OB[:, m:m + n], T[P][:].indirect(T.ow[:, a // 16:(a + n) // 16]), [P, ("ow", a, a + n)], [("OB", m, m + n)])
-        keep16(T.SELO[:, b:b + n], T.OB[:, b:b + n], [("OB", b, b + n)], [("SELO", b, b + n)])
+        act(T.OB[:, m:m + n], T[P][:].indirect(T.ow[:, a // 16:(a + n) // 16]), [P, ("ow", a // 16, (a + n) // 16)], [("OB", m, m + n)])
 
-    def enlist(m, n):
+    def order_list(m, n):
         b = 0 if m < 16 else m
-        ts(T.ow[:, b // 16:(b + n) // 16], T.SELO[:, b + 15:b + n:16], T.off[:, 0:1], None, A.subtract, None,
-           [("SELO", b, b + n), "off"], [("ow", b, b + n)])
+        keep16("SELO", "OB", b, b + n)
+        enlist("ow", "SELO", b, b + n)
 
-    jump("PTa", "IOTA", "La", True)
-    for i in range(TOP + 1):
-        L, L2 = ("La", "Lb") if i % 2 == 0 else ("Lb", "La")
+    def guests(lo, hi):
+        gather("s", "GU", "APS", "ow", lo, hi)
+
+    def guest_list(lo, hi):
+        keep16("SELA", "GU", lo, hi)
+        enlist("aw", "SELA", lo, hi)
+
+    extra = {
+        0: [columns],
+        1: [ucols],
+        2: [lambda: quant("xq1", "xs1", 0, C, T.X0[:], ["X0"]), lambda: scores(1, 0, 0, C), lambda: unpack(1, 0, 0, C)]
+           + ([] if OWN[1] else [lambda: ship(1, 0, "x%s1"), lambda: ship(1, 1, "x%s1")]),
+        3: [lambda: signs("v", 0, 0, C), lambda: lay("lnx1", 0, 128)],
+        4: [lambda: lay("lnx1", 128, 256), lambda: lay("lnx1", 256, C)],
+        5: [lambda: keep16("SELH", "BPS"), lambda: enlist("lnx1", "SELH", 0, C, C), lambda: leavers("lnx1")],
+        6: [lambda: stayers("v"), lambda: keep16("SELL", "lv")],
+    }
+    jump("PTa", "IOTA", "L1", SHARE[0])
+    for i in range(TOP):
+        L, L2 = "L1" if i == 0 else ("La", "Lb")[i % 2], ("La", "Lb")[1 - i % 2]
         P, P2 = (("PTa", "PTb"), ("PTb", "PTc"), ("PTc", "PTa"))[i % 3]
         n = "SEL%d" % (i % 3)
-        if i < TOP:
-            jump(P2, P, L, i < 3)
-        if i < TOP - 1:
-            for lo, hi in CH0:
-                keep16(T[n][:, lo:hi], T[P2][:, lo:hi], [(P2, lo, hi)], [(n, lo, hi)])
+        cut = jump(P2, P, L, SHARE[i + 1])
         ahead(P, 2 ** i, max(16, 2 ** i), 0)
         if i < TOP - 1:
-            ts(T[L2][:], T[n][:, 15:C:16], T.off[:, 0:1], None, A.subtract, None, [n, "off"], [L2])
-        enlist(2 ** i, max(16, 2 ** i))
-        table(i)
-        if i == 1:
-            ucols()
-        if i == 2:
-            etiles()
-        if i == 3:
-            for c, (lo, hi) in enumerate(CH):
-                quant("xq1", "xs1", lo, hi, T.X0[:, 4 * lo:4 * hi], ["X0"])
-                scores(1, c)
-                ship(1, c)
-            unpack(1)
+            keep16(n, P2, 0, cut)
+            keep16(n, P2, cut, C)
+            enlist(L2, n)
+        order_list(2 ** i, max(16, 2 ** i))
         if i == 4:
-            vcopy(T.lnx1[:, 0:W16], T.lnxi[:], ["lnxi"], [("lnx1", 0, W16)])
-            op("v", lambda: V.tensor_copy(T.BPS[:].indirect(T.lnx1[:, 0:W16]), T.IOTA[:]), ["IOTA", ("lnx1", 0, W16)], ["BPS"])
-        if i == 5:
-            far_ring("lnx1", ("lnx1", 0, W16))
-            signs()
-            keep16(T.SELA[:], T.BPS[:], ["BPS"], ["SELA"])
-            ts(T.lnx1[:, W16:2 * W16], T.SELA[:, 15:C:16], T.off[:, 0:1], None, A.subtract, None, ["SELA", "off"], [("lnx1", W16, 2 * W16)])
+            gather("s", "APS", "IOTA", "lnx1", 0, C)
+        for f in extra.get(i, []):
+            f()
     far = ("PTa", "PTb", "PTc")[TOP % 3]
-    leavers("lnx1")
-    ahead(far, 128, 64, 64)
-    enlist(128, 64)
+    ahead(far, 128, 128, 0)
     guests(0, 128)
-    act(T.SELB[:], T.SELD[:], ["SELD"], ["SELB"], scale=2.0 ** -19)
-    ahead(far, 192, 64, 128)
-    enlist(192, 64)
-    guest_scan(0, 128)
+    tt(T.dq[:], kept("SELH"), T.jm[:], A.subtract, ["SELH", "jm"], ["dq"])
+    order_list(128, 128)
+    ahead(far, 256, 96, 128)
+    tt(T.m2[:], kept("SELL"), T.dq[:], A.mult, ["SELL", "dq"], ["m2"])
+    guest_list(0, 128)
+    guests(128, 256)
+    tt(T.m3[:], T.m2[:], T.j2[:], A.add, ["m2", "j2"], ["m3"])
+    order_list(256, 96)
+    guests(256, C)
+    ts(T.hq[:], T.m3[:], 1 / E / E, None, A.mult, None, ["m3"], ["hq"])
+    lay("ow")
+    void(0)
+    guest_list(128, C)
+    gather("s", "VBP", "POS", "hq", 0, C)
+    sid(T.m1[:], kept("SELL"), ["SELL"], ["m1"], 0.5, (HALF + 0.125) * E)
+    real(0)
+    void(1)
+    keep16("SELP", "VBP")
+    real(1)
+    tt(T.m3[:], kept("SELP"), T.m1[:], A.add, ["SELP", "m1"], ["m3"])
     keep(0)
-    leaver_bits()
-    ahead(far, 256, 64, 192)
-    enlist(256, 64)
-    evens(0, 192)
-    ahead(far, 320, 32, 256)
-    enlist(320, 32)
-    guests(128, C)
-    op("v", lambda: V.tensor_copy(T.POS[:].indirect(T.ow[:]), T.CEV[:]), ["ow", "CEV"], ["POS"])
-    void_evens()
-    table(7)
+    first_real()
+    ts(T.slw[:], T.m3[:], 2 / E, None, A.mult, None, ["m3"], ["slw"])
+    last_real()
     keep(1)
-    far_places("lnx1")
-    guest_scan(128, C)
-    places()
-    guest_cols()
-    evens(192, C)
-    guest_list()
-    negatives()
-    hosts()
+    lists(1)
+    keep(2)
+    keep(3, "v")
 
     for k in range(1, ROUNDS + 1):
         last = k == ROUNDS
         if k > 1:
-            signs()
-        splice(k)
+            splice(k)
         abw, lab, lnx = "abw%d" % k, "lab%d" % k, "lnx%d" % (k + 1)
         xq, xs = "xq%d" % (k + 1), "xs%d" % (k + 1)
+        zq, zs = "zq%d" % k, "zs%d" % k
 
-        def own(t, q, lo=0, hi=C):
-            (act if q == "s" else vcopy)(T.TB[:, C * t + lo:C * t + hi],
-                                         T.TH[:, C * t:C * t + C].indirect(T[abw][:, W16 + lo // 16:W16 + hi // 16]),
-                                         [("TH", C * t, C * t + C), abw], [("TB", C * t + lo, C * t + hi)])
+        def back(q, out, win, lst, t, lo=0, hi=C):
+            W = C * t
+            (act if q == "s" else vcopy)(T[out][:, W + lo:W + hi], T[win][:, W:W + C].indirect(T[lst][:, W16 + lo // 16:W16 + hi // 16]),
+                                         [(win, W, W + C), (lst, W16, 2 * W16)], [(out, W + lo, W + hi)])
+
+        def mean(out, win, lst, add, t, lo, hi):
+            W = C * t
+            tt(T[out][:, 4 * lo + t:4 * hi:4], T[win][:, W:W + C].indirect(T[lst][:, lo // 16:hi // 16]), T[add][:, W + lo:W + hi], A.add,
+               [(win, W, W + C), (lst, 0, W16), (add, W + lo, W + hi)], [(out + "_%d" % t, lo, hi)])
+
+        def new_order():
+            keep16("SELP", "POS")
+            enlist("p2u", "SELP")
+            own_slots()
+            lay("p2u")
+            keep16("SELO", "OB")
+            enlist("ow", "SELO")
+
         if not last:
-            scan(T.CNT[:, C:2 * C], T.ONES[:, C:2 * C], T.inv[:, C:2 * C], T.CNT[:, C - 1:C], A.add, A.subtract,
-                 ["ONES", "inve", "invo", "invp", ("CNT", 0, C)], [("CNT", C, 2 * C)])
-            unpack_far(k, 0)
-            act(T.POS[:], T.CNT[:].indirect(T.slw[:]), ["CNT", "slw"], ["POS"], scale=1024.0)
-            own(0, "v")
-            for b in (1, 2, 3):
-                unpack_far(k, b)
-            places()
-            own(1, "s")
-            lay_order()
-            keep16(T.SELO[:], T.OB[:], ["OB"], ["SELO"])
-            evens(0, C)
-            ts(T.ow[:], T.SELO[:, 15:C:16], T.off[:, 0:1], None, A.subtract, None, ["SELO", "off"], ["ow"])
-        else:
+            count()
+        if not OWN[k]:
+            if not last:
+                places()
+            back("v", "TB", "TH", abw, 0)
             for b in range(4):
                 unpack_far(k, b)
-            for t in range(4):
-                own(t, "v")
+            if not last:
+                back("s", "TB", "TH", abw, 1)
+                new_order()
+            else:
+                for t in (1, 2, 3):
+                    back("v", "TB", "TH", abw, t)
+                quant("vq", "vqs", 0, 128, T.vt[:], ["vt"])
+        win, lst, tb = ("TH", abw, "TB") if OWN[k] else ("THP", lab, "TBP")
         for c, (lo, hi) in enumerate(CH):
             for t in range(4):
-                W = C * t
-                act(T.TBP[:, W + lo:W + hi], T.THP[:, W:W + C].indirect(T[lab][:, W16 + lo // 16:W16 + hi // 16]),
-                    [("THP", W, W + C), lab], [("TBP", W + lo, W + hi)])
-                tt(T.Z[:, 4 * lo + t:4 * hi:4], T.THP[:, W:W + C].indirect(T[lab][:, lo // 16:hi // 16]), T.TBP[:, W + lo:W + hi], A.add,
-                   [("THP", W, W + C), lab, ("TBP", W + lo, W + hi)], [("Z%d" % t, lo, hi)])
-            quant("zq", "zqs", lo, hi, T.Z[:, 4 * lo:4 * hi], [("Z%d" % t, lo, hi) for t in range(4)])
-        if not last:
-            far_ring(lnx, lnx)
-        else:
-            act(T.nrs[:], T.IOTA[:].indirect(T[abw][:, 0:W16]), ["IOTA", abw], ["nrs"])
+                back("s", tb, win, lst, t, lo, hi)
+                mean("Z", win, lst, tb, t, lo, hi)
+            quant(zq, zs, lo, hi, T.Z[:, 4 * lo:4 * hi], [("Z_%d" % t, lo, hi) for t in range(4)])
+            if OWN[k]:
+                ship(k, c, "z%s" + str(k))
+        if last:
+            sid(T.nrs[:], T.GA[:], ["GA"], ["nrs"], 1.0, float(HALF))
             dma("y", "nr", T.nr[:], T.nrs[0:128:16, :], ["nrs"], [])
-        for c, (lo, hi) in enumerate(CH):
-            for b in range(4):
-                P, s = ("PA", b) if c == 0 else ("PB", b) if b < 2 else ("PA", b - 2)
-                mm(P, s, hi - lo, "wq", "wsq", 128 * b, "zq", "zqs", lo, hi)
-                src, key = bank(P, s, hi - lo)
-                if last and c == 1 and b % 2:
-                    ts(T.HH[:, C * b + lo:C * b + hi], src, 2.0 ** -6, None, A.mult, None, [key], [("HH", C * b + lo, C * b + hi)])
-                else:
-                    act(T.HH[:, C * b + lo:C * b + hi], src, [key], [("HH", C * b + lo, C * b + hi)], scale=2.0 ** -6)
-        if not last:
+            if OWN[k]:
+                quant("vq", "vqs", 0, 128, T.vt[:], ["vt"])
+        elif OWN[k]:
+            places()
+            gather("s", "APS", "IOTA", lnx, 0, C)
+            new_order()
+            gather("s", "VBP", "POS", lnx, 0, C, C)
+            host_slots()
+        hq, hs = ("lq%d" % k, "ls%d" % k) if OWN[k] else (zq, zs)
+        for c, b in HORDER[OWN[k]]:
+            lo, hi = CH[c]
+            P, s = place(c, b)
+            mm(P, s, hi - lo, "wq", "wsq", 128 * b, hq, hs, lo, hi)
+            src, key = bank(P, s, hi - lo)
+            halve("s", T.HH[:, C * b + lo:C * b + hi], src, key, ("HH", C * b + lo, C * b + hi), 2.0 ** -6)
+        if not last and not OWN[k]:
+            for t in (2, 3):
+                back("s", "TB", "TH", abw, t)
+            gather("s", "APS", "IOTA", lnx, 0, C)
             guests(0, C)
-            guest_scan(0, C)
-            guest_cols()
-            for lo, hi in CH:
-                for t in (2, 3):
-                    own(t, "s", lo, hi)
-            far_places(lnx)
-            negatives()
+            gather("s", "VBP", "POS", lnx, 0, C, C)
+        elif not last:
+            guests(0, C)
+        whole = 0 if last else XT
+        for t in range(whole):
+            mean("X1", "HH", abw, "TB", t, 0, C)
         for c, (lo, hi) in enumerate(CH):
-            for t in range(4):
-                W = C * t
-                tt(T.X1[:, 4 * lo + t:4 * hi:4], T.HH[:, W:W + C].indirect(T[abw][:, lo // 16:hi // 16]), T.TB[:, W + lo:W + hi], A.add,
-                   [("HH", W, W + C), abw, ("TB", W + lo, W + hi)], [("X1_%d" % t, lo, hi)])
-                if not last and c == 0 and t == 0:
-                    guest_list()
+            for t in range(whole, 4):
+                mean("X1", "HH", abw, "TB", t, lo, hi)
             quant(xq, xs, lo, hi, T.X1[:, 4 * lo:4 * hi], [("X1_%d" % t, lo, hi) for t in range(4)])
             if not last:
-                scores(k + 1, c)
-                ship(k + 1, c)
+                scores(k + 1, c, lo, hi)
+                if not OWN[k + 1]:
+                    ship(k + 1, c, "x%s" + str(k + 1))
+                if c == 1:
+                    unpack(k + 1, 0, 0, C)
+                    guest_list(0, C)
+                    if not OWN[k]:
+                        host_slots()
+                signs("sv"[c], c, lo, hi)
             else:
                 mm("PS", c, hi - lo, "vq", "vqs", 0, xq, xs, lo, hi)
                 dma("y", "oc%d" % c, T.oc[:, 4 * lo:4 * hi], T[xq][:, lo:hi].bitcast(dt.uint8), [(xq, lo, hi)], [])
@@ -516,10 +569,7 @@ def rank_program(g, core, T, topo):
                         dma("y", "osc%d" % i, T.osc[4 * i:4 * i + 4, :], T[xs][32 * i:32 * i + 4, :], [xs], [])
                 src, key = bank("PS", c, hi - lo)
                 act(T.ysb[:, lo:hi], src, [key], [("ysb", lo, hi)])
-                dma("y", "y%d" % c, T.y[:, lo:hi], T.ysb[:, lo:hi], [("ysb", lo, hi)], [])
-        if not last:
-            unpack(k + 1)
-            hosts()
+                dma("ys"[c], "y%d" % c, T.y[:, lo:hi], T.ysb[:, lo:hi], [("ysb", lo, hi)], [])
     for sem, val in total.items():
         if know["g"].get(sem, 0) < val:
             g.wait_ge(T.sem[sem], val)

@@ -12,12 +12,21 @@ E = 2.0 ** -30
 FB = 368
 RB = 16
 TOP = 7
-SHARE = [192, 192, 192, 160, 0, 0, 0, 0]
-GV = 224
+HALVES = [(0, 192), (192, C)]
+TAIL = [(0, 128), (128, 256), (256, C)]
+TAIL2 = [(0, 256), (256, C)]
+LV = [(0, C)]
+AP = "ss"
+JUMP = ["ss", "ss", "ss", "ss", "ss", "ss", "ss"]
+AT = [1, 2, 2, 4, 4]
+GV = 256
 XT = 2
 HORDER = {True: [(0, 0), (0, 1), (1, 0), (0, 2), (1, 1), (0, 3), (1, 2), (1, 3)],
           False: [(0, 0), (0, 1), (0, 2), (1, 0), (1, 1), (0, 3), (1, 2), (1, 3)]}
 F8 = "float8_e4m3fn_x4"
+CYCLE, WAKE, FLIGHT, LOAD, SPARE = 0.00092, 0.14, 2.2, 2.0, 0.25
+SLACK = 0.03
+RATE = {True: 200e3, False: 100e3}
 
 SCRATCH = {
     "nxi": ("sbuf", [128, W16], "int32"),
@@ -38,14 +47,14 @@ for _n in ("X0", "X1", "TH", "THP", "TB", "TBP", "Z", "HH"):
     SCRATCH[_n] = ("sbuf", [128, 4 * C], "bfloat16")
 for _n in ("ONES", "D0", "D1", "CNT"):
     SCRATCH[_n] = ("sbuf", [128, 2 * C], "bfloat16")
-for _n in ("IOTA", "DG", "PTa", "PTb", "PTc", "OB", "GU", "SELO", "SELA", "SELP", "SELH", "SELL", "SEL0", "SEL1", "SEL2",
-           "POS", "BPS", "APS", "VBP", "GA", "GB", "sc", "up", "lv", "st"):
+for _n in ("IOTA", "DG", "OB", "GU", "SELO", "SELA", "SELP", "SELH", "SELL", "SELB", "SELC", "SELJ0", "SELJ1",
+           "POS", "BPS", "APS", "VBP", "GA", "GB", "sc", "up", "lv", "st", "PT0", "PT1", "PT2", "PT3"):
     SCRATCH[_n] = ("sbuf", [128, C], "bfloat16")
 for _n in ("ysb", "nrs"):
     SCRATCH[_n] = ("sbuf", [128, C], "float32")
 for _n in ("C16", "jw", "jm", "j2", "m1", "m2", "m3", "pw", "dq", "dk"):
     SCRATCH[_n] = ("sbuf", [128, W16], "float32")
-for _n in ("lp", "l16", "L1", "La", "Lb", "slw", "p2u", "ow", "aw", "hq"):
+for _n in ("lp", "l16", "L1", "LB", "LJ0", "LJ1", "slw", "p2u", "ow", "aw", "hq"):
     SCRATCH[_n] = ("sbuf", [128, W16], "uint16")
 for _k in range(1, ROUNDS + 2):
     SCRATCH["xq%d" % _k] = ("sbuf", [128, C], F8)
@@ -58,8 +67,43 @@ for _k in range(1, ROUNDS + 1):
         SCRATCH[_n + str(_k)] = ("sbuf", [128, 2 * W16], "uint16")
 
 LOCAL = ["nx", "x", "u", "ws", "wc", "v", "y0", "y1", "nr", "oc0", "oc1", "osc0", "osc1", "osc2", "osc3"]
-REMOTE = ["nx1", "nx2", "nx3", "ab1", "ab2", "ab3"] + [n + str(k) + str(c) for k in (1, 2, 3) for n in "qs" for c in (0, 1)]
+REMOTE = ["nb1", "nx1", "nx2", "nx3", "ab1", "ab2", "ab3"] + [n + str(k) + str(c) for k in (1, 2, 3) for n in "qs" for c in (0, 1)]
 SEMAPHORES = ["cv", "cs", "ct", "cg"] + ["d_" + n for n in LOCAL] + ["r_" + n for n in REMOTE] + ["l_" + n for n in REMOTE]
+
+
+def lay_out(calls):
+    busy, place = {}, {}
+
+    def put(i):
+        c = calls[i]
+        for p in sorted(c["needs"] | c["behind"]):
+            if p not in place:
+                put(p)
+        ready = max([place[p][2] + calls[p]["lag"] for p in c["needs"]] + [place[p][2] for p in c["behind"]], default=0.0)
+        best = None
+        for q, (_, t) in c["on"].items():
+            at, line = ready, busy.setdefault(q, [])
+            k = len(line)
+            while k > 0 and line[k - 1][1] > ready:
+                k -= 1
+            while q and k < len(line) and at + t > line[k][0] + SLACK:
+                at = max(at, line[k][1])
+                k += 1
+            score = at + t + (SPARE if q == "v" and len(c["on"]) > 1 else 0.0)
+            if best is None or score < best[0]:
+                best = (score, k, q, at, at + t)
+        place[i] = best[2:]
+        if best[2]:
+            busy[best[2]].insert(best[1], best[3:])
+
+    for late in (False, True):
+        for i, c in enumerate(calls):
+            if c["late"] == late and i not in place:
+                put(i)
+    return [(i, place[i][0]) for i in sorted(place, key=lambda i: (place[i][1], i))]
+
+
+ORDER = []
 
 
 def rank_program(g, core, T, topo):
@@ -68,130 +112,148 @@ def rank_program(g, core, T, topo):
         return
     A = AluOpType
     AF = ActivationFunctionType
-    eng = {"v": g.vector, "s": g.scalar, "t": g.tensor, "g": g, "y": g.sync}
-    total, know = {}, {q: {} for q in eng}
-    writes, reads = {}, {}
+    V, S = g.vector, g.scalar
+    eng = {"v": V, "s": S, "t": g.tensor, "g": g, "y": g.sync}
+    COUNT = {"v": "cv", "s": "cs", "t": "ct", "g": "cg"}
+    calls, writes, reads, latest, mood = [], {}, {}, {}, [False]
+
+    def late(f, *args):
+        mood[0] = True
+        f(*args)
+        mood[0] = False
 
     def norm(k):
         return k if isinstance(k, tuple) else (k, 0, 1 << 20)
 
-    def conflicts(table, k):
-        return [e for e in table.get(k[0], []) if e[0] < k[2] and k[1] < e[1]]
+    def meets(table, k):
+        return {e[2] for e in table.get(k[0], []) if e[0] < k[2] and k[1] < e[1]}
 
-    def order(q, rd, wr):
-        need = []
+    def call(on, rd, wr, lag=WAKE, sem=None, inc=1, row=None):
+        rd, wr, needs = [norm(k) for k in rd], [norm(k) for k in wr], set()
         for k in rd:
-            need += [e[2] for e in conflicts(writes, k)]
+            needs |= meets(writes, k)
             if k[0] in ("PA", "PB", "PS"):
-                need += [e[2] for e in conflicts(reads, k) if e[2][3] != q]
+                needs |= {p for p in meets(reads, k) if len(on) > 1 or list(calls[p]["on"]) != list(on)}
         for k in wr:
-            need += [e[2] for e in conflicts(writes, k)]
-            need += [e[2] for e in conflicts(reads, k)]
-        kn = know[q]
-        want = {}
-        for sem, val, clock, _ in need:
-            if kn.get(sem, 0) < val and want.get(sem, (0,))[0] < val:
-                want[sem] = (val, clock)
-        for sem in list(want):
-            if any(o != sem and want[o][1].get(sem, 0) >= want[sem][0] for o in want):
-                del want[sem]
-        for sem, (val, clock) in want.items():
-            eng[q].wait_ge(T.sem[sem], val)
-            for s2, v2 in clock.items():
-                kn[s2] = max(kn.get(s2, 0), v2)
-            kn[sem] = max(kn.get(sem, 0), val)
-
-    def note(q, sem, inc, rd, wr):
-        total[sem] = total.get(sem, 0) + inc
-        clock = dict(know[q])
-        clock[sem] = total[sem]
-        ev = (sem, total[sem], clock, q)
+            needs |= meets(writes, k) | meets(reads, k)
+        i = len(calls)
+        calls.append({"on": on, "needs": needs, "behind": {latest[row]} if row in latest else set(), "lag": lag, "sem": sem,
+                      "inc": inc, "late": mood[0]})
+        if row:
+            latest[row] = i
         for k in wr:
             for t in (writes, reads):
                 t[k[0]] = [e for e in t.get(k[0], []) if not (k[1] <= e[0] and e[1] <= k[2])]
-            writes[k[0]].append((k[1], k[2], ev))
+            writes[k[0]].append((k[1], k[2], i))
         for k in rd:
-            reads[k[0]] = reads.get(k[0], []) + [(k[1], k[2], ev)]
+            reads[k[0]] = reads.get(k[0], []) + [(k[1], k[2], i)]
+        return i
 
-    COUNT = {"v": "cv", "s": "cs", "t": "ct", "g": "cg"}
+    def issue():
+        total, know, event = {}, {q: {} for q in eng}, {}
+        if not ORDER:
+            ORDER.extend(lay_out(calls))
+        for i, q in ORDER:
+            c = calls[i]
+            if q is None:
+                total[c["sem"]] = c["inc"]
+                event[i] = (c["sem"], c["inc"], {c["sem"]: c["inc"]})
+                continue
+            kn, want = know[q], {}
+            for sem, val, clock in [event[p] for p in c["needs"]]:
+                if kn.get(sem, 0) < val and want.get(sem, (0,))[0] < val:
+                    want[sem] = (val, clock)
+            for sem in sorted(want):
+                if any(o != sem and want[o][1].get(sem, 0) >= want[sem][0] for o in want):
+                    del want[sem]
+            for sem, (val, clock) in sorted(want.items()):
+                eng[q].wait_ge(T.sem[sem], val)
+                for s2, v2 in clock.items():
+                    kn[s2] = max(kn.get(s2, 0), v2)
+            sem = c["sem"] or COUNT[q]
+            done = c["on"][q][0]()
+            if not sem.startswith("l_"):
+                done.then_inc(T.sem[sem], c["inc"])
+            total[sem] = total.get(sem, 0) + c["inc"]
+            event[i] = (sem, total[sem], dict(kn, **{sem: total[sem]}))
+        for sem, val in total.items():
+            if know["g"].get(sem, 0) < val:
+                g.wait_ge(T.sem[sem], val)
 
-    def op(q, call, rd, wr):
-        rd, wr = [norm(k) for k in rd], [norm(k) for k in wr]
-        order(q, rd, wr)
-        call().then_inc(T.sem[COUNT[q]], 1)
-        note(q, COUNT[q], 1, rd, wr)
+    def plain(n, rate=1.0):
+        return max(64, n * rate) * CYCLE
 
-    def dma(q, name, out, in_, rd, wr):
-        rd, wr = [norm(k) for k in rd], [norm(k) for k in wr]
-        order(q, rd, wr)
-        eng[q].dma_start(out, in_).then_inc(T.sem["d_" + name], 16)
-        note(q, "d_" + name, 16, rd, wr)
+    def picked(n, rate=1.56):
+        return 0.055 + n * rate * CYCLE
 
-    def send(name, dst, out, in_, rd):
-        order("g", [norm(rd)], [])
+    def dma(q, name, out, in_, rd, wr, lag=LOAD):
+        call({q: (lambda: eng[q].dma_start(out, in_), 0.05)}, rd, wr, lag, "d_" + name, 16, "dma" + q)
+
+    def send(name, dst, out, in_, rd, lands, width):
         rid, pid = topo.addr(dst)[:2]
-        g.remote_dma(out, in_, T.sem["r_" + name], T.sem["l_" + name], pid, rid, topo.mask(core, dst))
-        note("g", "l_" + name, len(topo.engines(core, dst)), [norm(rd)], [])
-
-    def arrives(name, src, buf, lo=0, hi=1 << 20):
-        n = len(topo.engines(src, core))
-        total["r_" + name] = n
-        writes[buf] = writes.get(buf, []) + [(lo, hi, ("r_" + name, n, {"r_" + name: n}, "x"))]
+        lag = FLIGHT + 128 * width / RATE[topo.chip(core) == topo.chip(dst)]
+        i = call({"g": (lambda: g.remote_dma(out, in_, T.sem["r_" + name], T.sem["l_" + name], pid, rid, topo.mask(core, dst)), 0.1)},
+                 [rd], [], lag, "l_" + name, len(topo.engines(core, dst)), "g")
+        j = call({None: (None, 0.0)}, [], [lands], 0.0, "r_" + name, len(topo.engines(dst, core)))
+        calls[j]["needs"] = {i}
+        if "landed" in latest:
+            calls[j]["behind"] = {latest["landed"]}
+        latest["landed"] = j
 
     partner = [T.cores[rank ^ m] for m in MASKS]
-    for k in (1, 2, 3):
-        for c, (lo, hi) in enumerate(CH):
-            arrives("q%d%d" % (k, c), partner[k - 1], "lq%d" % k, lo, hi)
-            if OWN[k]:
-                arrives("s%d%d" % (k, c), partner[k - 1], "ls%d" % k, lo, hi)
-        if not OWN[k]:
-            arrives("s%d1" % k, partner[k - 1], "ls%d" % k)
-            arrives("ab%d" % k, partner[k - 1], "lab%d" % k)
-        arrives("nx%d" % k, partner[k - 1], "lnx%d" % k, 0, W16 if k == 1 else 2 * W16)
 
-    V, S = g.vector, g.scalar
+    def ts(out, in0, s1, s2, o0, o1, rd, wr, rate=1.0):
+        ops = (o0,) if o1 is None else (o0, o1)
+        call({"v": (lambda: V.tensor_scalar(out, in0, s1, s2, *ops), plain(out.shape[1], rate))}, rd, wr)
 
-    def ts(out, in0, s1, s2, o0, o1, rd, wr):
-        if o1 is None:
-            op("v", lambda: V.tensor_scalar(out, in0, s1, None, o0), rd, wr)
-        else:
-            op("v", lambda: V.tensor_scalar(out, in0, s1, s2, o0, o1), rd, wr)
+    def tt(out, in0, in1, o, rd, wr, pick=False):
+        n = out.shape[1]
+        call({"v": (lambda: V.tensor_tensor(out, in0, in1, o), picked(n) if pick else plain(n, 2))}, rd, wr)
 
-    def tt(out, in0, in1, o, rd, wr):
-        op("v", lambda: V.tensor_tensor(out, in0, in1, o), rd, wr)
-
-    def vcopy(out, in_, rd, wr):
-        op("v", lambda: V.tensor_copy(out, in_), rd, wr)
+    def vcopy(out, in_, rd, wr, rate=1.0):
+        call({"v": (lambda: V.tensor_copy(out, in_), plain(out.shape[1], rate))}, rd, wr)
 
     def fill(ap, val, wr):
-        op("v", lambda: V.memset(ap, val), [], wr)
+        call({"v": (lambda: V.memset(ap, val), plain(ap.shape[1], 0.5))}, [], wr)
 
     def scan(out, d0, d1, init, o0, o1, rd, wr):
-        op("v", lambda: V.tensor_tensor_scan(out, d0, d1, init, o0, o1), rd, wr)
+        call({"v": (lambda: V.tensor_tensor_scan(out, d0, d1, init, o0, o1), plain(out.shape[1], 0.5))}, rd, wr)
 
-    def act(out, in_, rd, wr, scale=None, func=AF.Copy):
-        if scale is None:
-            op("s", lambda: S.activation(out, in_, func), rd, wr)
-        else:
-            op("s", lambda: S.activation(out, in_, func, scale=scale), rd, wr)
+    def act(out, in_, rd, wr, func):
+        call({"s": (lambda: S.activation(out, in_, func), plain(out.shape[1]))}, rd, wr)
 
-    def sid(out, in_, rd, wr, scale, bias):
-        op("s", lambda: S.activation(out, in_, AF.Identity, bias=bias, scale=scale), rd, wr)
+    def line(qs, out, in_, rd, wr, scale, bias=0.0, rate=1.0):
+        n = out.shape[1]
+        on = {"s": (lambda: S.activation(out, in_, AF.Identity, bias=bias, scale=scale), plain(n)),
+              "v": (lambda: V.tensor_scalar(out, in_, scale, bias, A.mult, A.add), plain(n, rate))}
+        call({q: on[q] for q in qs}, rd, wr)
+
+    def pick(qs, out, win, rd, wr):
+        n = out.shape[1]
+        on = {"s": (lambda: S.activation(out, win, AF.Copy), picked(n) + 0.015), "v": (lambda: V.tensor_copy(out, win), picked(n))}
+        call({q: on[q] for q in qs}, rd, wr)
 
     def quant(codes, plane, lo, hi, src, rd):
-        op("v", lambda: V.quantize_mx(T[codes][:, lo:hi], T[plane][:, lo:hi], src), rd, [(codes, lo, hi), (plane, lo, hi)])
+        call({"v": (lambda: V.quantize_mx(T[codes][:, lo:hi], T[plane][:, lo:hi], src), 0.013 + 0.00097 * (hi - lo))},
+             rd, [(codes, lo, hi), (plane, lo, hi)])
 
     def mm(P, s, n, l, ls, a, r, rs, lo, hi):
-        op("t", lambda: g.tensor.matmul_mx(T[P][:, 512 * s:512 * s + n], T[l][:, a:a + 128], T[ls][:, a:a + 128],
-                                           T[r][:, lo:hi], T[rs][:, lo:hi], True, True),
-           [(l, a, a + 128), (ls, a, a + 128), (r, lo, hi), (rs, lo, hi)], [(P, 512 * s, 512 * s + 512)])
+        call({"t": (lambda: g.tensor.matmul_mx(T[P][:, 512 * s:512 * s + n], T[l][:, a:a + 128], T[ls][:, a:a + 128],
+                                               T[r][:, lo:hi], T[rs][:, lo:hi], True, True), 1.4 * (n + 16) * CYCLE)},
+             [(l, a, a + 128), (ls, a, a + 128), (r, lo, hi), (rs, lo, hi)], [(P, 512 * s, 512 * s + 512)])
+
+    def pool(f, n, rd, wr):
+        call({"g": (f, 0.15 + 2 * n * CYCLE)}, rd, wr, row="g")
 
     def bank(P, s, n):
         return T[P][:, 512 * s:512 * s + n], (P, 512 * s, 512 * s + 512)
 
-    def gather(q, out, win, lst, lo, hi, at=0):
-        (vcopy if q == "v" else act)(T[out][:, lo:hi], T[win][:].indirect(T[lst][:, (at + lo) // 16:(at + hi) // 16]),
-                                     [win, (lst, (at + lo) // 16, (at + hi) // 16)], [(out, lo, hi)])
+    def cols(lst, lo, hi, at=0):
+        return T[lst][:, (at + lo) // 16:(at + hi) // 16], (lst, (at + lo) // 16, (at + hi) // 16)
+
+    def gather(qs, out, win, lst, lo=0, hi=C, at=0):
+        off, key = cols(lst, lo, hi, at)
+        pick(qs, T[out][:, lo:hi], T[win][:].indirect(off), [win, key], [(out, lo, hi)])
 
     def keep16(out, src, lo=0, hi=C):
         scan(T[out][:, lo:hi], T[src][:, lo:hi], T.DG[:, 0:hi - lo], 0.0, A.add, A.mult, ["DG", (src, lo, hi)], [(out, lo, hi)])
@@ -200,20 +262,28 @@ def rank_program(g, core, T, topo):
         return T[sel][:, lo + 15:hi:16]
 
     def enlist(lst, sel, lo=0, hi=C, at=0):
-        ts(T[lst][:, (at + lo) // 16:(at + hi) // 16], kept(sel, lo, hi), 1 / E, HALF + 0.25, A.mult, A.add,
-           [(sel, lo, hi)], [(lst, (at + lo) // 16, (at + hi) // 16)])
+        off, key = cols(lst, lo, hi, at)
+        ts(off, kept(sel, lo, hi), 1 / E, HALF + 0.25, A.mult, A.add, [(sel, lo, hi)], [key])
+
+    def listed(lst, sel, src, lo=0, hi=C, at=0):
+        keep16(sel, src, lo, hi)
+        enlist(lst, sel, lo, hi, at)
+
+    def invert(out, lst, lo=0, hi=C):
+        off, key = cols(lst, lo, hi)
+        call({"v": (lambda: V.tensor_copy(T[out][:].indirect(off), T.IOTA[:, lo:hi]), picked(hi - lo, 3.8))}, ["IOTA", key], [out])
 
     dma("y", "nx", T.nxi[:], T.nx[:], [], ["nxi"])
-    dma("y", "u", T.ut[:], T.u[:], [], ["ut"])
-    dma("y", "x", T.X0[:], T.x[:], [], ["X0"])
+    dma("y", "u", T.ut[:], T.u[:], [], ["ut"], LOAD + 0.6)
+    dma("y", "x", T.X0[:], T.x[:], [], ["X0"], LOAD + 2.0)
 
     def iota(name, pattern):
-        op("g", lambda: g.iota(T[name][:], pattern, 0, 0, allow_small_or_imprecise_dtypes=True), [], [name])
+        pool(lambda: g.iota(T[name][:], pattern, 0, 0, allow_small_or_imprecise_dtypes=True), pattern[0][1], [], [name])
 
-    op("g", lambda: g.iota(T.pi[:], [[0, 1]], 0, 1), [], ["pi"])
+    pool(lambda: g.iota(T.pi[:], [[0, 1]], 0, 1), 1, [], ["pi"])
     iota("J16", [[1, 16]])
     fill(T.ONES[:], 1.0, ["ONES"])
-    op("g", lambda: g.affine_select(T.EB[:], T.ONES[:, 0:516], [[1, 516]], A.is_equal, 0.0, -4, -4), ["ONES"], ["EB"])
+    pool(lambda: g.affine_select(T.EB[:], T.ONES[:, 0:516], [[1, 516]], A.is_equal, 0.0, -4, -4), 516, ["ONES"], ["EB"])
     iota("C16", [[16, W16]])
     ts(T.pj[:], T.pi[:], 15, None, A.bitwise_and, None, ["pi"], ["pj"])
     scan(T.IOTA[:], T.ONES[:, 0:C], T.ONES[:, 0:C], -HALF - 1.0, A.mult, A.add, ["ONES"], ["IOTA"])
@@ -225,249 +295,200 @@ def rank_program(g, core, T, topo):
     tt(T.D16[:], T.DA[:], T.DB[:], A.add, ["DA", "DB"], ["D16"])
     fill(T.OB[:, 0:1], -float(HALF), [("OB", 0, 1)])
     ts(T.D16[:, 15:16], T.D16[:, 15:16], E * E, None, A.mult, None, ["D16"], ["D16"])
-    gather("s", "DG", "D16", "lp", 0, C)
+    gather("s", "DG", "D16", "lp")
     for b in range(4):
-        quant("eq", "eqs", 128 * b, 128 * b + 128, T.EB[:, 4 - b:516 - b], ["EB"])
+        late(quant, "eq", "eqs", 128 * b, 128 * b + 128, T.EB[:, 4 - b:516 - b], ["EB"])
     vcopy(T.L1[:], T.nxi[:], ["nxi"], ["L1"])
-    send("nx1", partner[0], T.lnx1[:, 0:W16], T.L1[:], "L1")
-    dma("y", "ws", T.wsq[:], T.ws[:], [("lnx1", 0, W16)], ["wsq"])
-    dma("y", "wc", T.wq[:].bitcast(dt.uint8), T.wc[:], [], ["wq"])
-    dma("y", "v", T.vt[:], T.v[:], [], ["vt"])
-
-    def columns():
-        vcopy(T.l16[:], T.C16[:], ["C16"], ["l16"])
-        sid(T.jw[:], T.C16[:], ["C16", "p16"], ["jw"], 1.0, T.p16[:, 0:1])
-        sid(T.jm[:], T.jw[:], ["jw"], ["jm"], E, -HALF * E)
-        sid(T.j2[:], T.jw[:], ["jw"], ["j2"], E * E, 0.25 * E * E)
+    send("nx1", partner[0], T.lnx1[:, 0:W16], T.L1[:], "L1", ("lnx1", 0, W16), 2 * W16)
+    late(lambda: vcopy(T.l16[:], T.C16[:], ["C16"], ["l16"]))
+    late(lambda: line("s", T.jw[:], T.C16[:], ["C16", "p16"], ["jw"], 1.0, T.p16[:, 0:1]))
+    late(lambda: line("sv", T.jm[:], T.jw[:], ["jw"], ["jm"], E, -HALF * E))
+    late(lambda: line("sv", T.j2[:], T.jw[:], ["jw"], ["j2"], E * E, 0.25 * E * E))
 
     def ucols():
         quant("uq", "uqs", 0, 128, T.ut[:], ["ut"])
-        act(T.up16s[:, 0:128], T.uqs[:, 0:128].indirect(T.l16[:, 0:8]), ["uqs", "l16"], ["up16s"])
-        vcopy(T.up16[:, 0:128].bitcast(dt.uint32), T.uq[:, 0:128].bitcast(dt.uint32).indirect(T.l16[:, 0:8]), ["uq", "l16"], ["up16"])
+        pick("v", T.up16s[:, 0:128], T.uqs[:, 0:128].indirect(T.l16[:, 0:8]), ["uqs", "l16"], ["up16s"])
+        pick("v", T.up16[:, 0:128].bitcast(dt.uint32), T.uq[:, 0:128].bitcast(dt.uint32).indirect(T.l16[:, 0:8]), ["uq", "l16"], ["up16"])
 
     def scores(k, c, lo, hi):
         mm("PS", c, hi - lo, "up16", "up16s", 0, "xq%d" % k, "xs%d" % k, lo, hi)
 
     def ship(k, c, n):
         p, (lo, hi) = partner[k - 1], CH[c]
-        send("q%d%d" % (k, c), p, T["lq%d" % k][:, lo:hi].bitcast(dt.uint8), T[n % "q"][:, lo:hi].bitcast(dt.uint8), (n % "q", lo, hi))
+        lq, ls = "lq%d" % k, "ls%d" % k
+        send("q%d%d" % (k, c), p, T[lq][:, lo:hi].bitcast(dt.uint8), T[n % "q"][:, lo:hi].bitcast(dt.uint8), (n % "q", lo, hi),
+             (lq, lo, hi), 4 * (hi - lo))
         if not OWN[k]:
             if c == 0:
                 return
             lo = 0
-        send("s%d%d" % (k, c), p, T["ls%d" % k][:, lo:hi], T[n % "s"][:, lo:hi], (n % "s", lo, hi))
+        send("s%d%d" % (k, c), p, T[ls][:, lo:hi], T[n % "s"][:, lo:hi], (n % "s", lo, hi), (ls, lo, hi), 5 * (hi - lo))
 
     def signs(q, c, lo, hi):
         src, key = bank("PS", c, hi - lo)
         if q == "v":
-            ts(T.up[:, lo:hi], src, 0.0, None, A.is_gt, None, [key], [("up", lo, hi)])
-            if hi - lo < C:
-                ts(T.sc[:, lo:hi], src, 0.0, None, A.is_gt, None, [key], [("sc", lo, hi)])
-            else:
-                vcopy(T.sc[:], T.up[:], ["up"], ["sc"])
+            for n in ("up", "sc"):
+                ts(T[n][:, lo:hi], src, 0.0, None, A.is_gt, None, [key], [(n, lo, hi)])
         else:
-            act(T.sc[:, lo:hi], src, [key], [("sc", lo, hi)], func=AF.Sign)
-            act(T.up[:, lo:hi], T.sc[:, lo:hi], [("sc", lo, hi)], [("up", lo, hi)], func=AF.Relu)
+            act(T.sc[:, lo:hi], src, [key], [("sc", lo, hi)], AF.Sign)
+            act(T.up[:, lo:hi], T.sc[:, lo:hi], [("sc", lo, hi)], [("up", lo, hi)], AF.Relu)
 
     def place(c, b):
         return ("PA", b) if c == 0 else ("PB", b) if b < 2 else ("PA", b - 2)
 
-    def unpack(k, c, lo, hi, bs=range(4)):
-        for b in bs:
-            mm(*place(c, b), hi - lo, "eq", "eqs", 128 * b, "xq%d" % k, "xs%d" % k, lo, hi)
+    def product(P, s, l, ls, b, r, rs, lo, hi, out, scale, qs="sv"):
+        mm(P, s, hi - lo, l, ls, 128 * b, r, rs, lo, hi)
+        src, key = bank(P, s, hi - lo)
+        line(qs, T[out][:, C * b + lo:C * b + hi], src, [key], [(out, C * b + lo, C * b + hi)], scale)
 
-    def halve(q, out, src, key, okey, scale):
-        if q == "s":
-            act(out, src, [key], [okey], scale=scale)
-        else:
-            ts(out, src, scale, None, A.mult, None, [key], [okey])
+    def unpack(k):
+        for b in range(4):
+            product("PA", b, "eq", "eqs", b, "xq%d" % k, "xs%d" % k, 0, C, "TH", 0.5)
 
-    def keep(b, q="s", c=0, lo=0, hi=C):
-        src, key = bank(*place(c, b), hi - lo)
-        halve(q, T.TH[:, C * b + lo:C * b + hi], src, key, ("TH", C * b + lo, C * b + hi), 0.5)
+    def unpack_far(k):
+        for b in range(4):
+            product("PB", b % 2, "eq", "eqs", b, "lq%d" % k, "ls%d" % k, 0, C, "THP", 0.5)
 
-    def unpack_far(k, b, q="s"):
-        src, key = bank("PA", 2 + b % 2, C)
-        mm("PA", 2 + b % 2, C, "eq", "eqs", 128 * b, "lq%d" % k, "ls%d" % k, 0, C)
-        halve(q, T.THP[:, C * b:C * b + C], src, key, ("THP", C * b, C * b + C), 0.5)
+    def leavers(lst, runs=((0, C),)):
+        for lo, hi in runs:
+            off, key = cols(lst, lo, hi, C)
+            tt(T.lv[:, lo:hi], T.up[:].indirect(off), T.sc[:, lo:hi], A.is_lt, ["up", ("sc", lo, hi), key], [("lv", lo, hi)], True)
+        line("v", T.st[:], T.lv[:], ["lv"], ["st"], -1.0, 1.0, 0.5)
+        keep16("SELL", "lv")
 
-    def leavers(lst):
-        tt(T.lv[:], T.up[:].indirect(T[lst][:, W16:2 * W16]), T.sc[:], A.is_lt, ["up", "sc", lst], ["lv"])
+    def slots(odd, lo=0, hi=C):
+        off, key = cols("aw" if odd else "ow", lo, hi)
+        gone, there, who = ("st", "lv", "GU") if odd else ("lv", "st", "OB")
+        pick("s", T.D0[:, 2 * lo + odd:2 * hi:2], T[gone][:].indirect(off), [gone, key], [("D0%d" % odd, lo, hi)])
+        tt(T.D1[:, 2 * lo + odd:2 * hi:2], T[there][:].indirect(off), T[who][:, lo:hi], A.mult,
+           [there, key, (who, lo, hi)], [("D1%d" % odd, lo, hi)], True)
 
-    def stayers(q):
-        if q == "s":
-            sid(T.st[:], T.lv[:], ["lv"], ["st"], -1.0, 1.0)
-        else:
-            ts(T.st[:], T.lv[:], -1.0, 1.0, A.mult, A.add, ["lv"], ["st"])
-
-    def void(odd, lo=0, hi=C):
-        w, l = ("st", "aw") if odd else ("lv", "ow")
-        act(T.D0[:, 2 * lo + odd:2 * hi:2], T[w][:].indirect(T[l][:, lo // 16:hi // 16]), [w, (l, lo // 16, hi // 16)], [("D0%d" % odd, lo, hi)])
-
-    def real(odd, lo=0, hi=C):
-        w, l, t = ("lv", "aw", "GU") if odd else ("st", "ow", "OB")
-        tt(T.D1[:, 2 * lo + odd:2 * hi:2], T[w][:].indirect(T[l][:, lo // 16:hi // 16]), T[t][:, lo:hi], A.mult,
-           [w, (l, lo // 16, hi // 16), (t, lo, hi)], [("D1%d" % odd, lo, hi)])
-
-    def slots(odds, lo=0, hi=C):
+    def keys(odds, lo=0, hi=C):
         return [("D%d%d" % (d, o), lo, hi) for d in (0, 1) for o in odds]
-
-    def first_real():
-        r = RB + 2 * C - 1
-        scan(T.RS[:, r + MOST - 1:r - 1:-1], T.D0[:, 2 * MOST - 2::-2], T.D1[:, 2 * MOST - 2::-2], 0.0, A.mult, A.add,
-             slots([0], 0, MOST), [("RS", r, r + MOST)])
-
-    def last_real():
-        a = 2 * (C - MOST)
-        scan(T.FS[:, FB + 1 - 2 * MOST:FB + 1], T.D0[:, a:2 * C], T.D1[:, a:2 * C], 0.0, A.mult, A.add,
-             slots([0, 1], C - MOST, C), [("FS", 0, FB + 1)])
-
-    def before():
-        scan(T.FS[:, FB + 1:FB + 1 + 2 * C], T.D0[:], T.D1[:], T.FS[:, FB:FB + 1], A.mult, A.add,
-             slots([0, 1]) + [("FS", FB, FB + 1)], [("FS", FB + 1, FB + 1 + 2 * C)])
-
-    def behind():
-        r = RB + 2 * C - 1
-        scan(T.RS[:, r - 1:RB - 2:-1], T.D0[:, ::-1], T.D1[:, ::-1], T.RS[:, r:r + 1], A.mult, A.add,
-             slots([0, 1]) + [("RS", r, r + 1)], [("RS", 0, r)])
 
     def neighbours(q, out, lo, hi):
         win, a = ("RS", RB) if out == "GA" else ("FS", FB)
-        (vcopy if q == "v" else act)(T[out][:, lo:hi], T[win][:, a:a + 2 * C].indirect(T.slw[:, lo // 16:hi // 16]),
-                                     [(win, a, a + 2 * C), "slw"], [(out, lo, hi)])
+        off, key = cols("slw", lo, hi)
+        pick(q, T[out][:, lo:hi], T[win][:, a:a + 2 * C].indirect(off), [(win, a, a + 2 * C), key], [(out, lo, hi)])
 
     def lists(k):
-        abw = "abw%d" % k
-        before()
+        abw, r, a = "abw%d" % k, RB + 2 * C - 1, 2 * (C - MOST)
+        scan(T.RS[:, r + MOST - 1:r - 1:-1], T.D0[:, 2 * MOST - 2::-2], T.D1[:, 2 * MOST - 2::-2], 0.0, A.mult, A.add,
+             keys([0], 0, MOST), [("RS", r, r + MOST)])
+        scan(T.FS[:, FB + 1 - 2 * MOST:FB + 1], T.D0[:, a:2 * C], T.D1[:, a:2 * C], 0.0, A.mult, A.add,
+             keys([0, 1], C - MOST, C), [("FS", 0, FB + 1)])
+        scan(T.FS[:, FB + 1:FB + 1 + 2 * C], T.D0[:], T.D1[:], T.FS[:, FB:FB + 1], A.mult, A.add,
+             keys([0, 1]) + [("FS", FB, FB + 1)], [("FS", FB + 1, FB + 1 + 2 * C)])
+        scan(T.RS[:, r - 1:RB - 2:-1], T.D0[:, ::-1], T.D1[:, ::-1], T.RS[:, r:r + 1], A.mult, A.add,
+             keys([0, 1]) + [("RS", r, r + 1)], [("RS", 0, r)])
         neighbours("s", "GB", 0, C)
-        behind()
         neighbours("v", "GA", 0, GV)
         neighbours("s", "GA", GV, C)
-        keep16("SEL1", "GB")
-        enlist(abw, "SEL1", 0, C, C)
-        keep16("SEL2", "GA")
-        enlist(abw, "SEL2")
+        keep16("SELB", "GB")
+        keep16("SELC", "GA")
+        enlist(abw, "SELC")
+        enlist(abw, "SELB", 0, C, C)
         if not OWN[k]:
-            send("ab%d" % k, partner[k - 1], T["lab%d" % k][:], T[abw][:], abw)
+            send("ab%d" % k, partner[k - 1], T["lab%d" % k][:], T[abw][:], abw, "lab%d" % k, 4 * W16)
         if k < ROUNDS:
-            send("nx%d" % (k + 1), partner[k], T["lnx%d" % (k + 1)][:], T[abw][:], abw)
+            send("nx%d" % (k + 1), partner[k], T["lnx%d" % (k + 1)][:], T[abw][:], abw, "lnx%d" % (k + 1), 4 * W16)
 
     def splice(k):
         leavers("lnx%d" % k)
-        keep(0)
-        stayers("s")
-        real(1)
-        void(0)
-        keep16("SELL", "lv")
-        real(0)
-        void(1)
+        slots(0)
         tt(T.m2[:], kept("SELL"), T.dk[:], A.mult, ["SELL", "dk"], ["m2"])
-        first_real()
+        slots(1)
         tt(T.m3[:], T.m2[:], T.pw[:], A.add, ["m2", "pw"], ["m3"])
-        keep(1)
-        last_real()
-        ts(T.slw[:], T.m3[:], 1 / E / E, None, A.mult, None, ["m3"], ["slw"])
-        keep(2)
+        late(lambda: ts(T.slw[:], T.m3[:], 1 / E / E, None, A.mult, None, ["m3"], ["slw"]))
         lists(k)
-        keep(3)
 
-    def count():
+    def guests(lo=0, hi=C):
+        gather("s", "GU", "APS", "ow", lo, hi)
+        listed("aw", "SELA", "GU", lo, hi)
+
+    def new_places():
         scan(T.CNT[:], T.ONES[:], T.D0[:], -HALF - 1.0, A.add, A.subtract, ["ONES", "D00", "D01"], ["CNT"])
+        gather("s", "POS", "CNT", "slw")
 
-    def places():
-        gather("s", "POS", "CNT", "slw", 0, C)
+    def new_order():
+        listed("p2u", "SELP", "POS")
+        invert("OB", "p2u")
 
-    def lay(lst, lo=0, hi=C):
-        out, key = {"p2u": ("OB", "OB"), "ow": ("POS", "POS"), "lnx1": ("BPS", "BPS")}[lst]
-        op("v", lambda: V.tensor_copy(T[out][:].indirect(T[lst][:, lo // 16:hi // 16]), T.IOTA[:, lo:hi]),
-           ["IOTA", (lst, lo // 16, hi // 16)], [key])
-
-    def own_slots():
-        sid(T.pw[:], kept("SELP"), ["SELP"], ["pw"], 2 * E, (C + 0.25) * E * E)
-
-    def host_slots():
+    def new_slots(lnx):
+        listed("ow", "SELO", "OB")
+        gather("s", "APS", "IOTA", lnx)
+        gather("s", "VBP", "POS", lnx, 0, C, C)
+        guests()
+        line("s", T.pw[:], kept("SELP"), ["SELP"], ["pw"], 2 * E, (C + 0.25) * E * E)
         keep16("SELH", "VBP")
         tt(T.dq[:], kept("SELH"), kept("SELP"), A.subtract, ["SELH", "SELP"], ["dq"])
-        sid(T.dk[:], T.dq[:], ["dq"], ["dk"], 2.0, E)
+        line("s", T.dk[:], T.dq[:], ["dq"], ["dk"], 2.0, E)
 
-    def jump(out, win, lst, share):
-        cut = share or 192
-        gather("v" if share else "s", out, win, lst, 0, cut)
-        gather("s", out, win, lst, cut, C)
-        return cut
+    def first_signs():
+        quant("xq1", "xs1", 0, C, T.X0[:], ["X0"])
+        scores(1, 0, 0, C)
+
+    def first_hosts():
+        src, key = bank("PS", 0, C)
+        ts(T.up[:], src, 0.0, None, A.is_gt, None, [key], ["up"])
+        vcopy(T.sc[:], T.up[:], ["up"], ["sc"], 0.5)
+
+    def first_guests():
+        for q, (lo, hi) in zip(AP, HALVES):
+            gather(q, "APS", "IOTA", "lnx1", lo, hi)
+
+    def first_leavers():
+        leavers("lnx1", LV)
+        ts(T.dk[:], T.lnx1[:, W16:2 * W16], E, -HALF * E, A.mult, A.add, ["lnx1"], ["dk"])
+        tt(T.dq[:], T.dk[:], T.jm[:], A.subtract, ["dk", "jm"], ["dq"])
+        tt(T.m2[:], kept("SELL"), T.dq[:], A.mult, ["SELL", "dq"], ["m2"])
+        tt(T.m3[:], T.m2[:], T.j2[:], A.add, ["m2", "j2"], ["m3"])
+        ts(T.hq[:], T.m3[:], 1 / E / E, None, A.mult, None, ["m3"], ["hq"])
+        line("sv", T.m1[:], kept("SELL"), ["SELL"], ["m1"], 0.5, (HALF + 0.125) * E)
 
     def ahead(P, m, n, a):
-        act(T.OB[:, m:m + n], T[P][:].indirect(T.ow[:, a // 16:(a + n) // 16]), [P, ("ow", a // 16, (a + n) // 16)], [("OB", m, m + n)])
-
-    def order_list(m, n):
+        off, key = cols("ow", a, a + n)
+        pick("s", T.OB[:, m:m + n], T[P][:].indirect(off), [P, key], [("OB", m, m + n)])
         b = 0 if m < 16 else m
-        keep16("SELO", "OB", b, b + n)
-        enlist("ow", "SELO", b, b + n)
+        listed("ow", "SELO", "OB", b, b + n)
 
-    def guests(lo, hi):
-        gather("s", "GU", "APS", "ow", lo, hi)
-
-    def guest_list(lo, hi):
-        keep16("SELA", "GU", lo, hi)
-        enlist("aw", "SELA", lo, hi)
-
-    extra = {
-        0: [columns],
-        1: [ucols],
-        2: [lambda: quant("xq1", "xs1", 0, C, T.X0[:], ["X0"]), lambda: scores(1, 0, 0, C), lambda: unpack(1, 0, 0, C)]
-           + ([] if OWN[1] else [lambda: ship(1, 0, "x%s1"), lambda: ship(1, 1, "x%s1")]),
-        3: [lambda: signs("v", 0, 0, C), lambda: lay("lnx1", 0, 128)],
-        4: [lambda: lay("lnx1", 128, 256), lambda: lay("lnx1", 256, C)],
-        5: [lambda: keep16("SELH", "BPS"), lambda: enlist("lnx1", "SELH", 0, C, C), lambda: leavers("lnx1")],
-        6: [lambda: stayers("v"), lambda: keep16("SELL", "lv")],
-    }
-    jump("PTa", "IOTA", "L1", SHARE[0])
+    gather("s", "PT0", "IOTA", "L1")
+    invert("BPS", "L1")
+    late(listed, "LB", "SELH", "BPS")
+    late(send, "nb1", partner[0], T.lnx1[:, W16:2 * W16], T.LB[:], "LB", ("lnx1", W16, 2 * W16), 2 * W16)
+    late(dma, "y", "ws", T.wsq[:], T.ws[:], ["lnx1"], ["wsq"])
+    late(dma, "y", "wc", T.wq[:].bitcast(dt.uint8), T.wc[:], [], ["wq"], LOAD + 1.5)
+    late(dma, "y", "v", T.vt[:], T.v[:], [], ["vt"], LOAD + 2.0)
     for i in range(TOP):
-        L, L2 = "L1" if i == 0 else ("La", "Lb")[i % 2], ("La", "Lb")[1 - i % 2]
-        P, P2 = (("PTa", "PTb"), ("PTb", "PTc"), ("PTc", "PTa"))[i % 3]
-        n = "SEL%d" % (i % 3)
-        cut = jump(P2, P, L, SHARE[i + 1])
-        ahead(P, 2 ** i, max(16, 2 ** i), 0)
+        L, L2, sel = "L1" if i == 0 else "LJ%d" % (i % 2), "LJ%d" % (1 - i % 2), "SELJ%d" % (i % 2)
+        P, P2 = "PT%d" % (i % 4), "PT%d" % ((i + 1) % 4)
+        if i == 0:
+            ahead(P, 1, 16, 0)
+        for q, (lo, hi) in zip(JUMP[i], HALVES):
+            gather(q, P2, P, L, lo, hi)
         if i < TOP - 1:
-            keep16(n, P2, 0, cut)
-            keep16(n, P2, cut, C)
-            enlist(L2, n)
-        order_list(2 ** i, max(16, 2 ** i))
-        if i == 4:
-            gather("s", "APS", "IOTA", "lnx1", 0, C)
-        for f in extra.get(i, []):
-            f()
-    far = ("PTa", "PTb", "PTc")[TOP % 3]
-    ahead(far, 128, 128, 0)
-    guests(0, 128)
-    tt(T.dq[:], kept("SELH"), T.jm[:], A.subtract, ["SELH", "jm"], ["dq"])
-    order_list(128, 128)
-    ahead(far, 256, 96, 128)
-    tt(T.m2[:], kept("SELL"), T.dq[:], A.mult, ["SELL", "dq"], ["m2"])
-    guest_list(0, 128)
-    guests(128, 256)
-    tt(T.m3[:], T.m2[:], T.j2[:], A.add, ["m2", "j2"], ["m3"])
-    order_list(256, 96)
-    guests(256, C)
-    ts(T.hq[:], T.m3[:], 1 / E / E, None, A.mult, None, ["m3"], ["hq"])
-    lay("ow")
-    void(0)
-    guest_list(128, C)
-    gather("s", "VBP", "POS", "hq", 0, C)
-    sid(T.m1[:], kept("SELL"), ["SELL"], ["m1"], 0.5, (HALF + 0.125) * E)
-    real(0)
-    void(1)
+            for lo, hi in HALVES:
+                listed(L2, sel, P2, lo, hi)
+        ahead(P2, 2 ** (i + 1), max(16, 2 ** (i + 1)), 0)
+        for at, f in zip(AT, (ucols, first_signs, first_hosts, first_guests, first_leavers)):
+            if at == i:
+                f()
+    m = 2 ** TOP
+    for a in range(2 * m, C, m):
+        ahead("PT%d" % (TOP % 4), a, min(m, C - a), a - m)
+    late(unpack, 1)
+    for lo, hi in TAIL:
+        invert("POS", "ow", lo, hi)
+        guests(lo, hi)
+    gather("s", "VBP", "POS", "hq")
+    for lo, hi in TAIL2:
+        slots(0, lo, hi)
+        slots(1, lo, hi)
     keep16("SELP", "VBP")
-    real(1)
     tt(T.m3[:], kept("SELP"), T.m1[:], A.add, ["SELP", "m1"], ["m3"])
-    keep(0)
-    first_real()
-    ts(T.slw[:], T.m3[:], 2 / E, None, A.mult, None, ["m3"], ["slw"])
-    last_real()
-    keep(1)
+    late(lambda: ts(T.slw[:], T.m3[:], 2 / E, None, A.mult, None, ["m3"], ["slw"]))
     lists(1)
-    keep(2)
-    keep(3, "v")
+    late(quant, "vq", "vqs", 0, 128, T.vt[:], ["vt"])
 
     for k in range(1, ROUNDS + 1):
         last = k == ROUNDS
@@ -477,89 +498,56 @@ def rank_program(g, core, T, topo):
         xq, xs = "xq%d" % (k + 1), "xs%d" % (k + 1)
         zq, zs = "zq%d" % k, "zs%d" % k
 
-        def back(q, out, win, lst, t, lo=0, hi=C):
+        def back(qs, out, win, lst, t, lo=0, hi=C):
             W = C * t
-            (act if q == "s" else vcopy)(T[out][:, W + lo:W + hi], T[win][:, W:W + C].indirect(T[lst][:, W16 + lo // 16:W16 + hi // 16]),
-                                         [(win, W, W + C), (lst, W16, 2 * W16)], [(out, W + lo, W + hi)])
+            off, key = cols(lst, lo, hi, C)
+            pick(qs, T[out][:, W + lo:W + hi], T[win][:, W:W + C].indirect(off), [(win, W, W + C), key], [(out, W + lo, W + hi)])
 
         def mean(out, win, lst, add, t, lo, hi):
             W = C * t
-            tt(T[out][:, 4 * lo + t:4 * hi:4], T[win][:, W:W + C].indirect(T[lst][:, lo // 16:hi // 16]), T[add][:, W + lo:W + hi], A.add,
-               [(win, W, W + C), (lst, 0, W16), (add, W + lo, W + hi)], [(out + "_%d" % t, lo, hi)])
+            off, key = cols(lst, lo, hi)
+            tt(T[out][:, 4 * lo + t:4 * hi:4], T[win][:, W:W + C].indirect(off), T[add][:, W + lo:W + hi], A.add,
+               [(win, W, W + C), key, (add, W + lo, W + hi)], [(out + "_%d" % t, lo, hi)], True)
 
-        def new_order():
-            keep16("SELP", "POS")
-            enlist("p2u", "SELP")
-            own_slots()
-            lay("p2u")
-            keep16("SELO", "OB")
-            enlist("ow", "SELO")
+        def tile(out, win, lst, add, whole, pair, ahead):
+            steps = [(t, 0, C) for t in range(whole)] + [(t, lo, hi) for lo, hi in CH for t in range(whole, 4)]
+            for n, (t, lo, hi) in enumerate(steps):
+                if ahead:
+                    back("s", add, win, lst, t, lo, hi)
+                mean(out, win, lst, add, t, lo, hi)
+                c = {5 - whole + whole: 0, len(steps): 1}.get(n + 1)
+                if c is not None:
+                    lo, hi = CH[c]
+                    quant(*pair, lo, hi, T[out][:, 4 * lo:4 * hi], [(out + "_%d" % t, lo, hi) for t in range(4)])
 
-        if not last:
-            count()
         if not OWN[k]:
             if not last:
-                places()
-            back("v", "TB", "TH", abw, 0)
-            for b in range(4):
-                unpack_far(k, b)
-            if not last:
-                back("s", "TB", "TH", abw, 1)
+                new_places()
                 new_order()
-            else:
-                for t in (1, 2, 3):
-                    back("v", "TB", "TH", abw, t)
-                quant("vq", "vqs", 0, 128, T.vt[:], ["vt"])
-        win, lst, tb = ("TH", abw, "TB") if OWN[k] else ("THP", lab, "TBP")
-        for c, (lo, hi) in enumerate(CH):
+            unpack_far(k)
             for t in range(4):
-                back("s", tb, win, lst, t, lo, hi)
-                mean("Z", win, lst, tb, t, lo, hi)
-            quant(zq, zs, lo, hi, T.Z[:, 4 * lo:4 * hi], [("Z_%d" % t, lo, hi) for t in range(4)])
-            if OWN[k]:
-                ship(k, c, "z%s" + str(k))
+                late(back, "sv", "TB", "TH", abw, t)
         if last:
-            sid(T.nrs[:], T.GA[:], ["GA"], ["nrs"], 1.0, float(HALF))
-            dma("y", "nr", T.nr[:], T.nrs[0:128:16, :], ["nrs"], [])
-            if OWN[k]:
-                quant("vq", "vqs", 0, 128, T.vt[:], ["vt"])
-        elif OWN[k]:
-            places()
-            gather("s", "APS", "IOTA", lnx, 0, C)
-            new_order()
-            gather("s", "VBP", "POS", lnx, 0, C, C)
-            host_slots()
+            late(lambda: line("s", T.nrs[:], T.GA[:], ["GA"], ["nrs"], 1.0, float(HALF)))
+            late(lambda: dma("y", "nr", T.nr[:], T.nrs[0:128:16, :], ["nrs"], []))
+        tile("Z", *(("TH", abw, "TB") if OWN[k] else ("THP", lab, "TBP")), 0, (zq, zs), True)
+        if OWN[k]:
+            for c in (0, 1):
+                ship(k, c, "z%s" + str(k))
+            if not last:
+                new_places()
+                new_order()
         hq, hs = ("lq%d" % k, "ls%d" % k) if OWN[k] else (zq, zs)
         for c, b in HORDER[OWN[k]]:
-            lo, hi = CH[c]
-            P, s = place(c, b)
-            mm(P, s, hi - lo, "wq", "wsq", 128 * b, hq, hs, lo, hi)
-            src, key = bank(P, s, hi - lo)
-            halve("s", T.HH[:, C * b + lo:C * b + hi], src, key, ("HH", C * b + lo, C * b + hi), 2.0 ** -6)
-        if not last and not OWN[k]:
-            for t in (2, 3):
-                back("s", "TB", "TH", abw, t)
-            gather("s", "APS", "IOTA", lnx, 0, C)
-            guests(0, C)
-            gather("s", "VBP", "POS", lnx, 0, C, C)
-        elif not last:
-            guests(0, C)
-        whole = 0 if last else XT
-        for t in range(whole):
-            mean("X1", "HH", abw, "TB", t, 0, C)
+            product(*place(c, b), "wq", "wsq", b, hq, hs, *CH[c], "HH", 2.0 ** -6, "s")
+        if not last:
+            late(new_slots, lnx)
+        tile("X1", "HH", abw, "TB", 0 if last else XT, (xq, xs), False)
         for c, (lo, hi) in enumerate(CH):
-            for t in range(whole, 4):
-                mean("X1", "HH", abw, "TB", t, lo, hi)
-            quant(xq, xs, lo, hi, T.X1[:, 4 * lo:4 * hi], [("X1_%d" % t, lo, hi) for t in range(4)])
             if not last:
                 scores(k + 1, c, lo, hi)
                 if not OWN[k + 1]:
                     ship(k + 1, c, "x%s" + str(k + 1))
-                if c == 1:
-                    unpack(k + 1, 0, 0, C)
-                    guest_list(0, C)
-                    if not OWN[k]:
-                        host_slots()
                 signs("sv"[c], c, lo, hi)
             else:
                 mm("PS", c, hi - lo, "vq", "vqs", 0, xq, xs, lo, hi)
@@ -568,8 +556,8 @@ def rank_program(g, core, T, topo):
                     for i in range(4):
                         dma("y", "osc%d" % i, T.osc[4 * i:4 * i + 4, :], T[xs][32 * i:32 * i + 4, :], [xs], [])
                 src, key = bank("PS", c, hi - lo)
-                act(T.ysb[:, lo:hi], src, [key], [("ysb", lo, hi)])
+                line("s", T.ysb[:, lo:hi], src, [key], [("ysb", lo, hi)], 1.0)
                 dma("ys"[c], "y%d" % c, T.y[:, lo:hi], T.ysb[:, lo:hi], [("ysb", lo, hi)], [])
-    for sem, val in total.items():
-        if know["g"].get(sem, 0) < val:
-            g.wait_ge(T.sem[sem], val)
+        if not last:
+            late(unpack, k + 1)
+    issue()

@@ -4,7 +4,6 @@ C = 352
 CH = [(0, 224), (224, 352)]
 MASKS = [1, 2, 4]
 ROUNDS = 3
-OWN = {1: True, 2: False, 3: False}
 W16 = C // 16
 HALF = C // 2
 MOST = C // 2 + 1
@@ -15,14 +14,29 @@ TOP = 7
 HALVES = [(0, 192), (192, C)]
 TAIL = [(0, 128), (128, 256), (256, C)]
 TAIL2 = [(0, 256), (256, C)]
-LV = [(0, C)]
-AP = "ss"
+LV = [(0, 128), (128, 256), (256, C)]
+BESIDE = [("keep", "u", "hosts us"), ("", "", "uq"), ("", "x1", "x0"), ("", "up1", "up0"), ("sc", "dk", "lv0"), ("lv2", "dq", "lv1")]
+EVEN = "s"
+TINY = 2.0 ** -40
 JUMP = ["ss", "ss", "ss", "ss", "ss", "ss", "ss"]
-AT = [1, 2, 2, 4, 4]
-GV = 256
+AT = [1, 2, 2, 4, 7, 6]
+EARLY = 256
+FIRST = [(0, C)]
+SPLICE = "st void bits odd m2 even m3 last first slot before behind"
+SPLICE1 = ("gone on1 guest pos0 keep1 bits list1 st on2 pos1 keep2 m2 odd0s stay list2 own even0s pos2 host m1 "
+           "at0s at1s odd1v even1v void0 void1 first last place m3 before slot behind")
+US = "v"
+GQ = {1: "vs", 3: "vs"}
+SC = "v"
+PARTS = {1: CH, 2: [(0, C)], 3: [(0, 160), (160, C)]}
+ZR = {1: [(0, 224, True), (224, C, True)], 2: [(0, 224, False), (224, C, False)], 3: [(0, 160, True), (160, C, False)]}
+GV = {1: 256, 2: 256, 3: 256}
 XT = 2
-HORDER = {True: [(0, 0), (0, 1), (1, 0), (0, 2), (1, 1), (0, 3), (1, 2), (1, 3)],
-          False: [(0, 0), (0, 1), (0, 2), (1, 0), (1, 1), (0, 3), (1, 2), (1, 3)]}
+HORDER = {1: [(0, 0), (0, 1), (1, 0), (0, 2), (1, 1), (0, 3), (1, 2), (1, 3)],
+          2: [(0, 0), (0, 1), (0, 2), (1, 0), (1, 1), (0, 3), (1, 2), (1, 3)],
+          3: [(1, 0), (1, 1), (0, 0), (1, 2), (0, 1), (1, 3), (0, 2), (0, 3)]}
+XL = 0
+AFTER = [(), (), (), ()]
 F8 = "float8_e4m3fn_x4"
 CYCLE, WAKE, FLIGHT, LOAD, SPARE = 0.00092, 0.14, 2.2, 2.0, 0.25
 SLACK = 0.03
@@ -48,7 +62,7 @@ for _n in ("X0", "X1", "TH", "THP", "TB", "TBP", "Z", "HH"):
 for _n in ("ONES", "D0", "D1", "CNT"):
     SCRATCH[_n] = ("sbuf", [128, 2 * C], "bfloat16")
 for _n in ("IOTA", "DG", "OB", "GU", "SELO", "SELA", "SELP", "SELH", "SELL", "SELB", "SELC", "SELJ0", "SELJ1",
-           "POS", "BPS", "APS", "VBP", "GA", "GB", "sc", "up", "lv", "st", "PT0", "PT1", "PT2", "PT3"):
+           "POS", "BPS", "APS", "VBP", "GA", "GB", "sc", "up", "lv", "st", "IT", "WL", "WN", "PT0", "PT1", "PT2", "PT3"):
     SCRATCH[_n] = ("sbuf", [128, C], "bfloat16")
 for _n in ("ysb", "nrs"):
     SCRATCH[_n] = ("sbuf", [128, C], "float32")
@@ -60,14 +74,17 @@ for _k in range(1, ROUNDS + 2):
     SCRATCH["xq%d" % _k] = ("sbuf", [128, C], F8)
     SCRATCH["xs%d" % _k] = ("sbuf", [128, C], "uint8")
 for _k in range(1, ROUNDS + 1):
-    for _n in "lz":
+    for _n in "lz" if _k > 1 else "z":
         SCRATCH[_n + "q%d" % _k] = ("sbuf", [128, C], F8)
         SCRATCH[_n + "s%d" % _k] = ("sbuf", [128, C], "uint8")
+    SCRATCH["mq%d" % _k] = ("sbuf", [128, C], F8)
+    SCRATCH["ms%d" % _k] = ("sbuf", [128, C], "uint8")
     for _n in ("abw", "lab", "lnx"):
         SCRATCH[_n + str(_k)] = ("sbuf", [128, 2 * W16], "uint16")
 
 LOCAL = ["nx", "x", "u", "ws", "wc", "v", "y0", "y1", "nr", "oc0", "oc1", "osc0", "osc1", "osc2", "osc3"]
-REMOTE = ["nb1", "nx1", "nx2", "nx3", "ab1", "ab2", "ab3"] + [n + str(k) + str(c) for k in (1, 2, 3) for n in "qs" for c in (0, 1)]
+REMOTE = ["nb1", "nx1", "nx2", "nx3", "ab1", "ab2", "ab3"] + [
+    w + n + str(k) + str(c) for k in (1, 2, 3) for w in "xz" for n in "qs" for c in (0, 1)]
 SEMAPHORES = ["cv", "cs", "ct", "cg"] + ["d_" + n for n in LOCAL] + ["r_" + n for n in REMOTE] + ["l_" + n for n in REMOTE]
 
 
@@ -228,9 +245,12 @@ def rank_program(g, core, T, topo):
               "v": (lambda: V.tensor_scalar(out, in_, scale, bias, A.mult, A.add), plain(n, rate))}
         call({q: on[q] for q in qs}, rd, wr)
 
-    def pick(qs, out, win, rd, wr):
+    def pick(qs, out, win, rd, wr, scale=None):
         n = out.shape[1]
         on = {"s": (lambda: S.activation(out, win, AF.Copy), picked(n) + 0.015), "v": (lambda: V.tensor_copy(out, win), picked(n))}
+        if scale:
+            on = {"s": (lambda: S.activation(out, win, AF.Copy, scale=scale), picked(n) + 0.015),
+                  "v": (lambda: V.tensor_scalar(out, win, scale, None, A.mult), picked(n))}
         call({q: on[q] for q in qs}, rd, wr)
 
     def quant(codes, plane, lo, hi, src, rd):
@@ -277,52 +297,50 @@ def rank_program(g, core, T, topo):
     dma("y", "u", T.ut[:], T.u[:], [], ["ut"], LOAD + 0.6)
     dma("y", "x", T.X0[:], T.x[:], [], ["X0"], LOAD + 2.0)
 
-    def iota(name, pattern):
-        pool(lambda: g.iota(T[name][:], pattern, 0, 0, allow_small_or_imprecise_dtypes=True), pattern[0][1], [], [name])
-
     pool(lambda: g.iota(T.pi[:], [[0, 1]], 0, 1), 1, [], ["pi"])
-    iota("J16", [[1, 16]])
     fill(T.ONES[:], 1.0, ["ONES"])
     pool(lambda: g.affine_select(T.EB[:], T.ONES[:, 0:516], [[1, 516]], A.is_equal, 0.0, -4, -4), 516, ["ONES"], ["EB"])
-    iota("C16", [[16, W16]])
+    vcopy(T.L1[:], T.nxi[:], ["nxi"], ["L1"])
+    send("nx1", partner[0], T.lnx1[:, 0:W16], T.L1[:], "L1", ("lnx1", 0, W16), 2 * W16)
     ts(T.pj[:], T.pi[:], 15, None, A.bitwise_and, None, ["pi"], ["pj"])
     scan(T.IOTA[:], T.ONES[:, 0:C], T.ONES[:, 0:C], -HALF - 1.0, A.mult, A.add, ["ONES"], ["IOTA"])
     vcopy(T.p16[:], T.pj[:], ["pj"], ["p16"])
-    fill(T.ow[:], 0, ["ow"])
-    ts(T.DA[:], T.J16[:], T.p16[:, 0:1], None, A.is_gt, None, ["J16", "p16"], ["DA"])
-    ts(T.DB[:], T.J16[:], T.p16[:, 0:1], 1 / E, A.is_equal, A.mult, ["J16", "p16"], ["DB"])
+    J16 = T.IOTA[:, HALF:HALF + 16]
+    ts(T.DA[:], J16, T.p16[:, 0:1], None, A.is_gt, None, ["IOTA", "p16"], ["DA"])
+    ts(T.DB[:], J16, T.p16[:, 0:1], 1 / E, A.is_equal, A.mult, ["IOTA", "p16"], ["DB"])
     ts(T.lp[:], T.ONES[:, 0:W16], T.p16[:, 0:1], None, A.mult, None, ["ONES", "p16"], ["lp"])
     tt(T.D16[:], T.DA[:], T.DB[:], A.add, ["DA", "DB"], ["D16"])
-    fill(T.OB[:, 0:1], -float(HALF), [("OB", 0, 1)])
     ts(T.D16[:, 15:16], T.D16[:, 15:16], E * E, None, A.mult, None, ["D16"], ["D16"])
     gather("s", "DG", "D16", "lp")
     for b in range(4):
         late(quant, "eq", "eqs", 128 * b, 128 * b + 128, T.EB[:, 4 - b:516 - b], ["EB"])
-    vcopy(T.L1[:], T.nxi[:], ["nxi"], ["L1"])
-    send("nx1", partner[0], T.lnx1[:, 0:W16], T.L1[:], "L1", ("lnx1", 0, W16), 2 * W16)
-    late(lambda: vcopy(T.l16[:], T.C16[:], ["C16"], ["l16"]))
-    late(lambda: line("s", T.jw[:], T.C16[:], ["C16", "p16"], ["jw"], 1.0, T.p16[:, 0:1]))
-    late(lambda: line("sv", T.jm[:], T.jw[:], ["jw"], ["jm"], E, -HALF * E))
-    late(lambda: line("sv", T.j2[:], T.jw[:], ["jw"], ["j2"], E * E, 0.25 * E * E))
+    fill(T.ow[:], 0, ["ow"])
+    fill(T.OB[:, 0:1], -float(HALF), [("OB", 0, 1)])
+    line("s", T.IT[:], T.IOTA[:], ["IOTA"], ["IT"], TINY)
+    fill(T.IT[:, HALF:HALF + 1], TINY / 64, ["IT"])
+    ts(T.l16[:], T.IOTA[:, 0:C:16], float(HALF), None, A.add, None, ["IOTA"], ["l16"])
+    line("s", T.jw[:], T.IOTA[:, 0:C:16], ["IOTA", "p16"], ["jw"], 1.0, T.p16[:, 0:1])
+    line("s", T.jm[:], T.jw[:], ["jw"], ["jm"], E)
+    line("s", T.j2[:], T.jw[:], ["jw"], ["j2"], E * E, (HALF + 0.25) * E * E)
 
     def ucols():
         quant("uq", "uqs", 0, 128, T.ut[:], ["ut"])
-        pick("v", T.up16s[:, 0:128], T.uqs[:, 0:128].indirect(T.l16[:, 0:8]), ["uqs", "l16"], ["up16s"])
+        pick(US, T.up16s[:, 0:128], T.uqs[:, 0:128].indirect(T.l16[:, 0:8]), ["uqs", "l16"], ["up16s"])
         pick("v", T.up16[:, 0:128].bitcast(dt.uint32), T.uq[:, 0:128].bitcast(dt.uint32).indirect(T.l16[:, 0:8]), ["uq", "l16"], ["up16"])
 
     def scores(k, c, lo, hi):
         mm("PS", c, hi - lo, "up16", "up16s", 0, "xq%d" % k, "xs%d" % k, lo, hi)
 
-    def ship(k, c, n):
-        p, (lo, hi) = partner[k - 1], CH[c]
-        lq, ls = "lq%d" % k, "ls%d" % k
-        send("q%d%d" % (k, c), p, T[lq][:, lo:hi].bitcast(dt.uint8), T[n % "q"][:, lo:hi].bitcast(dt.uint8), (n % "q", lo, hi),
+    def ship(k, c, w, lo, hi):
+        p, land = partner[k - 1], {"x": "l", "z": "m"}[w]
+        q, s, lq, ls = w + "q%d" % k, w + "s%d" % k, land + "q%d" % k, land + "s%d" % k
+        send(w + "q%d%d" % (k, c), p, T[lq][:, lo:hi].bitcast(dt.uint8), T[q][:, lo:hi].bitcast(dt.uint8), (q, lo, hi),
              (lq, lo, hi), 4 * (hi - lo))
-        if not OWN[k]:
+        if w == "x":
             if c == 0:
                 return
             lo = 0
-        send("s%d%d" % (k, c), p, T[ls][:, lo:hi], T[n % "s"][:, lo:hi], (n % "s", lo, hi), (ls, lo, hi), 5 * (hi - lo))
+        send(w + "s%d%d" % (k, c), p, T[ls][:, lo:hi], T[s][:, lo:hi], (s, lo, hi), (ls, lo, hi), 5 * (hi - lo))
 
     def signs(q, c, lo, hi):
         src, key = bank("PS", c, hi - lo)
@@ -345,23 +363,25 @@ def rank_program(g, core, T, topo):
         for b in range(4):
             product("PA", b, "eq", "eqs", b, "xq%d" % k, "xs%d" % k, 0, C, "TH", 0.5)
 
-    def unpack_far(k):
-        for b in range(4):
-            product("PB", b % 2, "eq", "eqs", b, "lq%d" % k, "ls%d" % k, 0, C, "THP", 0.5)
+    def unpack_far(k, bs=range(4), qs="sv"):
+        for b in bs:
+            product("PA", b, "eq", "eqs", b, "lq%d" % k, "ls%d" % k, 0, C, "THP", 0.5, qs)
 
-    def leavers(lst, runs=((0, C),)):
+    def leavers(lst, runs):
         for lo, hi in runs:
             off, key = cols(lst, lo, hi, C)
             tt(T.lv[:, lo:hi], T.up[:].indirect(off), T.sc[:, lo:hi], A.is_lt, ["up", ("sc", lo, hi), key], [("lv", lo, hi)], True)
-        line("v", T.st[:], T.lv[:], ["lv"], ["st"], -1.0, 1.0, 0.5)
-        keep16("SELL", "lv")
 
-    def slots(odd, lo=0, hi=C):
-        off, key = cols("aw" if odd else "ow", lo, hi)
-        gone, there, who = ("st", "lv", "GU") if odd else ("lv", "st", "OB")
-        pick("s", T.D0[:, 2 * lo + odd:2 * hi:2], T[gone][:].indirect(off), [gone, key], [("D0%d" % odd, lo, hi)])
-        tt(T.D1[:, 2 * lo + odd:2 * hi:2], T[there][:].indirect(off), T[who][:, lo:hi], A.mult,
-           [there, key, (who, lo, hi)], [("D1%d" % odd, lo, hi)], True)
+    def stayers():
+        line("v", T.st[:], T.lv[:], ["lv"], ["st"], -1.0, 1.0, 0.5)
+
+    def void(odd):
+        lst, flag = (("ow", "lv"), ("aw", "st"))[odd]
+        pick("s", T.D0[:, odd:2 * C:2], T[flag][:].indirect(T[lst][:]), [flag, lst], ["D0%d" % odd])
+
+    def there(odd):
+        lst, flag, who = (("ow", "st", "OB"), ("aw", "lv", "GU"))[odd]
+        tt(T.D1[:, odd:2 * C:2], T[flag][:].indirect(T[lst][:]), T[who][:], A.mult, [flag, lst, who], ["D1%d" % odd], True)
 
     def keys(odds, lo=0, hi=C):
         return [("D%d%d" % (d, o), lo, hi) for d in (0, 1) for o in odds]
@@ -371,44 +391,77 @@ def rank_program(g, core, T, topo):
         off, key = cols("slw", lo, hi)
         pick(q, T[out][:, lo:hi], T[win][:, a:a + 2 * C].indirect(off), [(win, a, a + 2 * C), key], [(out, lo, hi)])
 
-    def lists(k):
-        abw, r, a = "abw%d" % k, RB + 2 * C - 1, 2 * (C - MOST)
+    def far(k):
+        return [lo for lo, hi, own in ZR[k] if not own]
+
+    def first_there():
+        r = RB + 2 * C - 1
         scan(T.RS[:, r + MOST - 1:r - 1:-1], T.D0[:, 2 * MOST - 2::-2], T.D1[:, 2 * MOST - 2::-2], 0.0, A.mult, A.add,
              keys([0], 0, MOST), [("RS", r, r + MOST)])
+
+    def last_there():
+        a = 2 * (C - MOST)
         scan(T.FS[:, FB + 1 - 2 * MOST:FB + 1], T.D0[:, a:2 * C], T.D1[:, a:2 * C], 0.0, A.mult, A.add,
              keys([0, 1], C - MOST, C), [("FS", 0, FB + 1)])
+
+    def before():
         scan(T.FS[:, FB + 1:FB + 1 + 2 * C], T.D0[:], T.D1[:], T.FS[:, FB:FB + 1], A.mult, A.add,
              keys([0, 1]) + [("FS", FB, FB + 1)], [("FS", FB + 1, FB + 1 + 2 * C)])
+
+    def behind():
+        r = RB + 2 * C - 1
         scan(T.RS[:, r - 1:RB - 2:-1], T.D0[:, ::-1], T.D1[:, ::-1], T.RS[:, r:r + 1], A.mult, A.add,
              keys([0, 1]) + [("RS", r, r + 1)], [("RS", 0, r)])
-        neighbours("s", "GB", 0, C)
-        neighbours("v", "GA", 0, GV)
-        neighbours("s", "GA", GV, C)
-        keep16("SELB", "GB")
-        keep16("SELC", "GA")
-        enlist(abw, "SELC")
-        enlist(abw, "SELB", 0, C, C)
-        if not OWN[k]:
-            send("ab%d" % k, partner[k - 1], T["lab%d" % k][:], T[abw][:], abw, "lab%d" % k, 4 * W16)
+
+    def in_turn(*steps):
+        turn = {}
+        for f in steps:
+            n = len(calls)
+            f()
+            for c in range(n, len(calls)):
+                q = "".join(map(str, calls[c]["on"]))
+                if q in ("v", "s"):
+                    calls[c]["behind"] |= {turn[q]} if q in turn else set()
+                    turn[q] = c
+
+    def lists(k):
+        abw = "abw%d" % k
+        for lo, hi in PARTS[k]:
+            neighbours("s", "GB", lo, hi)
+            if hi - lo == C:
+                neighbours("v", "GA", 0, GV[k])
+                neighbours("s", "GA", GV[k], C)
+            else:
+                neighbours(GQ[k][lo > 0], "GA", lo, hi)
+            keep16("SELB", "GB", lo, hi)
+            keep16("SELC", "GA", lo, hi)
+            enlist(abw, "SELC", lo, hi)
+            enlist(abw, "SELB", lo, hi, C)
+        if far(k):
+            n = far(k)[0] // 16
+            send("ab%d" % k, partner[k - 1], T["lab%d" % k][:, n:], T[abw][:, n:], abw, "lab%d" % k, 4 * W16 - 2 * n)
         if k < ROUNDS:
             send("nx%d" % (k + 1), partner[k], T["lnx%d" % (k + 1)][:], T[abw][:], abw, "lnx%d" % (k + 1), 4 * W16)
 
     def splice(k):
-        leavers("lnx%d" % k)
-        slots(0)
-        tt(T.m2[:], kept("SELL"), T.dk[:], A.mult, ["SELL", "dk"], ["m2"])
-        slots(1)
-        tt(T.m3[:], T.m2[:], T.pw[:], A.add, ["m2", "pw"], ["m3"])
-        late(lambda: ts(T.slw[:], T.m3[:], 1 / E / E, None, A.mult, None, ["m3"], ["slw"]))
+        leavers("lnx%d" % k, CH)
+        void(0)
+        step = {"st": stayers, "bits": lambda: keep16("SELL", "lv"), "even": lambda: there(0), "odd": lambda: there(1),
+                "void": lambda: void(1),
+                "m2": lambda: tt(T.m2[:], kept("SELL"), T.dk[:], A.mult, ["SELL", "dk"], ["m2"]),
+                "m3": lambda: tt(T.m3[:], T.m2[:], T.pw[:], A.add, ["m2", "pw"], ["m3"]),
+                "slot": lambda: ts(T.slw[:], T.m3[:], 1 / E / E, None, A.mult, None, ["m3"], ["slw"]),
+                "first": first_there, "last": last_there, "before": before, "behind": behind}
+        in_turn(*[step[n] for n in SPLICE.split()])
         lists(k)
 
     def guests(lo=0, hi=C):
         gather("s", "GU", "APS", "ow", lo, hi)
         listed("aw", "SELA", "GU", lo, hi)
 
-    def new_places():
+    def new_places(q="s"):
         scan(T.CNT[:], T.ONES[:], T.D0[:], -HALF - 1.0, A.add, A.subtract, ["ONES", "D00", "D01"], ["CNT"])
-        gather("s", "POS", "CNT", "slw")
+        gather(q, "POS", "CNT", "slw")
 
     def new_order():
         listed("p2u", "SELP", "POS")
@@ -425,20 +478,41 @@ def rank_program(g, core, T, topo):
         line("s", T.dk[:], T.dq[:], ["dq"], ["dk"], 2.0, E)
 
     def first_signs():
-        quant("xq1", "xs1", 0, C, T.X0[:], ["X0"])
-        scores(1, 0, 0, C)
+        for c, (lo, hi) in enumerate(FIRST):
+            quant("xq1", "xs1", lo, hi, T.X0[:, 4 * lo:4 * hi], ["X0"])
+            scores(1, c, lo, hi)
 
     def first_hosts():
-        src, key = bank("PS", 0, C)
-        ts(T.up[:], src, 0.0, None, A.is_gt, None, [key], ["up"])
-        vcopy(T.sc[:], T.up[:], ["up"], ["sc"], 0.5)
+        for c, (lo, hi) in enumerate(FIRST):
+            src, key = bank("PS", c, hi - lo)
+            ts(T.up[:, lo:hi], src, 0.0, None, A.is_gt, None, [key], [("up", lo, hi)])
+        if SC == "g":
+            pool(lambda: g.affine_select(T.sc[:], T.up[:], [[0, C]], A.is_ge, 0.0, 0, 0), C, ["up"], ["sc"])
+        else:
+            vcopy(T.sc[:], T.up[:], ["up"], ["sc"], 0.5)
+
+    def flagged(out, flag):
+        scan(T[out][:], T[flag][:], T.IT[:], 0.0, A.max, A.mult, [flag, "IT"], [out])
 
     def first_guests():
-        for q, (lo, hi) in zip(AP, HALVES):
-            gather(q, "APS", "IOTA", "lnx1", lo, hi)
+        flagged("WL", "lv")
+        off, key = cols("lnx1", 0, C)
+        pick("s", T.GU[:], T.WL[:].indirect(off), ["WL", key], ["GU"], 1 / TINY)
+
+    def first_slots(lo, hi):
+        off, key = cols("ow", lo, hi)
+        pick(EVEN, T.D1[:, 2 * lo:2 * hi:2], T.WN[:].indirect(off), ["WN", key], [("D10", lo, hi)], 1 / TINY)
+        pick("s", T.D1[:, 2 * lo + 1:2 * hi:2], T.GU[:].indirect(off), ["GU", key], [("D11", lo, hi)])
+        ts(T.D0[:, 2 * lo:2 * hi], T.D1[:, 2 * lo:2 * hi], 2.0 ** 16, 2.0 ** 16, A.add, A.is_equal,
+           [("D10", lo, hi), ("D11", lo, hi)], [("D00", lo, hi), ("D01", lo, hi)], 0.5)
 
     def first_leavers():
         leavers("lnx1", LV)
+
+    def first_lists():
+        stayers()
+        keep16("SELL", "lv")
+        flagged("WN", "st")
         ts(T.dk[:], T.lnx1[:, W16:2 * W16], E, -HALF * E, A.mult, A.add, ["lnx1"], ["dk"])
         tt(T.dq[:], T.dk[:], T.jm[:], A.subtract, ["dk", "jm"], ["dq"])
         tt(T.m2[:], kept("SELL"), T.dq[:], A.mult, ["SELL", "dq"], ["m2"])
@@ -454,11 +528,33 @@ def rank_program(g, core, T, topo):
 
     gather("s", "PT0", "IOTA", "L1")
     invert("BPS", "L1")
-    late(listed, "LB", "SELH", "BPS")
-    late(send, "nb1", partner[0], T.lnx1[:, W16:2 * W16], T.LB[:], "LB", ("lnx1", W16, 2 * W16), 2 * W16)
-    late(dma, "y", "ws", T.wsq[:], T.ws[:], ["lnx1"], ["wsq"])
-    late(dma, "y", "wc", T.wq[:].bitcast(dt.uint8), T.wc[:], [], ["wq"], LOAD + 1.5)
-    late(dma, "y", "v", T.vt[:], T.v[:], [], ["vt"], LOAD + 2.0)
+
+    def hosts():
+        enlist("LB", "SELH")
+        send("nb1", partner[0], T.lnx1[:, W16:2 * W16], T.LB[:], "LB", ("lnx1", W16, 2 * W16), 2 * W16)
+        late(dma, "y", "ws", T.wsq[:], T.ws[:], ["lnx1"], ["wsq"])
+        late(dma, "y", "wc", T.wq[:].bitcast(dt.uint8), T.wc[:], [], ["wq"], LOAD + 1.5)
+        late(dma, "y", "v", T.vt[:], T.v[:], [], ["vt"], LOAD + 2.0)
+
+    def xrun(c):
+        lo, hi = CH[c]
+        quant("xq1", "xs1", lo, hi, T.X0[:, 4 * lo:4 * hi], ["X0"])
+        scores(1, c, lo, hi)
+
+    def ups(c):
+        lo, hi = CH[c]
+        src, key = bank("PS", c, hi - lo)
+        ts(T.up[:, lo:hi], src, 0.0, None, A.is_gt, None, [key], [("up", lo, hi)])
+
+    beside = {"keep": lambda: keep16("SELH", "BPS"), "hosts": hosts, "u": lambda: quant("uq", "uqs", 0, 128, T.ut[:], ["ut"]),
+              "us": lambda: pick("v", T.up16s[:, 0:128], T.uqs[:, 0:128].indirect(T.l16[:, 0:8]), ["uqs", "l16"], ["up16s"]),
+              "uq": lambda: pick("v", T.up16[:, 0:128].bitcast(dt.uint32), T.uq[:, 0:128].bitcast(dt.uint32).indirect(T.l16[:, 0:8]),
+                                 ["uq", "l16"], ["up16"]),
+              "x0": lambda: xrun(0), "x1": lambda: xrun(1), "up0": lambda: ups(0), "up1": lambda: ups(1),
+              "dk": lambda: ts(T.dk[:], T.lnx1[:, W16:2 * W16], E, -HALF * E, A.mult, A.add, ["lnx1"], ["dk"]),
+              "dq": lambda: tt(T.dq[:], T.dk[:], T.jm[:], A.subtract, ["dk", "jm"], ["dq"]),
+              "sc": lambda: vcopy(T.sc[:], T.up[:], ["up"], ["sc"], 0.5),
+              "lv0": lambda: leavers("lnx1", LV[0:1]), "lv1": lambda: leavers("lnx1", LV[1:2]), "lv2": lambda: leavers("lnx1", LV[2:3])}
     for i in range(TOP):
         L, L2, sel = "L1" if i == 0 else "LJ%d" % (i % 2), "LJ%d" % (1 - i % 2), "SELJ%d" % (i % 2)
         P, P2 = "PT%d" % (i % 4), "PT%d" % ((i + 1) % 4)
@@ -466,29 +562,55 @@ def rank_program(g, core, T, topo):
             ahead(P, 1, 16, 0)
         for q, (lo, hi) in zip(JUMP[i], HALVES):
             gather(q, P2, P, L, lo, hi)
+        n = 2 ** (i + 1)
         if i < TOP - 1:
-            for lo, hi in HALVES:
-                listed(L2, sel, P2, lo, hi)
-        ahead(P2, 2 ** (i + 1), max(16, 2 ** (i + 1)), 0)
-        for at, f in zip(AT, (ucols, first_signs, first_hosts, first_guests, first_leavers)):
-            if at == i:
-                f()
-    m = 2 ** TOP
-    for a in range(2 * m, C, m):
-        ahead("PT%d" % (TOP % 4), a, min(m, C - a), a - m)
+            one, two, three = [[beside[w] for w in ws.split()] for ws in BESIDE[i]]
+            b = 0 if n < 16 else n
+            off, key = cols("ow", 0, max(16, n))
+            pick("s", T.OB[:, n:n + max(16, n)], T[P2][:].indirect(off), [P2, key], [("OB", n, n + max(16, n))])
+            in_turn(lambda: keep16(sel, P2, *HALVES[0]), *one, lambda: enlist(L2, sel, *HALVES[0]),
+                    lambda: keep16(sel, P2, *HALVES[1]), *two, lambda: enlist(L2, sel, *HALVES[1]),
+                    lambda: keep16("SELO", "OB", b, b + max(16, n)), *three, lambda: enlist("ow", "SELO", b, b + max(16, n)))
     late(unpack, 1)
-    for lo, hi in TAIL:
-        invert("POS", "ow", lo, hi)
-        guests(lo, hi)
-    gather("s", "VBP", "POS", "hq")
-    for lo, hi in TAIL2:
-        slots(0, lo, hi)
-        slots(1, lo, hi)
-    keep16("SELP", "VBP")
-    tt(T.m3[:], kept("SELP"), T.m1[:], A.add, ["SELP", "m1"], ["m3"])
-    late(lambda: ts(T.slw[:], T.m3[:], 2 / E, None, A.mult, None, ["m3"], ["slw"]))
+
+    def onward(c):
+        lo, hi = TAIL[c]
+        off, key = cols("ow", lo - 2 ** TOP, hi - 2 ** TOP)
+        pick("s", T.OB[:, lo:hi], T["PT%d" % (TOP % 4)][:].indirect(off), ["PT%d" % (TOP % 4), key], [("OB", lo, hi)])
+
+    def names(q, odd, lo, hi):
+        off, key = cols("ow", lo, hi)
+        win = "GU" if odd else "WN"
+        pick(q, T.D1[:, 2 * lo + odd:2 * hi:2], T[win][:].indirect(off), [win, key], [("D1%d" % odd, lo, hi)], None if odd else 1 / TINY)
+
+    def voids(lo, hi):
+        ts(T.D0[:, 2 * lo:2 * hi], T.D1[:, 2 * lo:2 * hi], 2.0 ** 16, 2.0 ** 16, A.add, A.is_equal,
+           [("D10", lo, hi), ("D11", lo, hi)], [("D00", lo, hi), ("D01", lo, hi)], 0.5)
+
+    step = {"gone": lambda: flagged("WL", "lv"), "st": stayers, "stay": lambda: flagged("WN", "st"), "bits": lambda: keep16("SELL", "lv"),
+            "guest": lambda: pick("s", T.GU[:], T.WL[:].indirect(T.lnx1[:, 0:W16]), ["WL", ("lnx1", 0, W16)], ["GU"], 1 / TINY),
+            "m2": lambda: tt(T.m2[:], kept("SELL"), T.dq[:], A.mult, ["SELL", "dq"], ["m2"]),
+            "own": lambda: tt(T.m3[:], T.m2[:], T.j2[:], A.add, ["m2", "j2"], ["m3"]),
+            "host": lambda: ts(T.hq[:], T.m3[:], 1 / E / E, None, A.mult, None, ["m3"], ["hq"]),
+            "m1": lambda: late(line, "sv", T.m1[:], kept("SELL"), ["SELL"], ["m1"], 0.5, (HALF + 0.125) * E),
+            "place": lambda: keep16("SELP", "VBP"),
+            "m3": lambda: tt(T.m3[:], kept("SELP"), T.m1[:], A.add, ["SELP", "m1"], ["m3"]),
+            "slot": lambda: ts(T.slw[:], T.m3[:], 2 / E, None, A.mult, None, ["m3"], ["slw"]),
+            "first": first_there, "last": last_there, "before": before, "behind": behind}
+    for c, run in enumerate(TAIL):
+        step["on%d" % c] = lambda c=c: onward(c)
+        step["keep%d" % c] = lambda run=run: keep16("SELO", "OB", *run)
+        step["list%d" % c] = lambda run=run: enlist("ow", "SELO", *run)
+        step["pos%d" % c] = lambda run=run: invert("POS", "ow", *run)
+    for c, run in enumerate(TAIL2):
+        step["void%d" % c] = lambda run=run: voids(*run)
+        for q in "sv":
+            step["even%d" % c + q] = lambda run=run, q=q: names(q, 0, *run)
+            step["odd%d" % c + q] = lambda run=run, q=q: names(q, 1, *run)
+            step["at%d" % c + q] = lambda c=c, q=q: gather(q, "VBP", "POS", "hq", *HALVES[c])
+    in_turn(*[step[n] for n in SPLICE1.split()])
     lists(1)
-    late(quant, "vq", "vqs", 0, 128, T.vt[:], ["vt"])
+    late(quant, "vq", "vqs", 0, 128, T.vt[:], ["vt", "abw1"])
 
     for k in range(1, ROUNDS + 1):
         last = k == ROUNDS
@@ -498,10 +620,10 @@ def rank_program(g, core, T, topo):
         xq, xs = "xq%d" % (k + 1), "xs%d" % (k + 1)
         zq, zs = "zq%d" % k, "zs%d" % k
 
-        def back(qs, out, win, lst, t, lo=0, hi=C):
+        def back(qs, out, win, lst, t, lo=0, hi=C, behind=()):
             W = C * t
             off, key = cols(lst, lo, hi, C)
-            pick(qs, T[out][:, W + lo:W + hi], T[win][:, W:W + C].indirect(off), [(win, W, W + C), key], [(out, W + lo, W + hi)])
+            pick(qs, T[out][:, W + lo:W + hi], T[win][:, W:W + C].indirect(off), [(win, W, W + C), key] + list(behind), [(out, W + lo, W + hi)])
 
         def mean(out, win, lst, add, t, lo, hi):
             W = C * t
@@ -509,45 +631,53 @@ def rank_program(g, core, T, topo):
             tt(T[out][:, 4 * lo + t:4 * hi:4], T[win][:, W:W + C].indirect(off), T[add][:, W + lo:W + hi], A.add,
                [(win, W, W + C), key, (add, W + lo, W + hi)], [(out + "_%d" % t, lo, hi)], True)
 
-        def tile(out, win, lst, add, whole, pair, ahead):
-            steps = [(t, 0, C) for t in range(whole)] + [(t, lo, hi) for lo, hi in CH for t in range(whole, 4)]
-            for n, (t, lo, hi) in enumerate(steps):
+        def tile(out, runs, whole, pair, ahead):
+            steps = [(t, 0, C) + runs[0][2:] for t in range(whole)] + [(t,) + run for run in runs for t in range(whole, 4)]
+            apart = len(runs) == 2 and runs[0][2] != runs[1][2]
+            for n, (t, lo, hi, win, lst, add) in enumerate(steps):
                 if ahead:
                     back("s", add, win, lst, t, lo, hi)
                 mean(out, win, lst, add, t, lo, hi)
-                c = {5 - whole + whole: 0, len(steps): 1}.get(n + 1)
+                c = {4 if apart or whole == 3 else 5: 0, len(steps): 1}.get(n + 1)
                 if c is not None:
-                    lo, hi = CH[c]
+                    lo, hi = runs[c][:2]
                     quant(*pair, lo, hi, T[out][:, 4 * lo:4 * hi], [(out + "_%d" % t, lo, hi) for t in range(4)])
+                    if ahead and win == "TH":
+                        ship(k, c, "z", lo, hi)
+                    if apart and c == 0:
+                        unpack_far(k)
 
-        if not OWN[k]:
+        if far(k):
             if not last:
-                new_places()
+                new_places("v")
                 new_order()
-            unpack_far(k)
-            for t in range(4):
+                for t in (0, 1):
+                    back("s", "TB", "TH", abw, t)
+                unpack_far(k, range(4), "s")
+            elif far(k)[0] == 0:
+                unpack_far(k)
+            for t in range(4 if last else 2, 4):
                 late(back, "sv", "TB", "TH", abw, t)
+        tile("Z", [(lo, hi) + (("TH", abw, "TB") if own else ("THP", lab, "TBP")) for lo, hi, own in ZR[k]], 0, (zq, zs), True)
         if last:
+            for t in range(4):
+                late(back, "sv", "TB", "TH", abw, t, far(k)[0], C, AFTER[t])
             late(lambda: line("s", T.nrs[:], T.GA[:], ["GA"], ["nrs"], 1.0, float(HALF)))
-            late(lambda: dma("y", "nr", T.nr[:], T.nrs[0:128:16, :], ["nrs"], []))
-        tile("Z", *(("TH", abw, "TB") if OWN[k] else ("THP", lab, "TBP")), 0, (zq, zs), True)
-        if OWN[k]:
-            for c in (0, 1):
-                ship(k, c, "z%s" + str(k))
-            if not last:
-                new_places()
-                new_order()
-        hq, hs = ("lq%d" % k, "ls%d" % k) if OWN[k] else (zq, zs)
-        for c, b in HORDER[OWN[k]]:
-            product(*place(c, b), "wq", "wsq", b, hq, hs, *CH[c], "HH", 2.0 ** -6, "s")
+            late(lambda: dma("y", "nr", T.nr[:], T.nrs[0:128:16, :], ["nrs", "ms%d" % k], []))
+        if not far(k) and not last:
+            new_places()
+            new_order()
+        for c, b in HORDER[k]:
+            lo, hi, own = ZR[k][c]
+            product(*place(c, b), "wq", "wsq", b, *(("mq%d" % k, "ms%d" % k) if own else (zq, zs)), lo, hi, "HH", 2.0 ** -6, "s")
         if not last:
             late(new_slots, lnx)
-        tile("X1", "HH", abw, "TB", 0 if last else XT, (xq, xs), False)
+        tile("X1", [run + ("HH", abw, "TB") for run in CH], XL if last else XT, (xq, xs), False)
         for c, (lo, hi) in enumerate(CH):
             if not last:
                 scores(k + 1, c, lo, hi)
-                if not OWN[k + 1]:
-                    ship(k + 1, c, "x%s" + str(k + 1))
+                if far(k + 1):
+                    ship(k + 1, c, "x", lo, hi)
                 signs("sv"[c], c, lo, hi)
             else:
                 mm("PS", c, hi - lo, "vq", "vqs", 0, xq, xs, lo, hi)

from concourse.mybir import dt, AluOpType, ActivationFunctionType

C = 352
CH = [(0, 224), (224, 352)]
MASKS = [1, 2, 4]
ROUNDS = 3
W16 = C // 16
HALF = C // 2
MOST = C // 2 + 1
E = 2.0 ** -30
FB = 368
RB = 16
TOP = 7
HALVES = [(0, 192), (192, C)]
TAIL = [(0, 128), (128, 256), (256, C)]
TAIL2 = [(0, 256), (256, C)]
LV = [(0, 128), (128, 256), (256, C)]
BESIDE = [("keep", "u", "hosts us"), ("", "", "uq"), ("", "x1", "x0"), ("", "up1", "up0"), ("sc", "dk", "lv0"), ("lv2", "dq", "lv1")]
EVEN = "s"
TINY = 2.0 ** -40
JUMP = ["ss", "ss", "ss", "ss", "ss", "ss", "ss"]
AT = [1, 2, 2, 4, 7, 6]
EARLY = 256
FIRST = [(0, C)]
SPLICE = "st void bits odd m2 even m3 last first slot before behind"
SPLICE1 = ("gone on1 guest pos0 keep1 bits list1 st on2 pos1 keep2 m2 odd0s stay list2 own even0s pos2 host m1 "
           "at0s at1s odd1v even1v void0 void1 first last place m3 before slot behind")
US = "v"
GQ = {1: "vs", 3: "vs"}
SC = "v"
PARTS = {1: CH, 2: [(0, C)], 3: [(0, 160), (160, C)]}
ZR = {1: [(0, 224, True), (224, C, True)], 2: [(0, 224, False), (224, C, False)], 3: [(0, 160, True), (160, C, False)]}
GV = {1: 256, 2: 256, 3: 256}
XT = 2
HORDER = {1: [(0, 0), (0, 1), (1, 0), (0, 2), (1, 1), (0, 3), (1, 2), (1, 3)],
          2: [(0, 0), (0, 1), (0, 2), (1, 0), (1, 1), (0, 3), (1, 2), (1, 3)],
          3: [(1, 0), (1, 1), (0, 0), (1, 2), (0, 1), (1, 3), (0, 2), (0, 3)]}
XL = 0
AFTER = [(), (), (), ()]
F8 = "float8_e4m3fn_x4"
CYCLE, WAKE, FLIGHT, LOAD, SPARE = 0.00092, 0.14, 2.2, 2.0, 0.25
SLACK = 0.03
RATE = {True: 200e3, False: 100e3}

SCRATCH = {
    "nxi": ("sbuf", [128, W16], "int32"),
    "ut": ("sbuf", [128, 512], "bfloat16"), "vt": ("sbuf", [128, 512], "bfloat16"),
    "wq": ("sbuf", [128, 512], F8), "wsq": ("sbuf", [128, 512], "uint8"),
    "uq": ("sbuf", [128, 128], F8), "uqs": ("sbuf", [128, 128], "uint8"),
    "up16": ("sbuf", [128, 128], F8), "up16s": ("sbuf", [128, 128], "uint8"),
    "vq": ("sbuf", [128, 128], F8), "vqs": ("sbuf", [128, 128], "uint8"),
    "eq": ("sbuf", [128, 512], F8), "eqs": ("sbuf", [128, 512], "uint8"),
    "EB": ("sbuf", [128, 516], "bfloat16"),
    "pi": ("sbuf", [128, 1], "int32"), "pj": ("sbuf", [128, 1], "int32"), "p16": ("sbuf", [128, 1], "float32"),
    "FS": ("sbuf", [128, FB + 2 * C + 16], "bfloat16"), "RS": ("sbuf", [128, RB + 2 * C + MOST + 15], "bfloat16"),
    "J16": ("sbuf", [128, 16], "float32"), "DA": ("sbuf", [128, 16], "float32"), "DB": ("sbuf", [128, 16], "float32"),
    "D16": ("sbuf", [128, 16], "bfloat16"),
    "PA": ("psum", [128, 2048], "float32"), "PB": ("psum", [128, 1024], "float32"), "PS": ("psum", [128, 1024], "float32"),
}
for _n in ("X0", "X1", "TH", "THP", "TB", "TBP", "Z", "HH"):
    SCRATCH[_n] = ("sbuf", [128, 4 * C], "bfloat16")
for _n in ("ONES", "D0", "D1", "CNT"):
    SCRATCH[_n] = ("sbuf", [128, 2 * C], "bfloat16")
for _n in ("IOTA", "DG", "OB", "GU", "SELO", "SELA", "SELP", "SELH", "SELL", "SELB", "SELC", "SELJ0", "SELJ1",
           "POS", "BPS", "APS", "VBP", "GA", "GB", "sc", "up", "lv", "st", "IT", "WL", "WN", "PT0", "PT1", "PT2", "PT3"):
    SCRATCH[_n] = ("sbuf", [128, C], "bfloat16")
for _n in ("ysb", "nrs"):
    SCRATCH[_n] = ("sbuf", [128, C], "float32")
for _n in ("C16", "jw", "jm", "j2", "m1", "m2", "m3", "pw", "dq", "dk"):
    SCRATCH[_n] = ("sbuf", [128, W16], "float32")
for _n in ("lp", "l16", "L1", "LB", "LJ0", "LJ1", "slw", "p2u", "ow", "aw", "hq"):
    SCRATCH[_n] = ("sbuf", [128, W16], "uint16")
for _k in range(1, ROUNDS + 2):
    SCRATCH["xq%d" % _k] = ("sbuf", [128, C], F8)
    SCRATCH["xs%d" % _k] = ("sbuf", [128, C], "uint8")
for _k in range(1, ROUNDS + 1):
    for _n in "lz" if _k > 1 else "z":
        SCRATCH[_n + "q%d" % _k] = ("sbuf", [128, C], F8)
        SCRATCH[_n + "s%d" % _k] = ("sbuf", [128, C], "uint8")
    SCRATCH["mq%d" % _k] = ("sbuf", [128, C], F8)
    SCRATCH["ms%d" % _k] = ("sbuf", [128, C], "uint8")
    for _n in ("abw", "lab", "lnx"):
        SCRATCH[_n + str(_k)] = ("sbuf", [128, 2 * W16], "uint16")

LOCAL = ["nx", "x", "u", "ws", "wc", "v", "y0", "y1", "nr", "oc0", "oc1", "osc0", "osc1", "osc2", "osc3"]
REMOTE = ["nb1", "nx1", "nx2", "nx3", "ab1", "ab2", "ab3"] + [
    w + n + str(k) + str(c) for k in (1, 2, 3) for w in "xz" for n in "qs" for c in (0, 1)]
SEMAPHORES = ["cv", "cs", "ct", "cg"] + ["d_" + n for n in LOCAL] + ["r_" + n for n in REMOTE] + ["l_" + n for n in REMOTE]


def lay_out(calls):
    busy, place = {}, {}

    def put(i):
        c = calls[i]
        for p in sorted(c["needs"] | c["behind"]):
            if p not in place:
                put(p)
        ready = max([place[p][2] + calls[p]["lag"] for p in c["needs"]] + [place[p][2] for p in c["behind"]], default=0.0)
        best = None
        for q, (_, t) in c["on"].items():
            at, line = ready, busy.setdefault(q, [])
            k = len(line)
            while k > 0 and line[k - 1][1] > ready:
                k -= 1
            while q and k < len(line) and at + t > line[k][0] + SLACK:
                at = max(at, line[k][1])
                k += 1
            score = at + t + (SPARE if q == "v" and len(c["on"]) > 1 else 0.0)
            if best is None or score < best[0]:
                best = (score, k, q, at, at + t)
        place[i] = best[2:]
        if best[2]:
            busy[best[2]].insert(best[1], best[3:])

    for late in (False, True):
        for i, c in enumerate(calls):
            if c["late"] == late and i not in place:
                put(i)
    return [(i, place[i][0]) for i in sorted(place, key=lambda i: (place[i][1], i))]


ORDER = []


def rank_program(g, core, T, topo):
    rank = T.rank_of(core)
    if rank is None:
        return
    A = AluOpType
    AF = ActivationFunctionType
    V, S = g.vector, g.scalar
    eng = {"v": V, "s": S, "t": g.tensor, "g": g, "y": g.sync}
    COUNT = {"v": "cv", "s": "cs", "t": "ct", "g": "cg"}
    calls, writes, reads, latest, mood = [], {}, {}, {}, [False]

    def late(f, *args):
        mood[0] = True
        f(*args)
        mood[0] = False

    def norm(k):
        return k if isinstance(k, tuple) else (k, 0, 1 << 20)

    def meets(table, k):
        return {e[2] for e in table.get(k[0], []) if e[0] < k[2] and k[1] < e[1]}

    def call(on, rd, wr, lag=WAKE, sem=None, inc=1, row=None):
        rd, wr, needs = [norm(k) for k in rd], [norm(k) for k in wr], set()
        for k in rd:
            needs |= meets(writes, k)
            if k[0] in ("PA", "PB", "PS"):
                needs |= {p for p in meets(reads, k) if len(on) > 1 or list(calls[p]["on"]) != list(on)}
        for k in wr:
            needs |= meets(writes, k) | meets(reads, k)
        i = len(calls)
        calls.append({"on": on, "needs": needs, "behind": {latest[row]} if row in latest else set(), "lag": lag, "sem": sem,
                      "inc": inc, "late": mood[0]})
        if row:
            latest[row] = i
        for k in wr:
            for t in (writes, reads):
                t[k[0]] = [e for e in t.get(k[0], []) if not (k[1] <= e[0] and e[1] <= k[2])]
            writes[k[0]].append((k[1], k[2], i))
        for k in rd:
            reads[k[0]] = reads.get(k[0], []) + [(k[1], k[2], i)]
        return i

    def issue():
        total, know, event = {}, {q: {} for q in eng}, {}
        if not ORDER:
            ORDER.extend(lay_out(calls))
        for i, q in ORDER:
            c = calls[i]
            if q is None:
                total[c["sem"]] = c["inc"]
                event[i] = (c["sem"], c["inc"], {c["sem"]: c["inc"]})
                continue
            kn, want = know[q], {}
            for sem, val, clock in [event[p] for p in c["needs"]]:
                if kn.get(sem, 0) < val and want.get(sem, (0,))[0] < val:
                    want[sem] = (val, clock)
            for sem in sorted(want):
                if any(o != sem and want[o][1].get(sem, 0) >= want[sem][0] for o in want):
                    del want[sem]
            for sem, (val, clock) in sorted(want.items()):
                eng[q].wait_ge(T.sem[sem], val)
                for s2, v2 in clock.items():
                    kn[s2] = max(kn.get(s2, 0), v2)
            sem = c["sem"] or COUNT[q]
            done = c["on"][q][0]()
            if not sem.startswith("l_"):
                done.then_inc(T.sem[sem], c["inc"])
            total[sem] = total.get(sem, 0) + c["inc"]
            event[i] = (sem, total[sem], dict(kn, **{sem: total[sem]}))
        for sem, val in total.items():
            if know["g"].get(sem, 0) < val:
                g.wait_ge(T.sem[sem], val)

    def plain(n, rate=1.0):
        return max(64, n * rate) * CYCLE

    def picked(n, rate=1.56):
        return 0.055 + n * rate * CYCLE

    def dma(q, name, out, in_, rd, wr, lag=LOAD):
        call({q: (lambda: eng[q].dma_start(out, in_), 0.05)}, rd, wr, lag, "d_" + name, 16, "dma" + q)

    def send(name, dst, out, in_, rd, lands, width):
        rid, pid = topo.addr(dst)[:2]
        lag = FLIGHT + 128 * width / RATE[topo.chip(core) == topo.chip(dst)]
        i = call({"g": (lambda: g.remote_dma(out, in_, T.sem["r_" + name], T.sem["l_" + name], pid, rid, topo.mask(core, dst)), 0.1)},
                 [rd], [], lag, "l_" + name, len(topo.engines(core, dst)), "g")
        j = call({None: (None, 0.0)}, [], [lands], 0.0, "r_" + name, len(topo.engines(dst, core)))
        calls[j]["needs"] = {i}
        if "landed" in latest:
            calls[j]["behind"] = {latest["landed"]}
        latest["landed"] = j

    partner = [T.cores[rank ^ m] for m in MASKS]

    def ts(out, in0, s1, s2, o0, o1, rd, wr, rate=1.0):
        ops = (o0,) if o1 is None else (o0, o1)
        call({"v": (lambda: V.tensor_scalar(out, in0, s1, s2, *ops), plain(out.shape[1], rate))}, rd, wr)

    def tt(out, in0, in1, o, rd, wr, pick=False):
        n = out.shape[1]
        call({"v": (lambda: V.tensor_tensor(out, in0, in1, o), picked(n) if pick else plain(n, 2))}, rd, wr)

    def vcopy(out, in_, rd, wr, rate=1.0):
        call({"v": (lambda: V.tensor_copy(out, in_), plain(out.shape[1], rate))}, rd, wr)

    def fill(ap, val, wr):
        call({"v": (lambda: V.memset(ap, val), plain(ap.shape[1], 0.5))}, [], wr)

    def scan(out, d0, d1, init, o0, o1, rd, wr):
        call({"v": (lambda: V.tensor_tensor_scan(out, d0, d1, init, o0, o1), plain(out.shape[1], 0.5))}, rd, wr)

    def act(out, in_, rd, wr, func):
        call({"s": (lambda: S.activation(out, in_, func), plain(out.shape[1]))}, rd, wr)

    def line(qs, out, in_, rd, wr, scale, bias=0.0, rate=1.0):
        n = out.shape[1]
        on = {"s": (lambda: S.activation(out, in_, AF.Identity, bias=bias, scale=scale), plain(n)),
              "v": (lambda: V.tensor_scalar(out, in_, scale, bias, A.mult, A.add), plain(n, rate))}
        call({q: on[q] for q in qs}, rd, wr)

    def pick(qs, out, win, rd, wr, scale=None):
        n = out.shape[1]
        on = {"s": (lambda: S.activation(out, win, AF.Copy), picked(n) + 0.015), "v": (lambda: V.tensor_copy(out, win), picked(n))}
        if scale:
            on = {"s": (lambda: S.activation(out, win, AF.Copy, scale=scale), picked(n) + 0.015),
                  "v": (lambda: V.tensor_scalar(out, win, scale, None, A.mult), picked(n))}
        call({q: on[q] for q in qs}, rd, wr)

    def quant(codes, plane, lo, hi, src, rd):
        call({"v": (lambda: V.quantize_mx(T[codes][:, lo:hi], T[plane][:, lo:hi], src), 0.013 + 0.00097 * (hi - lo))},
             rd, [(codes, lo, hi), (plane, lo, hi)])

    def mm(P, s, n, l, ls, a, r, rs, lo, hi):
        call({"t": (lambda: g.tensor.matmul_mx(T[P][:, 512 * s:512 * s + n], T[l][:, a:a + 128], T[ls][:, a:a + 128],
                                               T[r][:, lo:hi], T[rs][:, lo:hi], True, True), 1.4 * (n + 16) * CYCLE)},
             [(l, a, a + 128), (ls, a, a + 128), (r, lo, hi), (rs, lo, hi)], [(P, 512 * s, 512 * s + 512)])

    def pool(f, n, rd, wr):
        call({"g": (f, 0.15 + 2 * n * CYCLE)}, rd, wr, row="g")

    def bank(P, s, n):
        return T[P][:, 512 * s:512 * s + n], (P, 512 * s, 512 * s + 512)

    def cols(lst, lo, hi, at=0):
        return T[lst][:, (at + lo) // 16:(at + hi) // 16], (lst, (at + lo) // 16, (at + hi) // 16)

    def gather(qs, out, win, lst, lo=0, hi=C, at=0):
        off, key = cols(lst, lo, hi, at)
        pick(qs, T[out][:, lo:hi], T[win][:].indirect(off), [win, key], [(out, lo, hi)])

    def keep16(out, src, lo=0, hi=C):
        scan(T[out][:, lo:hi], T[src][:, lo:hi], T.DG[:, 0:hi - lo], 0.0, A.add, A.mult, ["DG", (src, lo, hi)], [(out, lo, hi)])

    def kept(sel, lo=0, hi=C):
        return T[sel][:, lo + 15:hi:16]

    def enlist(lst, sel, lo=0, hi=C, at=0):
        off, key = cols(lst, lo, hi, at)
        ts(off, kept(sel, lo, hi), 1 / E, HALF + 0.25, A.mult, A.add, [(sel, lo, hi)], [key])

    def listed(lst, sel, src, lo=0, hi=C, at=0):
        keep16(sel, src, lo, hi)
        enlist(lst, sel, lo, hi, at)

    def invert(out, lst, lo=0, hi=C):
        off, key = cols(lst, lo, hi)
        call({"v": (lambda: V.tensor_copy(T[out][:].indirect(off), T.IOTA[:, lo:hi]), picked(hi - lo, 3.8))}, ["IOTA", key], [out])

    dma("y", "nx", T.nxi[:], T.nx[:], [], ["nxi"])
    dma("y", "u", T.ut[:], T.u[:], [], ["ut"], LOAD + 0.6)
    dma("y", "x", T.X0[:], T.x[:], [], ["X0"], LOAD + 2.0)

    pool(lambda: g.iota(T.pi[:], [[0, 1]], 0, 1), 1, [], ["pi"])
    fill(T.ONES[:], 1.0, ["ONES"])
    pool(lambda: g.affine_select(T.EB[:], T.ONES[:, 0:516], [[1, 516]], A.is_equal, 0.0, -4, -4), 516, ["ONES"], ["EB"])
    vcopy(T.L1[:], T.nxi[:], ["nxi"], ["L1"])
    send("nx1", partner[0], T.lnx1[:, 0:W16], T.L1[:], "L1", ("lnx1", 0, W16), 2 * W16)
    ts(T.pj[:], T.pi[:], 15, None, A.bitwise_and, None, ["pi"], ["pj"])
    scan(T.IOTA[:], T.ONES[:, 0:C], T.ONES[:, 0:C], -HALF - 1.0, A.mult, A.add, ["ONES"], ["IOTA"])
    vcopy(T.p16[:], T.pj[:], ["pj"], ["p16"])
    J16 = T.IOTA[:, HALF:HALF + 16]
    ts(T.DA[:], J16, T.p16[:, 0:1], None, A.is_gt, None, ["IOTA", "p16"], ["DA"])
    ts(T.DB[:], J16, T.p16[:, 0:1], 1 / E, A.is_equal, A.mult, ["IOTA", "p16"], ["DB"])
    ts(T.lp[:], T.ONES[:, 0:W16], T.p16[:, 0:1], None, A.mult, None, ["ONES", "p16"], ["lp"])
    tt(T.D16[:], T.DA[:], T.DB[:], A.add, ["DA", "DB"], ["D16"])
    ts(T.D16[:, 15:16], T.D16[:, 15:16], E * E, None, A.mult, None, ["D16"], ["D16"])
    gather("s", "DG", "D16", "lp")
    for b in range(4):
        late(quant, "eq", "eqs", 128 * b, 128 * b + 128, T.EB[:, 4 - b:516 - b], ["EB"])
    fill(T.ow[:], 0, ["ow"])
    fill(T.OB[:, 0:1], -float(HALF), [("OB", 0, 1)])
    line("s", T.IT[:], T.IOTA[:], ["IOTA"], ["IT"], TINY)
    fill(T.IT[:, HALF:HALF + 1], TINY / 64, ["IT"])
    ts(T.l16[:], T.IOTA[:, 0:C:16], float(HALF), None, A.add, None, ["IOTA"], ["l16"])
    line("s", T.jw[:], T.IOTA[:, 0:C:16], ["IOTA", "p16"], ["jw"], 1.0, T.p16[:, 0:1])
    line("s", T.jm[:], T.jw[:], ["jw"], ["jm"], E)
    line("s", T.j2[:], T.jw[:], ["jw"], ["j2"], E * E, (HALF + 0.25) * E * E)

    def ucols():
        quant("uq", "uqs", 0, 128, T.ut[:], ["ut"])
        pick(US, T.up16s[:, 0:128], T.uqs[:, 0:128].indirect(T.l16[:, 0:8]), ["uqs", "l16"], ["up16s"])
        pick("v", T.up16[:, 0:128].bitcast(dt.uint32), T.uq[:, 0:128].bitcast(dt.uint32).indirect(T.l16[:, 0:8]), ["uq", "l16"], ["up16"])

    def scores(k, c, lo, hi):
        mm("PS", c, hi - lo, "up16", "up16s", 0, "xq%d" % k, "xs%d" % k, lo, hi)

    def ship(k, c, w, lo, hi):
        p, land = partner[k - 1], {"x": "l", "z": "m"}[w]
        q, s, lq, ls = w + "q%d" % k, w + "s%d" % k, land + "q%d" % k, land + "s%d" % k
        send(w + "q%d%d" % (k, c), p, T[lq][:, lo:hi].bitcast(dt.uint8), T[q][:, lo:hi].bitcast(dt.uint8), (q, lo, hi),
             (lq, lo, hi), 4 * (hi - lo))
        if w == "x":
            if c == 0:
                return
            lo = 0
        send(w + "s%d%d" % (k, c), p, T[ls][:, lo:hi], T[s][:, lo:hi], (s, lo, hi), (ls, lo, hi), 5 * (hi - lo))

    def signs(q, c, lo, hi):
        src, key = bank("PS", c, hi - lo)
        if q == "v":
            for n in ("up", "sc"):
                ts(T[n][:, lo:hi], src, 0.0, None, A.is_gt, None, [key], [(n, lo, hi)])
        else:
            act(T.sc[:, lo:hi], src, [key], [("sc", lo, hi)], AF.Sign)
            act(T.up[:, lo:hi], T.sc[:, lo:hi], [("sc", lo, hi)], [("up", lo, hi)], AF.Relu)

    def place(c, b):
        return ("PA", b) if c == 0 else ("PB", b) if b < 2 else ("PA", b - 2)

    def product(P, s, l, ls, b, r, rs, lo, hi, out, scale, qs="sv"):
        mm(P, s, hi - lo, l, ls, 128 * b, r, rs, lo, hi)
        src, key = bank(P, s, hi - lo)
        line(qs, T[out][:, C * b + lo:C * b + hi], src, [key], [(out, C * b + lo, C * b + hi)], scale)

    def unpack(k):
        for b in range(4):
            product("PA", b, "eq", "eqs", b, "xq%d" % k, "xs%d" % k, 0, C, "TH", 0.5)

    def unpack_far(k, bs=range(4), qs="sv"):
        for b in bs:
            product("PA", b, "eq", "eqs", b, "lq%d" % k, "ls%d" % k, 0, C, "THP", 0.5, qs)

    def leavers(lst, runs):
        for lo, hi in runs:
            off, key = cols(lst, lo, hi, C)
            tt(T.lv[:, lo:hi], T.up[:].indirect(off), T.sc[:, lo:hi], A.is_lt, ["up", ("sc", lo, hi), key], [("lv", lo, hi)], True)

    def stayers():
        line("v", T.st[:], T.lv[:], ["lv"], ["st"], -1.0, 1.0, 0.5)

    def void(odd):
        lst, flag = (("ow", "lv"), ("aw", "st"))[odd]
        pick("s", T.D0[:, odd:2 * C:2], T[flag][:].indirect(T[lst][:]), [flag, lst], ["D0%d" % odd])

    def there(odd):
        lst, flag, who = (("ow", "st", "OB"), ("aw", "lv", "GU"))[odd]
        tt(T.D1[:, odd:2 * C:2], T[flag][:].indirect(T[lst][:]), T[who][:], A.mult, [flag, lst, who], ["D1%d" % odd], True)

    def keys(odds, lo=0, hi=C):
        return [("D%d%d" % (d, o), lo, hi) for d in (0, 1) for o in odds]

    def neighbours(q, out, lo, hi):
        win, a = ("RS", RB) if out == "GA" else ("FS", FB)
        off, key = cols("slw", lo, hi)
        pick(q, T[out][:, lo:hi], T[win][:, a:a + 2 * C].indirect(off), [(win, a, a + 2 * C), key], [(out, lo, hi)])

    def far(k):
        return [lo for lo, hi, own in ZR[k] if not own]

    def first_there():
        r = RB + 2 * C - 1
        scan(T.RS[:, r + MOST - 1:r - 1:-1], T.D0[:, 2 * MOST - 2::-2], T.D1[:, 2 * MOST - 2::-2], 0.0, A.mult, A.add,
             keys([0], 0, MOST), [("RS", r, r + MOST)])

    def last_there():
        a = 2 * (C - MOST)
        scan(T.FS[:, FB + 1 - 2 * MOST:FB + 1], T.D0[:, a:2 * C], T.D1[:, a:2 * C], 0.0, A.mult, A.add,
             keys([0, 1], C - MOST, C), [("FS", 0, FB + 1)])

    def before():
        scan(T.FS[:, FB + 1:FB + 1 + 2 * C], T.D0[:], T.D1[:], T.FS[:, FB:FB + 1], A.mult, A.add,
             keys([0, 1]) + [("FS", FB, FB + 1)], [("FS", FB + 1, FB + 1 + 2 * C)])

    def behind():
        r = RB + 2 * C - 1
        scan(T.RS[:, r - 1:RB - 2:-1], T.D0[:, ::-1], T.D1[:, ::-1], T.RS[:, r:r + 1], A.mult, A.add,
             keys([0, 1]) + [("RS", r, r + 1)], [("RS", 0, r)])

    def in_turn(*steps):
        turn = {}
        for f in steps:
            n = len(calls)
            f()
            for c in range(n, len(calls)):
                q = "".join(map(str, calls[c]["on"]))
                if q in ("v", "s"):
                    calls[c]["behind"] |= {turn[q]} if q in turn else set()
                    turn[q] = c

    def lists(k):
        abw = "abw%d" % k
        for lo, hi in PARTS[k]:
            neighbours("s", "GB", lo, hi)
            if hi - lo == C:
                neighbours("v", "GA", 0, GV[k])
                neighbours("s", "GA", GV[k], C)
            else:
                neighbours(GQ[k][lo > 0], "GA", lo, hi)
            keep16("SELB", "GB", lo, hi)
            keep16("SELC", "GA", lo, hi)
            enlist(abw, "SELC", lo, hi)
            enlist(abw, "SELB", lo, hi, C)
        if far(k):
            n = far(k)[0] // 16
            send("ab%d" % k, partner[k - 1], T["lab%d" % k][:, n:], T[abw][:, n:], abw, "lab%d" % k, 4 * W16 - 2 * n)
        if k < ROUNDS:
            send("nx%d" % (k + 1), partner[k], T["lnx%d" % (k + 1)][:], T[abw][:], abw, "lnx%d" % (k + 1), 4 * W16)

    def splice(k):
        leavers("lnx%d" % k, CH)
        void(0)
        step = {"st": stayers, "bits": lambda: keep16("SELL", "lv"), "even": lambda: there(0), "odd": lambda: there(1),
                "void": lambda: void(1),
                "m2": lambda: tt(T.m2[:], kept("SELL"), T.dk[:], A.mult, ["SELL", "dk"], ["m2"]),
                "m3": lambda: tt(T.m3[:], T.m2[:], T.pw[:], A.add, ["m2", "pw"], ["m3"]),
                "slot": lambda: ts(T.slw[:], T.m3[:], 1 / E / E, None, A.mult, None, ["m3"], ["slw"]),
                "first": first_there, "last": last_there, "before": before, "behind": behind}
        in_turn(*[step[n] for n in SPLICE.split()])
        lists(k)

    def guests(lo=0, hi=C):
        gather("s", "GU", "APS", "ow", lo, hi)
        listed("aw", "SELA", "GU", lo, hi)

    def new_places(q="s"):
        scan(T.CNT[:], T.ONES[:], T.D0[:], -HALF - 1.0, A.add, A.subtract, ["ONES", "D00", "D01"], ["CNT"])
        gather(q, "POS", "CNT", "slw")

    def new_order():
        listed("p2u", "SELP", "POS")
        invert("OB", "p2u")

    def new_slots(lnx):
        listed("ow", "SELO", "OB")
        gather("s", "APS", "IOTA", lnx)
        gather("s", "VBP", "POS", lnx, 0, C, C)
        guests()
        line("s", T.pw[:], kept("SELP"), ["SELP"], ["pw"], 2 * E, (C + 0.25) * E * E)
        keep16("SELH", "VBP")
        tt(T.dq[:], kept("SELH"), kept("SELP"), A.subtract, ["SELH", "SELP"], ["dq"])
        line("s", T.dk[:], T.dq[:], ["dq"], ["dk"], 2.0, E)

    def first_signs():
        for c, (lo, hi) in enumerate(FIRST):
            quant("xq1", "xs1", lo, hi, T.X0[:, 4 * lo:4 * hi], ["X0"])
            scores(1, c, lo, hi)

    def first_hosts():
        for c, (lo, hi) in enumerate(FIRST):
            src, key = bank("PS", c, hi - lo)
            ts(T.up[:, lo:hi], src, 0.0, None, A.is_gt, None, [key], [("up", lo, hi)])
        if SC == "g":
            pool(lambda: g.affine_select(T.sc[:], T.up[:], [[0, C]], A.is_ge, 0.0, 0, 0), C, ["up"], ["sc"])
        else:
            vcopy(T.sc[:], T.up[:], ["up"], ["sc"], 0.5)

    def flagged(out, flag):
        scan(T[out][:], T[flag][:], T.IT[:], 0.0, A.max, A.mult, [flag, "IT"], [out])

    def first_guests():
        flagged("WL", "lv")
        off, key = cols("lnx1", 0, C)
        pick("s", T.GU[:], T.WL[:].indirect(off), ["WL", key], ["GU"], 1 / TINY)

    def first_slots(lo, hi):
        off, key = cols("ow", lo, hi)
        pick(EVEN, T.D1[:, 2 * lo:2 * hi:2], T.WN[:].indirect(off), ["WN", key], [("D10", lo, hi)], 1 / TINY)
        pick("s", T.D1[:, 2 * lo + 1:2 * hi:2], T.GU[:].indirect(off), ["GU", key], [("D11", lo, hi)])
        ts(T.D0[:, 2 * lo:2 * hi], T.D1[:, 2 * lo:2 * hi], 2.0 ** 16, 2.0 ** 16, A.add, A.is_equal,
           [("D10", lo, hi), ("D11", lo, hi)], [("D00", lo, hi), ("D01", lo, hi)], 0.5)

    def first_leavers():
        leavers("lnx1", LV)

    def first_lists():
        stayers()
        keep16("SELL", "lv")
        flagged("WN", "st")
        ts(T.dk[:], T.lnx1[:, W16:2 * W16], E, -HALF * E, A.mult, A.add, ["lnx1"], ["dk"])
        tt(T.dq[:], T.dk[:], T.jm[:], A.subtract, ["dk", "jm"], ["dq"])
        tt(T.m2[:], kept("SELL"), T.dq[:], A.mult, ["SELL", "dq"], ["m2"])
        tt(T.m3[:], T.m2[:], T.j2[:], A.add, ["m2", "j2"], ["m3"])
        ts(T.hq[:], T.m3[:], 1 / E / E, None, A.mult, None, ["m3"], ["hq"])
        line("sv", T.m1[:], kept("SELL"), ["SELL"], ["m1"], 0.5, (HALF + 0.125) * E)

    def ahead(P, m, n, a):
        off, key = cols("ow", a, a + n)
        pick("s", T.OB[:, m:m + n], T[P][:].indirect(off), [P, key], [("OB", m, m + n)])
        b = 0 if m < 16 else m
        listed("ow", "SELO", "OB", b, b + n)

    gather("s", "PT0", "IOTA", "L1")
    invert("BPS", "L1")

    def hosts():
        enlist("LB", "SELH")
        send("nb1", partner[0], T.lnx1[:, W16:2 * W16], T.LB[:], "LB", ("lnx1", W16, 2 * W16), 2 * W16)
        late(dma, "y", "ws", T.wsq[:], T.ws[:], ["lnx1"], ["wsq"])
        late(dma, "y", "wc", T.wq[:].bitcast(dt.uint8), T.wc[:], [], ["wq"], LOAD + 1.5)
        late(dma, "y", "v", T.vt[:], T.v[:], [], ["vt"], LOAD + 2.0)

    def xrun(c):
        lo, hi = CH[c]
        quant("xq1", "xs1", lo, hi, T.X0[:, 4 * lo:4 * hi], ["X0"])
        scores(1, c, lo, hi)

    def ups(c):
        lo, hi = CH[c]
        src, key = bank("PS", c, hi - lo)
        ts(T.up[:, lo:hi], src, 0.0, None, A.is_gt, None, [key], [("up", lo, hi)])

    beside = {"keep": lambda: keep16("SELH", "BPS"), "hosts": hosts, "u": lambda: quant("uq", "uqs", 0, 128, T.ut[:], ["ut"]),
              "us": lambda: pick("v", T.up16s[:, 0:128], T.uqs[:, 0:128].indirect(T.l16[:, 0:8]), ["uqs", "l16"], ["up16s"]),
              "uq": lambda: pick("v", T.up16[:, 0:128].bitcast(dt.uint32), T.uq[:, 0:128].bitcast(dt.uint32).indirect(T.l16[:, 0:8]),
                                 ["uq", "l16"], ["up16"]),
              "x0": lambda: xrun(0), "x1": lambda: xrun(1), "up0": lambda: ups(0), "up1": lambda: ups(1),
              "dk": lambda: ts(T.dk[:], T.lnx1[:, W16:2 * W16], E, -HALF * E, A.mult, A.add, ["lnx1"], ["dk"]),
              "dq": lambda: tt(T.dq[:], T.dk[:], T.jm[:], A.subtract, ["dk", "jm"], ["dq"]),
              "sc": lambda: vcopy(T.sc[:], T.up[:], ["up"], ["sc"], 0.5),
              "lv0": lambda: leavers("lnx1", LV[0:1]), "lv1": lambda: leavers("lnx1", LV[1:2]), "lv2": lambda: leavers("lnx1", LV[2:3])}
    for i in range(TOP):
        L, L2, sel = "L1" if i == 0 else "LJ%d" % (i % 2), "LJ%d" % (1 - i % 2), "SELJ%d" % (i % 2)
        P, P2 = "PT%d" % (i % 4), "PT%d" % ((i + 1) % 4)
        if i == 0:
            ahead(P, 1, 16, 0)
        for q, (lo, hi) in zip(JUMP[i], HALVES):
            gather(q, P2, P, L, lo, hi)
        n = 2 ** (i + 1)
        if i < TOP - 1:
            one, two, three = [[beside[w] for w in ws.split()] for ws in BESIDE[i]]
            b = 0 if n < 16 else n
            off, key = cols("ow", 0, max(16, n))
            pick("s", T.OB[:, n:n + max(16, n)], T[P2][:].indirect(off), [P2, key], [("OB", n, n + max(16, n))])
            in_turn(lambda: keep16(sel, P2, *HALVES[0]), *one, lambda: enlist(L2, sel, *HALVES[0]),
                    lambda: keep16(sel, P2, *HALVES[1]), *two, lambda: enlist(L2, sel, *HALVES[1]),
                    lambda: keep16("SELO", "OB", b, b + max(16, n)), *three, lambda: enlist("ow", "SELO", b, b + max(16, n)))
    late(unpack, 1)

    def onward(c):
        lo, hi = TAIL[c]
        off, key = cols("ow", lo - 2 ** TOP, hi - 2 ** TOP)
        pick("s", T.OB[:, lo:hi], T["PT%d" % (TOP % 4)][:].indirect(off), ["PT%d" % (TOP % 4), key], [("OB", lo, hi)])

    def names(q, odd, lo, hi):
        off, key = cols("ow", lo, hi)
        win = "GU" if odd else "WN"
        pick(q, T.D1[:, 2 * lo + odd:2 * hi:2], T[win][:].indirect(off), [win, key], [("D1%d" % odd, lo, hi)], None if odd else 1 / TINY)

    def voids(lo, hi):
        ts(T.D0[:, 2 * lo:2 * hi], T.D1[:, 2 * lo:2 * hi], 2.0 ** 16, 2.0 ** 16, A.add, A.is_equal,
           [("D10", lo, hi), ("D11", lo, hi)], [("D00", lo, hi), ("D01", lo, hi)], 0.5)

    step = {"gone": lambda: flagged("WL", "lv"), "st": stayers, "stay": lambda: flagged("WN", "st"), "bits": lambda: keep16("SELL", "lv"),
            "guest": lambda: pick("s", T.GU[:], T.WL[:].indirect(T.lnx1[:, 0:W16]), ["WL", ("lnx1", 0, W16)], ["GU"], 1 / TINY),
            "m2": lambda: tt(T.m2[:], kept("SELL"), T.dq[:], A.mult, ["SELL", "dq"], ["m2"]),
            "own": lambda: tt(T.m3[:], T.m2[:], T.j2[:], A.add, ["m2", "j2"], ["m3"]),
            "host": lambda: ts(T.hq[:], T.m3[:], 1 / E / E, None, A.mult, None, ["m3"], ["hq"]),
            "m1": lambda: late(line, "sv", T.m1[:], kept("SELL"), ["SELL"], ["m1"], 0.5, (HALF + 0.125) * E),
            "place": lambda: keep16("SELP", "VBP"),
            "m3": lambda: tt(T.m3[:], kept("SELP"), T.m1[:], A.add, ["SELP", "m1"], ["m3"]),
            "slot": lambda: ts(T.slw[:], T.m3[:], 2 / E, None, A.mult, None, ["m3"], ["slw"]),
            "first": first_there, "last": last_there, "before": before, "behind": behind}
    for c, run in enumerate(TAIL):
        step["on%d" % c] = lambda c=c: onward(c)
        step["keep%d" % c] = lambda run=run: keep16("SELO", "OB", *run)
        step["list%d" % c] = lambda run=run: enlist("ow", "SELO", *run)
        step["pos%d" % c] = lambda run=run: invert("POS", "ow", *run)
    for c, run in enumerate(TAIL2):
        step["void%d" % c] = lambda run=run: voids(*run)
        for q in "sv":
            step["even%d" % c + q] = lambda run=run, q=q: names(q, 0, *run)
            step["odd%d" % c + q] = lambda run=run, q=q: names(q, 1, *run)
            step["at%d" % c + q] = lambda c=c, q=q: gather(q, "VBP", "POS", "hq", *HALVES[c])
    in_turn(*[step[n] for n in SPLICE1.split()])
    lists(1)
    late(quant, "vq", "vqs", 0, 128, T.vt[:], ["vt", "abw1"])

    for k in range(1, ROUNDS + 1):
        last = k == ROUNDS
        if k > 1:
            splice(k)
        abw, lab, lnx = "abw%d" % k, "lab%d" % k, "lnx%d" % (k + 1)
        xq, xs = "xq%d" % (k + 1), "xs%d" % (k + 1)
        zq, zs = "zq%d" % k, "zs%d" % k

        def back(qs, out, win, lst, t, lo=0, hi=C, behind=()):
            W = C * t
            off, key = cols(lst, lo, hi, C)
            pick(qs, T[out][:, W + lo:W + hi], T[win][:, W:W + C].indirect(off), [(win, W, W + C), key] + list(behind), [(out, W + lo, W + hi)])

        def mean(out, win, lst, add, t, lo, hi):
            W = C * t
            off, key = cols(lst, lo, hi)
            tt(T[out][:, 4 * lo + t:4 * hi:4], T[win][:, W:W + C].indirect(off), T[add][:, W + lo:W + hi], A.add,
               [(win, W, W + C), key, (add, W + lo, W + hi)], [(out + "_%d" % t, lo, hi)], True)

        def tile(out, runs, whole, pair, ahead):
            steps = [(t, 0, C) + runs[0][2:] for t in range(whole)] + [(t,) + run for run in runs for t in range(whole, 4)]
            apart = len(runs) == 2 and runs[0][2] != runs[1][2]
            for n, (t, lo, hi, win, lst, add) in enumerate(steps):
                if ahead:
                    back("s", add, win, lst, t, lo, hi)
                mean(out, win, lst, add, t, lo, hi)
                c = {4 if apart or whole == 3 else 5: 0, len(steps): 1}.get(n + 1)
                if c is not None:
                    lo, hi = runs[c][:2]
                    quant(*pair, lo, hi, T[out][:, 4 * lo:4 * hi], [(out + "_%d" % t, lo, hi) for t in range(4)])
                    if ahead and win == "TH":
                        ship(k, c, "z", lo, hi)
                    if apart and c == 0:
                        unpack_far(k)

        if far(k):
            if not last:
                new_places("v")
                new_order()
                for t in (0, 1):
                    back("s", "TB", "TH", abw, t)
                unpack_far(k, range(4), "s")
            elif far(k)[0] == 0:
                unpack_far(k)
            for t in range(4 if last else 2, 4):
                late(back, "sv", "TB", "TH", abw, t)
        tile("Z", [(lo, hi) + (("TH", abw, "TB") if own else ("THP", lab, "TBP")) for lo, hi, own in ZR[k]], 0, (zq, zs), True)
        if last:
            for t in range(4):
                late(back, "sv", "TB", "TH", abw, t, far(k)[0], C, AFTER[t])
            late(lambda: line("s", T.nrs[:], T.GA[:], ["GA"], ["nrs"], 1.0, float(HALF)))
            late(lambda: dma("y", "nr", T.nr[:], T.nrs[0:128:16, :], ["nrs", "ms%d" % k], []))
        if not far(k) and not last:
            new_places()
            new_order()
        for c, b in HORDER[k]:
            lo, hi, own = ZR[k][c]
            product(*place(c, b), "wq", "wsq", b, *(("mq%d" % k, "ms%d" % k) if own else (zq, zs)), lo, hi, "HH", 2.0 ** -6, "s")
        if not last:
            late(new_slots, lnx)
        tile("X1", [run + ("HH", abw, "TB") for run in CH], XL if last else XT, (xq, xs), False)
        for c, (lo, hi) in enumerate(CH):
            if not last:
                scores(k + 1, c, lo, hi)
                if far(k + 1):
                    ship(k + 1, c, "x", lo, hi)
                signs("sv"[c], c, lo, hi)
            else:
                mm("PS", c, hi - lo, "vq", "vqs", 0, xq, xs, lo, hi)
                dma("y", "oc%d" % c, T.oc[:, 4 * lo:4 * hi], T[xq][:, lo:hi].bitcast(dt.uint8), [(xq, lo, hi)], [])
                if c == 1:
                    for i in range(4):
                        dma("y", "osc%d" % i, T.osc[4 * i:4 * i + 4, :], T[xs][32 * i:32 * i + 4, :], [xs], [])
                src, key = bank("PS", c, hi - lo)
                line("s", T.ysb[:, lo:hi], src, [key], [("ysb", lo, hi)], 1.0)
                dma("ys"[c], "y%d" % c, T.y[:, lo:hi], T.ysb[:, lo:hi], [("ysb", lo, hi)], [])
        if not last:
            late(unpack, k + 1)
    issue()
